import numpy as np
import ml_dtypes


def mxq(x, axis, fmt="e4m3"):
    dtype, down = {"e4m3": (ml_dtypes.float8_e4m3fn, 7), "e5m2": (ml_dtypes.float8_e5m2, 14)}[fmt]
    v = np.moveaxis(np.asarray(x, np.float32).astype(ml_dtypes.bfloat16).astype(np.float64), axis, -1)
    blocks = v.reshape(v.shape[:-1] + (-1, 32))
    amax = np.abs(blocks).max(-1, keepdims=True)
    byte = np.maximum(np.where(amax > 0, np.frexp(amax)[1] - 1 + 127, 0) - down, 1)
    scale = np.exp2(byte - 127.0)
    codes = (blocks / scale).astype(np.float32).astype(dtype).astype(np.float64)
    return np.moveaxis((codes * scale).reshape(v.shape), -1, axis)


WIDE = False


def mx_kscale(k):
    if not WIDE:
        return np.ones(k)
    levels = np.array([10, -10, 5, -5, 0])
    if k % 512:
        return np.exp2(np.random.permutation(np.resize(levels, k // 32))).repeat(32)
    a = np.empty((k // 512, 16))
    for p in range(k // 512):
        a[p, :8] = np.random.permutation(np.resize(levels, 8))
        for g in range(8):
            far = levels[np.abs(levels - a[p, g]) >= 10]
            a[p, g + 8] = far[np.random.randint(len(far))]
    return np.exp2(a.ravel()).repeat(32)


def f64(x):
    return np.asarray(x).astype(np.float64)


def striped(idx):
    return np.tile(idx.reshape(-1, 16).T, (8, 1)).astype(np.uint16)


def unstriped(offs):
    return offs[:16].T.reshape(-1).astype(np.int64)


E2M1 = np.array([0.0, 0.5, 1.0, 1.5, 2.0, 3.0, 4.0, 6.0, -0.0, -0.5, -1.0, -1.5, -2.0, -3.0, -4.0, -6.0])


def pack_weight(w, fmt):
    k, n = w.shape
    w = f64(np.asarray(w, np.float32).astype(ml_dtypes.bfloat16)).reshape(k // 32, 32, n)
    amax = np.abs(w).max(1)
    if fmt == "e4m3":
        byte = np.frexp(amax)[1] - 1 + 127 - 7
    else:
        mant, ex = np.frexp(amax / 6.0)
        byte = np.where(mant > 0.5, ex, ex - 1) + 127
    byte = np.clip(np.where(amax > 0, byte, 1), 1, 254)
    scaled = (w * np.exp2(127.0 - byte)[:, None, :]).reshape(k, n).astype(np.float32)
    by_word = np.ascontiguousarray(scaled.reshape(k // 512, 128, 4, n).transpose(0, 1, 3, 2))
    if fmt == "e4m3":
        words = by_word.astype(ml_dtypes.float8_e4m3fn).view(np.uint8)
    else:
        c = by_word.astype(ml_dtypes.float4_e2m1fn).view(np.uint8) & 0xF
        words = (c[..., 0::2] | (c[..., 1::2] << 4)).reshape(k // 512, 128, 2 * n)
    return np.ascontiguousarray(words), np.ascontiguousarray(byte.astype(np.uint8).reshape(k // 512, 16, n))


def unpack_weight(words, scales, fmt):
    g, _, n = scales.shape
    words = np.ascontiguousarray(words).reshape(g, 128, n, -1)
    if fmt == "e4m3":
        vals = words.view(ml_dtypes.float8_e4m3fn).astype(np.float64)
    else:
        nib = np.empty((g, 128, n, 4), np.uint8)
        nib[..., 0::2] = words & 0xF
        nib[..., 1::2] = words >> 4
        vals = E2M1[nib]
    vals = vals * np.repeat(np.exp2(scales.astype(np.float64) - 127.0), 8, axis=1)[..., None]
    return vals.transpose(0, 1, 3, 2).reshape(g * 512, n)


def gelu(v):
    return 0.5 * v * (1.0 + np.tanh(np.sqrt(2.0 / np.pi) * (v + 0.044715 * v**3)))


def striped8(idx):
    return np.concatenate([v.reshape(-1, 16).T for v in idx]).astype(np.uint16)


def unstriped8(offs):
    return np.stack([offs[16 * g:16 * g + 16].T.reshape(-1) for g in range(8)]).astype(np.int64)


def runs(v, idx8):
    k = np.arange(v.shape[0])
    return v[k[:, None], idx8[k % 512 // 64]]


def put_heads(h, wgs, idx8, t2):
    r = np.arange(h.shape[0])
    page = np.zeros((h.shape[0], t2))
    page[r[:, None], idx8[r % 512 // 64]] = wgs[r // 4 % 128] * h
    return page


def often(T, S):
    return np.random.permutation(T)[(T * np.random.uniform(0, 1, S) ** 4).astype(np.int64)]


K, H, N, T, S, T2 = 512, 1024, 512, 2048, 1024, 2048


def setup_inputs():
    n = np.random.standard_normal
    s = mx_kscale(K)[:, None]
    u = mx_kscale(H)[:, None]
    tab_words, tab_scales = pack_weight(n((K, T)) * s, "e4m3")
    wa_words, wa_scales = pack_weight(1.5 * n((K, H)) / np.sqrt(K) / s, "e2m1")
    wb = n((K, H)) / np.sqrt(K) / s * u.T
    wc_words, wc_scales = pack_weight(1.5 * n((H, N)) / np.sqrt(H) / u, "e4m3")
    wd = (np.eye(K, N) + 0.5 * n((K, N)) / np.sqrt(K)) / s
    offs = striped8(np.stack([often(T, S) for _ in range(8)]))
    offs2 = striped8(np.stack([np.random.permutation(T2)[:S] for _ in range(8)]))
    wgo = np.repeat(np.random.uniform(0.5, 2.0, (8, S)), 16, axis=0)
    return {"tab_words": tab_words, "tab_scales": tab_scales,
            "wa_words": wa_words, "wa_scales": wa_scales,
            "wb": wb.astype(np.float32),
            "wc_words": wc_words, "wc_scales": wc_scales,
            "wd": wd.astype(np.float32),
            "bo": (0.5 * n(N)).astype(np.float32),
            "wgo": wgo.astype(np.float32),
            "offs": offs, "offs2": offs2}


def reference(tab_words, tab_scales, wa_words, wa_scales, wb, wc_words, wc_scales,
              wd, bo, wgo, offs, offs2):
    v = runs(unpack_weight(tab_words, tab_scales, "e4m3"), unstriped8(offs))
    wa = unpack_weight(wa_words, wa_scales, "e2m1")
    wc = unpack_weight(wc_words, wc_scales, "e4m3")
    a = wa.T @ v
    b = mxq(f64(wb), 0, "e4m3").T @ v
    h = a / (1.0 + np.exp(-a)) * b
    y = wc.T @ mxq(h, 0, "e4m3") + mxq(f64(wd), 0, "e4m3").T @ v
    y = y + f64(bo)[:, None]
    return put_heads(y, f64(wgo), unstriped8(offs2), T2)

@@ -1,0 +1,231 @@
+from contextlib import ExitStack
+
+import concourse.mybir as mybir
+
+K, H, N, T, S, T2 = 512, 1024, 512, 2048, 1024, 2048
+FLOPS = 2 * S * (2 * K * H + H * N + K * N)
+
+F32 = mybir.dt.float32
+BF16 = mybir.dt.bfloat16
+I32 = mybir.dt.int32
+U32 = mybir.dt.uint32
+U16 = mybir.dt.uint16
+U8 = mybir.dt.uint8
+FP8X4 = mybir.dt.float8_e4m3fn_x4
+FP4X4 = mybir.dt.float4_e2m1fn_x4
+ACT = mybir.ActivationFunctionType
+MULT = mybir.AluOpType.mult
+
+P = 128
+PACK = 4
+PASS = P * PACK
+HALF = 512
+JT = 128
+PARTS = 4
+
+
+def tile_list_beam_cache_rewrite_kernel(
+    tc, tab_words, tab_scales, wa_words, wa_scales, wb, wc_words, wc_scales, wd, bo, wgo, offs, offs2, out
+):
+    nc = tc.nc
+    with ExitStack() as ctx:
+        lists = ctx.enter_context(tc.tile_pool(name="lists", bufs=1))
+        keep = ctx.enter_context(tc.tile_pool(name="keep", bufs=1))
+        ring = ctx.enter_context(tc.tile_pool(name="ring", bufs=4))
+        psum = ctx.enter_context(tc.psum_pool(name="psum", bufs=3))
+        psum_y = ctx.enter_context(tc.psum_pool(name="psum_y", bufs=2))
+
+        pick = lists.tile([P, S // 16], U16, name="pick")
+        put = lists.tile([P, S // 16], U16, name="put")
+        tab_s = keep.tile([P, T], U8, name="tab_s", align_bytes=64)
+        ws_raw = keep.tile([P, 2 * H], U8, name="ws_raw", align_bytes=64)
+        w_raw = {0: keep.tile([P, PACK, PASS], F32, name="w_raw0", align_bytes=64)}
+        bias = keep.tile([P, PACK], F32, name="bias")
+        warm = keep.tile([P, 1], F32, name="warm", tag="wa_raw", align_bytes=64)
+        warm_out = keep.tile([P, 1], F32, name="warm_out", tag="tab_w", align_bytes=64)
+
+        wb_rows = wb.rearrange("(p i) c -> p i c", i=PACK)
+        nc.vector.memset(tab_s[:].bitcast(I32), 0)
+        nc.vector.memset(ws_raw[:].bitcast(I32), 0)
+        nc.gpsimd.memset(warm[:], 0.0)
+        nc.sync.dma_start(pick[:], offs)
+        nc.sync.dma_start(put[:], offs2)
+        nc.sync.dma_start(tab_s[0:P:8, :].bitcast(I32), tab_scales[0].bitcast(I32))
+        nc.sync.dma_start(ws_raw[0:P:8, 0:H].bitcast(I32), wa_scales[0].bitcast(I32))
+        nc.sync.dma_start(
+            ws_raw[0:P:8, H : 2 * H].bitcast(I32).rearrange("q (a c) -> q a c", a=2),
+            wc_scales.bitcast(I32).rearrange("a q c -> q a c"),
+        )
+        nc.scalar.activation(warm_out[:], warm[:], ACT.Silu)
+        nc.sync.dma_start(w_raw[0][:], wb_rows[:, :, 0:PASS])
+        wa_raw = keep.tile([P, 2 * H], U8, name="wa_raw", align_bytes=64)
+        tab_w = keep.tile([P, T], I32, name="tab_w", align_bytes=64)
+        nc.sync.dma_start(wa_raw[:].bitcast(I32), wa_words[0].bitcast(I32))
+        nc.sync.dma_start(tab_w[:], tab_words[0].rearrange("p t i -> p (t i)").bitcast(I32))
+        nc.gpsimd.dma_start(bias[:], bo.rearrange("(p i) -> p i", i=PACK))
+
+        pages = {0: keep.tile([P, T2], F32, name="page0")}
+        nc.vector.memset(pages[0][:], 0.0)
+
+        picked_s = keep.tile([P, S], U8, name="picked_s", align_bytes=64)
+        planes = keep.tile([P, S + 2 * H], U8, name="planes", align_bytes=64)
+        v_w = keep.tile([P, S], U32, name="v_w", align_bytes=64)
+        nc.vector.tensor_copy(picked_s[:], tab_s[:].indirect(pick[:]))
+        nc.vector.tensor_copy(planes[:, 0:S].bitcast(I32), picked_s[:].bitcast(I32))
+        nc.vector.tensor_copy(
+            planes[:, S:].rearrange("p (b t g m) -> p b g t m", b=4, t=PACK, m=16),
+            ws_raw[:].rearrange("p (b g m t) -> p b g t m", b=4, t=PACK, m=16),
+        )
+        for r in range(1, 4):
+            nc.sync.dma_start(planes[r:P:32, :].bitcast(I32), planes[8 * r : P : 32, :].bitcast(I32))
+        v_s = planes[:, 0:S]
+        wa_s = planes[:, S : S + H]
+        wc_s = planes[:, S + H :]
+
+        w_raw[1] = keep.tile([P, PACK, PASS], F32, name="w_raw1", tag="tab_s", align_bytes=64)
+        nc.sync.dma_start(w_raw[1][:], wb_rows[:, :, PASS : 2 * PASS])
+
+        wa_p = keep.tile([P, 2 * H], U8, name="wa_p", align_bytes=64)
+        wc_p = keep.tile([P, 2 * N], I32, name="wc_p", align_bytes=64)
+        nc.vector.tensor_copy(
+            wa_p[:].bitcast(U16).rearrange("p (b t g m) -> p b g t m", b=2, t=PACK, m=8),
+            wa_raw[:].bitcast(U16).rearrange("p (b g m t) -> p b g t m", b=2, t=PACK, m=8),
+        )
+        wc_raw = keep.tile([P, 2 * N], I32, name="wc_raw", tag="wa_raw", align_bytes=64)
+        nc.sync.dma_start(
+            wc_raw[:].rearrange("p (a c) -> p a c", a=2),
+            wc_words.rearrange("a p c i -> p a (c i)").bitcast(I32),
+        )
+
+        w_bf = [keep.tile([P, PACK * PASS], BF16, name=f"w_bf{n}", align_bytes=64) for n in range(3)]
+        w_q = [keep.tile([P, PASS], U32, name=f"w_q{n}", align_bytes=64) for n in range(3)]
+        w_s = [keep.tile([P, PASS], U8, name=f"w_s{n}", align_bytes=64) for n in range(3)]
+
+        def round_weight(n, part):
+            ms = slice(part * P // PARTS, (part + 1) * P // PARTS)
+            nc.scalar.copy(
+                w_bf[n][:].rearrange("p (t m i) -> p m t i", t=PACK, i=PACK)[:, ms],
+                w_raw[n][:].rearrange("p i (m t) -> p m t i", t=PACK)[:, ms],
+            )
+
+        def quantise_weight(n):
+            nc.vector.quantize_mx(out=w_q[n][:].bitcast(FP8X4), scales=w_s[n][:], in_=w_bf[n][:])
+
+        def gather_words(c):
+            nc.vector.tensor_copy(
+                v_w[:, c * HALF : (c + 1) * HALF],
+                tab_w[:].bitcast(U32).indirect(pick[:, c * HALF // 16 : (c + 1) * HALF // 16]),
+            )
+
+        h_q = [keep.tile([P, S], U32, name=f"h_q{b}", align_bytes=64) for b in range(2)]
+        h_s = [keep.tile([P, S], U8, name=f"h_s{b}", align_bytes=64) for b in range(2)]
+
+        def hidden(b, c, beside):
+            h_bf = keep.tile([P, PACK * HALF], BF16, name=f"h_bf{b}{c}", align_bytes=64)
+            for u in range(HALF // JT):
+                js = slice(c * HALF + u * JT, c * HALF + (u + 1) * JT)
+                gate = psum.tile([P, PACK, JT], F32, name="gate")
+                up = psum.tile([P, PACK, JT], F32, name="up")
+                for t in range(PACK):
+                    col = b * PASS + t * P
+                    nc.tensor.matmul_mx(
+                        out=gate[:, t, :],
+                        lhsT=wa_p[:, 2 * col : 2 * (col + P)].bitcast(FP4X4),
+                        lhsT_scale=wa_s[:, col : col + P],
+                        rhs=v_w[:, js].bitcast(FP8X4),
+                        rhs_scale=v_s[:, js],
+                        start=True,
+                        stop=True,
+                    )
+                for t in range(PACK):
+                    nc.tensor.matmul_mx(
+                        out=up[:, t, :],
+                        lhsT=w_q[b][:, t * P : (t + 1) * P].bitcast(FP8X4),
+                        lhsT_scale=w_s[b][:, t * P : (t + 1) * P],
+                        rhs=v_w[:, js].bitcast(FP8X4),
+                        rhs_scale=v_s[:, js],
+                        start=True,
+                        stop=True,
+                    )
+                act = ring.tile([P, JT, PACK], F32, name="act")
+                nc.scalar.activation(act[:], gate[:].rearrange("p t j -> p j t"), ACT.Silu)
+                nc.vector.tensor_tensor(
+                    h_bf[:, u * JT * PACK : (u + 1) * JT * PACK].rearrange("p (j t) -> p j t", t=PACK),
+                    up[:].rearrange("p t j -> p j t"),
+                    act[:],
+                    MULT,
+                )
+                if u < len(beside):
+                    round_weight(*beside[u])
+            cs = slice(c * HALF, (c + 1) * HALF)
+            nc.vector.quantize_mx(out=h_q[b][:, cs].bitcast(FP8X4), scales=h_s[b][:, cs], in_=h_bf[:])
+
+        for part in range(PARTS):
+            round_weight(0, part)
+        quantise_weight(0)
+        gather_words(0)
+        gather_words(1)
+        w_raw[2] = keep.tile([P, PACK, PASS], F32, name="w_raw2", tag="tab_w", align_bytes=64)
+        nc.sync.dma_start(w_raw[2][:], wd.rearrange("(p i) c -> p i c", i=PACK))
+        hidden(0, 0, [(1, part) for part in range(PARTS)])
+        quantise_weight(1)
+        nc.vector.tensor_copy(
+            wc_p[:].rearrange("p (a t g m) -> p a g t m", a=2, t=PACK, m=4),
+            wc_raw[:].rearrange("p (a g m t) -> p a g t m", a=2, t=PACK, m=4),
+        )
+        weight = keep.tile([P, S], F32, name="weight", tag="wa_raw", align_bytes=64)
+        nc.sync.dma_start(weight[:], wgo)
+        hidden(0, 1, [(2, 0), (2, 1)])
+        hidden(1, 0, [(2, 2), (2, 3)])
+        quantise_weight(2)
+        hidden(1, 1, [])
+
+        def result(i, c, y):
+            cs = slice(c * HALF, (c + 1) * HALF)
+            acc = psum_y.tile([P, HALF], F32, name="acc")
+            nc.tensor.matmul_mx(
+                out=acc[:],
+                lhsT=w_q[2][:, i * P : (i + 1) * P].bitcast(FP8X4),
+                lhsT_scale=w_s[2][:, i * P : (i + 1) * P],
+                rhs=v_w[:, cs].bitcast(FP8X4),
+                rhs_scale=v_s[:, cs],
+                start=True,
+                stop=False,
+            )
+            for a in range(2):
+                col = a * N + i * P
+                nc.tensor.matmul_mx(
+                    out=acc[:],
+                    lhsT=wc_p[:, col : col + P].bitcast(FP8X4),
+                    lhsT_scale=wc_s[:, col : col + P],
+                    rhs=h_q[a][:, cs].bitcast(FP8X4),
+                    rhs_scale=h_s[a][:, cs],
+                    start=False,
+                    stop=(a == 1),
+                )
+            nc.scalar.activation(y, acc[:], ACT.Identity, bias=bias[:, i : i + 1])
+
+        def clear_page(i, tag):
+            pages[i] = keep.tile([P, T2], F32, name=f"page{i}", tag=tag)
+            nc.gpsimd.memset(pages[i][:], 0.0)
+
+        out_rows = out.rearrange("(p i) t -> p i t", i=PACK)
+        for c in range(2):
+            y = keep.tile([P, HALF], F32, name=f"y0{c}")
+            result(0, c, y[:])
+            nc.vector.tensor_tensor(
+                pages[0][:].indirect(put[:, c * HALF // 16 : (c + 1) * HALF // 16]),
+                y[:],
+                weight[:, c * HALF : (c + 1) * HALF],
+                MULT,
+            )
+            clear_page(c + 1, f"y0{c}")
+        nc.sync.dma_start(out_rows[:, 0, :], pages[0][:])
+        for i in range(1, PACK):
+            y = keep.tile([P, S], F32, name=f"y{i}")
+            for c in range(2):
+                result(i, c, y[:, c * HALF : (c + 1) * HALF])
+            nc.vector.tensor_tensor(pages[i][:].indirect(put[:]), y[:], weight[:], MULT)
+            if i == 1:
+                clear_page(3, "y1")
+            nc.sync.dma_start(out_rows[:, i, :], pages[i][:])

@@ -22,6 +22,7 @@ PASS = P * PACK
 HALF = 512
 JT = 128
 PARTS = 4
+WC_ROW = 4
 
 
 def tile_list_beam_cache_rewrite_kernel(
@@ -38,52 +39,57 @@ def tile_list_beam_cache_rewrite_kernel(
         pick = lists.tile([P, S // 16], U16, name="pick")
         put = lists.tile([P, S // 16], U16, name="put")
         tab_s = keep.tile([P, T], U8, name="tab_s", align_bytes=64)
-        ws_raw = keep.tile([P, 2 * H], U8, name="ws_raw", align_bytes=64)
+        ws_raw = keep.tile([P, H], U8, name="ws_raw", align_bytes=64)
+        wa_raw = keep.tile([P, 2 * H], U8, name="wa_raw", align_bytes=64)
         w_raw = {0: keep.tile([P, PACK, PASS], F32, name="w_raw0", align_bytes=64)}
         bias = keep.tile([P, PACK], F32, name="bias")
-        warm = keep.tile([P, 1], F32, name="warm", tag="wa_raw", align_bytes=64)
-        warm_out = keep.tile([P, 1], F32, name="warm_out", tag="tab_w", align_bytes=64)
+        warm = keep.tile([P, 1], F32, name="warm", tag="tab_w", align_bytes=64)
+        warm_out = keep.tile([P, 1], F32, name="warm_out", tag="w_raw1", align_bytes=64)
 
         wb_rows = wb.rearrange("(p i) c -> p i c", i=PACK)
-        nc.vector.memset(tab_s[:].bitcast(I32), 0)
-        nc.vector.memset(ws_raw[:].bitcast(I32), 0)
         nc.gpsimd.memset(warm[:], 0.0)
+        nc.gpsimd.memset(tab_s[:].bitcast(I32), 0)
+        nc.vector.memset(ws_raw[:].bitcast(I32), 0)
         nc.sync.dma_start(pick[:], offs)
         nc.sync.dma_start(put[:], offs2)
         nc.sync.dma_start(tab_s[0:P:8, :].bitcast(I32), tab_scales[0].bitcast(I32))
-        nc.sync.dma_start(ws_raw[0:P:8, 0:H].bitcast(I32), wa_scales[0].bitcast(I32))
+        nc.sync.dma_start(ws_raw[0:P:8, :].bitcast(I32), wa_scales[0].bitcast(I32))
         nc.sync.dma_start(
-            ws_raw[0:P:8, H : 2 * H].bitcast(I32).rearrange("q (a c) -> q a c", a=2),
+            ws_raw[WC_ROW:P:8, :].bitcast(I32).rearrange("q (a c) -> q a c", a=2),
             wc_scales.bitcast(I32).rearrange("a q c -> q a c"),
         )
         nc.scalar.activation(warm_out[:], warm[:], ACT.Silu)
-        nc.sync.dma_start(w_raw[0][:], wb_rows[:, :, 0:PASS])
-        wa_raw = keep.tile([P, 2 * H], U8, name="wa_raw", align_bytes=64)
-        tab_w = keep.tile([P, T], I32, name="tab_w", align_bytes=64)
         nc.sync.dma_start(wa_raw[:].bitcast(I32), wa_words[0].bitcast(I32))
+        nc.sync.dma_start(w_raw[0][:], wb_rows[:, :, 0:PASS])
+        tab_w = keep.tile([P, T], I32, name="tab_w", align_bytes=64)
+        w_raw[1] = keep.tile([P, PACK, PASS], F32, name="w_raw1", align_bytes=64)
         nc.sync.dma_start(tab_w[:], tab_words[0].rearrange("p t i -> p (t i)").bitcast(I32))
+        nc.sync.dma_start(w_raw[1][:], wb_rows[:, :, PASS : 2 * PASS])
         nc.gpsimd.dma_start(bias[:], bo.rearrange("(p i) -> p i", i=PACK))
 
-        pages = {0: keep.tile([P, T2], F32, name="page0")}
-        nc.vector.memset(pages[0][:], 0.0)
+        pages = {}
+        for i in range(2):
+            pages[i] = keep.tile([P, T2], F32, name=f"page{i}")
+            nc.vector.memset(pages[i][:], 0.0)
 
         picked_s = keep.tile([P, S], U8, name="picked_s", align_bytes=64)
-        planes = keep.tile([P, S + 2 * H], U8, name="planes", align_bytes=64)
+        planes = keep.tile([P, S + H], U8, name="planes", align_bytes=64)
         v_w = keep.tile([P, S], U32, name="v_w", align_bytes=64)
         nc.vector.tensor_copy(picked_s[:], tab_s[:].indirect(pick[:]))
-        nc.vector.tensor_copy(planes[:, 0:S].bitcast(I32), picked_s[:].bitcast(I32))
         nc.vector.tensor_copy(
-            planes[:, S:].rearrange("p (b t g m) -> p b g t m", b=4, t=PACK, m=16),
-            ws_raw[:].rearrange("p (b g m t) -> p b g t m", b=4, t=PACK, m=16),
+            planes[:, S:].rearrange("p (b t g m) -> p b g t m", b=2, t=PACK, m=16),
+            ws_raw[:].rearrange("p (b g m t) -> p b g t m", b=2, t=PACK, m=16),
         )
+        nc.vector.tensor_copy(planes[:, 0:S].bitcast(I32), picked_s[:].bitcast(I32))
         for r in range(1, 4):
             nc.sync.dma_start(planes[r:P:32, :].bitcast(I32), planes[8 * r : P : 32, :].bitcast(I32))
+        for r in range(1, 4):
+            nc.sync.dma_start(
+                planes[WC_ROW + r : P : 32, S:].bitcast(I32), planes[WC_ROW + 8 * r : P : 32, S:].bitcast(I32)
+            )
         v_s = planes[:, 0:S]
-        wa_s = planes[:, S : S + H]
-        wc_s = planes[:, S + H :]
-
-        w_raw[1] = keep.tile([P, PACK, PASS], F32, name="w_raw1", tag="tab_s", align_bytes=64)
-        nc.sync.dma_start(w_raw[1][:], wb_rows[:, :, PASS : 2 * PASS])
+        wa_s = planes[:, S:]
+        wc_s = planes[WC_ROW:, S:]
 
         wa_p = keep.tile([P, 2 * H], U8, name="wa_p", align_bytes=64)
         wc_p = keep.tile([P, 2 * N], I32, name="wc_p", align_bytes=64)
@@ -91,14 +97,14 @@ def tile_list_beam_cache_rewrite_kernel(
             wa_p[:].bitcast(U16).rearrange("p (b t g m) -> p b g t m", b=2, t=PACK, m=8),
             wa_raw[:].bitcast(U16).rearrange("p (b g m t) -> p b g t m", b=2, t=PACK, m=8),
         )
-        wc_raw = keep.tile([P, 2 * N], I32, name="wc_raw", tag="wa_raw", align_bytes=64)
+        wc_raw = keep.tile([P, 2 * N], I32, name="wc_raw", tag="picked_s", align_bytes=64)
         nc.sync.dma_start(
             wc_raw[:].rearrange("p (a c) -> p a c", a=2),
             wc_words.rearrange("a p c i -> p a (c i)").bitcast(I32),
         )
 
         w_bf = [keep.tile([P, PACK * PASS], BF16, name=f"w_bf{n}", align_bytes=64) for n in range(3)]
-        w_q = [keep.tile([P, PASS], U32, name=f"w_q{n}", align_bytes=64) for n in range(3)]
+        w_q = {}
         w_s = [keep.tile([P, PASS], U8, name=f"w_s{n}", align_bytes=64) for n in range(3)]
 
         def round_weight(n, part):
@@ -108,7 +114,8 @@ def tile_list_beam_cache_rewrite_kernel(
                 w_raw[n][:].rearrange("p i (m t) -> p m t i", t=PACK)[:, ms],
             )
 
-        def quantise_weight(n):
+        def quantise_weight(n, tag):
+            w_q[n] = keep.tile([P, PASS], U32, name=f"w_q{n}", tag=tag, align_bytes=64)
             nc.vector.quantize_mx(out=w_q[n][:].bitcast(FP8X4), scales=w_s[n][:], in_=w_bf[n][:])
 
         def gather_words(c):
@@ -120,8 +127,10 @@ def tile_list_beam_cache_rewrite_kernel(
         h_q = [keep.tile([P, S], U32, name=f"h_q{b}", align_bytes=64) for b in range(2)]
         h_s = [keep.tile([P, S], U8, name=f"h_s{b}", align_bytes=64) for b in range(2)]
 
+        h_bf = {}
+
         def hidden(b, c, beside):
-            h_bf = keep.tile([P, PACK * HALF], BF16, name=f"h_bf{b}{c}", align_bytes=64)
+            h_bf[b, c] = keep.tile([P, PACK * HALF], BF16, name=f"h_bf{b}{c}", align_bytes=64)
             for u in range(HALF // JT):
                 js = slice(c * HALF + u * JT, c * HALF + (u + 1) * JT)
                 gate = psum.tile([P, PACK, JT], F32, name="gate")
@@ -150,35 +159,63 @@ def tile_list_beam_cache_rewrite_kernel(
                 act = ring.tile([P, JT, PACK], F32, name="act")
                 nc.scalar.activation(act[:], gate[:].rearrange("p t j -> p j t"), ACT.Silu)
                 nc.vector.tensor_tensor(
-                    h_bf[:, u * JT * PACK : (u + 1) * JT * PACK].rearrange("p (j t) -> p j t", t=PACK),
+                    h_bf[b, c][:, u * JT * PACK : (u + 1) * JT * PACK].rearrange("p (j t) -> p j t", t=PACK),
                     up[:].rearrange("p t j -> p j t"),
                     act[:],
                     MULT,
                 )
-                if u < len(beside):
-                    round_weight(*beside[u])
+                for step in beside.get(u, ()):
+                    step()
+
+        def quantise_hidden(b, c):
             cs = slice(c * HALF, (c + 1) * HALF)
-            nc.vector.quantize_mx(out=h_q[b][:, cs].bitcast(FP8X4), scales=h_s[b][:, cs], in_=h_bf[:])
+            nc.vector.quantize_mx(out=h_q[b][:, cs].bitcast(FP8X4), scales=h_s[b][:, cs], in_=h_bf[b, c][:])
+
+        def clear_page(i, tag):
+            pages[i] = keep.tile([P, T2], F32, name=f"page{i}", tag=tag, align_bytes=64)
+            nc.gpsimd.memset(pages[i][:], 0.0)
 
         for part in range(PARTS):
             round_weight(0, part)
-        quantise_weight(0)
+        quantise_weight(0, "w_q0")
         gather_words(0)
         gather_words(1)
         w_raw[2] = keep.tile([P, PACK, PASS], F32, name="w_raw2", tag="tab_w", align_bytes=64)
         nc.sync.dma_start(w_raw[2][:], wd.rearrange("(p i) c -> p i c", i=PACK))
-        hidden(0, 0, [(1, part) for part in range(PARTS)])
-        quantise_weight(1)
+        for part in range(PARTS):
+            round_weight(1, part)
+        quantise_weight(1, "w_q1")
         nc.vector.tensor_copy(
             wc_p[:].rearrange("p (a t g m) -> p a g t m", a=2, t=PACK, m=4),
             wc_raw[:].rearrange("p (a g m t) -> p a g t m", a=2, t=PACK, m=4),
         )
-        weight = keep.tile([P, S], F32, name="weight", tag="wa_raw", align_bytes=64)
+        weight = keep.tile([P, S], F32, name="weight", tag="picked_s", align_bytes=64)
         nc.sync.dma_start(weight[:], wgo)
-        hidden(0, 1, [(2, 0), (2, 1)])
-        hidden(1, 0, [(2, 2), (2, 3)])
-        quantise_weight(2)
-        hidden(1, 1, [])
+        hidden(0, 0, {})
+        hidden(
+            0,
+            1,
+            {
+                0: [lambda: quantise_hidden(0, 0), lambda: clear_page(2, "h_bf00")],
+                1: [lambda: round_weight(2, 0)],
+                3: [lambda: round_weight(2, 1)],
+            },
+        )
+        hidden(
+            1,
+            0,
+            {
+                0: [lambda: quantise_hidden(0, 1), lambda: clear_page(3, "h_bf01")],
+                1: [lambda: round_weight(2, 2)],
+                3: [lambda: round_weight(2, 3)],
+            },
+        )
+        hidden(
+            1,
+            1,
+            {0: [lambda: quantise_hidden(1, 0), lambda: quantise_weight(2, "h_bf10")]},
+        )
+        quantise_hidden(1, 1)
 
         def result(i, c, y):
             cs = slice(c * HALF, (c + 1) * HALF)
@@ -205,27 +242,22 @@ def tile_list_beam_cache_rewrite_kernel(
                 )
             nc.scalar.activation(y, acc[:], ACT.Identity, bias=bias[:, i : i + 1])
 
-        def clear_page(i, tag):
-            pages[i] = keep.tile([P, T2], F32, name=f"page{i}", tag=tag)
-            nc.gpsimd.memset(pages[i][:], 0.0)
-
         out_rows = out.rearrange("(p i) t -> p i t", i=PACK)
         for c in range(2):
-            y = keep.tile([P, HALF], F32, name=f"y0{c}")
-            result(0, c, y[:])
-            nc.vector.tensor_tensor(
-                pages[0][:].indirect(put[:, c * HALF // 16 : (c + 1) * HALF // 16]),
-                y[:],
-                weight[:, c * HALF : (c + 1) * HALF],
-                MULT,
-            )
-            clear_page(c + 1, f"y0{c}")
-        nc.sync.dma_start(out_rows[:, 0, :], pages[0][:])
-        for i in range(1, PACK):
+            for i in range(2):
+                y = keep.tile([P, HALF], F32, name=f"y{i}{c}")
+                result(i, c, y[:])
+                nc.vector.tensor_tensor(
+                    pages[i][:].indirect(put[:, c * HALF // 16 : (c + 1) * HALF // 16]),
+                    y[:],
+                    weight[:, c * HALF : (c + 1) * HALF],
+                    MULT,
+                )
+                if c == 1:
+                    nc.sync.dma_start(out_rows[:, i, :], pages[i][:])
+        for i in range(2, PACK):
             y = keep.tile([P, S], F32, name=f"y{i}")
             for c in range(2):
                 result(i, c, y[:, c * HALF : (c + 1) * HALF])
             nc.vector.tensor_tensor(pages[i][:].indirect(put[:]), y[:], weight[:], MULT)
-            if i == 1:
-                clear_page(3, "y1")
             nc.sync.dma_start(out_rows[:, i, :], pages[i][:])

@@ -15,6 +15,7 @@ FP8X4 = mybir.dt.float8_e4m3fn_x4
 FP4X4 = mybir.dt.float4_e2m1fn_x4
 ACT = mybir.ActivationFunctionType
 MULT = mybir.AluOpType.mult
+ADD = mybir.AluOpType.add
 
 P = 128
 PACK = 4
@@ -41,7 +42,8 @@ def tile_list_beam_cache_rewrite_kernel(
         tab_s = keep.tile([P, T], U8, name="tab_s", align_bytes=64)
         ws_raw = keep.tile([P, H], U8, name="ws_raw", align_bytes=64)
         wa_raw = keep.tile([P, 2 * H], U8, name="wa_raw", align_bytes=64)
-        w_raw = {0: keep.tile([P, PACK, PASS], F32, name="w_raw0", align_bytes=64)}
+        w_raw = {}
+        first = [keep.tile([P, PACK, PASS // 2], F32, name=f"first{n}", align_bytes=64) for n in range(2)]
         bias = keep.tile([P, PACK], F32, name="bias")
         warm = keep.tile([P, 1], F32, name="warm", tag="tab_w", align_bytes=64)
         warm_out = keep.tile([P, 1], F32, name="warm_out", tag="w_raw1", align_bytes=64)
@@ -59,18 +61,17 @@ def tile_list_beam_cache_rewrite_kernel(
             wc_scales.bitcast(I32).rearrange("a q c -> q a c"),
         )
         nc.scalar.activation(warm_out[:], warm[:], ACT.Silu)
-        nc.sync.dma_start(wa_raw[:].bitcast(I32), wa_words[0].bitcast(I32))
-        nc.sync.dma_start(w_raw[0][:], wb_rows[:, :, 0:PASS])
+        nc.scalar.dma_start(wa_raw[:].bitcast(I32), wa_words[0].bitcast(I32))
+        for n in range(2):
+            nc.scalar.dma_start(first[n][:], wb_rows[:, :, n * PASS // 2 : (n + 1) * PASS // 2])
         tab_w = keep.tile([P, T], I32, name="tab_w", align_bytes=64)
         w_raw[1] = keep.tile([P, PACK, PASS], F32, name="w_raw1", align_bytes=64)
-        nc.sync.dma_start(tab_w[:], tab_words[0].rearrange("p t i -> p (t i)").bitcast(I32))
-        nc.sync.dma_start(w_raw[1][:], wb_rows[:, :, PASS : 2 * PASS])
+        nc.scalar.dma_start(tab_w[:], tab_words[0].rearrange("p t i -> p (t i)").bitcast(I32))
+        nc.scalar.dma_start(w_raw[1][:], wb_rows[:, :, PASS : 2 * PASS])
         nc.gpsimd.dma_start(bias[:], bo.rearrange("(p i) -> p i", i=PACK))
 
-        pages = {}
-        for i in range(2):
-            pages[i] = keep.tile([P, T2], F32, name=f"page{i}")
-            nc.vector.memset(pages[i][:], 0.0)
+        pages = {0: keep.tile([P, T2], F32, name="page0")}
+        nc.vector.memset(pages[0][:], 0.0)
 
         picked_s = keep.tile([P, S], U8, name="picked_s", align_bytes=64)
         planes = keep.tile([P, S + H], U8, name="planes", align_bytes=64)
@@ -103,7 +104,7 @@ def tile_list_beam_cache_rewrite_kernel(
             wc_words.rearrange("a p c i -> p a (c i)").bitcast(I32),
         )
 
-        w_bf = [keep.tile([P, PACK * PASS], BF16, name=f"w_bf{n}", align_bytes=64) for n in range(3)]
+        w_bf = [keep.tile([P, PACK * PASS], BF16, name=f"w_bf{n}", align_bytes=64) for n in range(2)]
         w_q = {}
         w_s = [keep.tile([P, PASS], U8, name=f"w_s{n}", align_bytes=64) for n in range(3)]
 
@@ -171,50 +172,49 @@ def tile_list_beam_cache_rewrite_kernel(
             cs = slice(c * HALF, (c + 1) * HALF)
             nc.vector.quantize_mx(out=h_q[b][:, cs].bitcast(FP8X4), scales=h_s[b][:, cs], in_=h_bf[b, c][:])
 
-        def clear_page(i, tag):
-            pages[i] = keep.tile([P, T2], F32, name=f"page{i}", tag=tag, align_bytes=64)
-            nc.gpsimd.memset(pages[i][:], 0.0)
+        wd_bf = {}
 
-        for part in range(PARTS):
-            round_weight(0, part)
+        def round_wd(half, tag):
+            wd_bf[half] = keep.tile([P, 2 * PASS], BF16, name=f"wd_bf{half}", tag=tag, align_bytes=64)
+            nc.gpsimd.tensor_scalar(
+                wd_bf[half][:].rearrange("p (t m i) -> p m t i", t=2, i=PACK),
+                w_raw[2][:].rearrange("p i (m t) -> p m t i", t=PACK)[:, :, 2 * half : 2 * half + 2],
+                1.0,
+                0.0,
+                MULT,
+                ADD,
+            )
+
+        def quantise_wd():
+            w_q[2] = keep.tile([P, PASS], U32, name="w_q2", tag="h_bf10", align_bytes=64)
+            for half in range(2):
+                cols = slice(half * 2 * P, (half + 1) * 2 * P)
+                nc.vector.quantize_mx(out=w_q[2][:, cols].bitcast(FP8X4), scales=w_s[2][:, cols], in_=wd_bf[half][:])
+
+        for n in range(2):
+            nc.scalar.copy(
+                w_bf[0][:].rearrange("p (t m i) -> p m t i", t=PACK, i=PACK)[:, n * P // 2 : (n + 1) * P // 2],
+                first[n][:].rearrange("p i (m t) -> p m t i", t=PACK),
+            )
         quantise_weight(0, "w_q0")
         gather_words(0)
         gather_words(1)
         w_raw[2] = keep.tile([P, PACK, PASS], F32, name="w_raw2", tag="tab_w", align_bytes=64)
         nc.sync.dma_start(w_raw[2][:], wd.rearrange("(p i) c -> p i c", i=PACK))
-        for part in range(PARTS):
-            round_weight(1, part)
-        quantise_weight(1, "w_q1")
         nc.vector.tensor_copy(
             wc_p[:].rearrange("p (a t g m) -> p a g t m", a=2, t=PACK, m=4),
             wc_raw[:].rearrange("p (a g m t) -> p a g t m", a=2, t=PACK, m=4),
         )
         weight = keep.tile([P, S], F32, name="weight", tag="picked_s", align_bytes=64)
         nc.sync.dma_start(weight[:], wgo)
-        hidden(0, 0, {})
+        hidden(0, 0, {u: [lambda u=u: round_weight(1, u)] for u in range(PARTS)})
         hidden(
             0,
             1,
-            {
-                0: [lambda: quantise_hidden(0, 0), lambda: clear_page(2, "h_bf00")],
-                1: [lambda: round_weight(2, 0)],
-                3: [lambda: round_weight(2, 1)],
-            },
+            {0: [lambda: quantise_hidden(0, 0), lambda: quantise_weight(1, "h_bf00"), lambda: round_wd(0, "w_bf1")]},
         )
-        hidden(
-            1,
-            0,
-            {
-                0: [lambda: quantise_hidden(0, 1), lambda: clear_page(3, "h_bf01")],
-                1: [lambda: round_weight(2, 2)],
-                3: [lambda: round_weight(2, 3)],
-            },
-        )
-        hidden(
-            1,
-            1,
-            {0: [lambda: quantise_hidden(1, 0), lambda: quantise_weight(2, "h_bf10")]},
-        )
+        hidden(1, 0, {0: [lambda: quantise_hidden(0, 1), lambda: round_wd(1, "h_bf01")]})
+        hidden(1, 1, {0: [lambda: quantise_hidden(1, 0), quantise_wd]})
         quantise_hidden(1, 1)
 
         def result(i, c, y):
@@ -242,22 +242,27 @@ def tile_list_beam_cache_rewrite_kernel(
                 )
             nc.scalar.activation(y, acc[:], ACT.Identity, bias=bias[:, i : i + 1])
 
+        def clear_page(i, tag):
+            pages[i] = keep.tile([P, T2], F32, name=f"page{i}", tag=tag)
+            nc.gpsimd.memset(pages[i][:], 0.0)
+
         out_rows = out.rearrange("(p i) t -> p i t", i=PACK)
         for c in range(2):
-            for i in range(2):
-                y = keep.tile([P, HALF], F32, name=f"y{i}{c}")
-                result(i, c, y[:])
-                nc.vector.tensor_tensor(
-                    pages[i][:].indirect(put[:, c * HALF // 16 : (c + 1) * HALF // 16]),
-                    y[:],
-                    weight[:, c * HALF : (c + 1) * HALF],
-                    MULT,
-                )
-                if c == 1:
-                    nc.sync.dma_start(out_rows[:, i, :], pages[i][:])
-        for i in range(2, PACK):
+            y = keep.tile([P, HALF], F32, name=f"y0{c}")
+            result(0, c, y[:])
+            nc.vector.tensor_tensor(
+                pages[0][:].indirect(put[:, c * HALF // 16 : (c + 1) * HALF // 16]),
+                y[:],
+                weight[:, c * HALF : (c + 1) * HALF],
+                MULT,
+            )
+            clear_page(c + 1, f"y0{c}")
+        nc.sync.dma_start(out_rows[:, 0, :], pages[0][:])
+        for i in range(1, PACK):
             y = keep.tile([P, S], F32, name=f"y{i}")
             for c in range(2):
                 result(i, c, y[:, c * HALF : (c + 1) * HALF])
             nc.vector.tensor_tensor(pages[i][:].indirect(put[:]), y[:], weight[:], MULT)
+            if i == 1:
+                clear_page(3, "y1")
             nc.sync.dma_start(out_rows[:, i, :], pages[i][:])

@@ -22,7 +22,7 @@ PACK = 4
 PASS = P * PACK
 HALF = 512
 JT = 128
-PARTS = 4
+QUARTER = 256
 WC_ROW = 4
 
 
@@ -43,31 +43,35 @@ def tile_list_beam_cache_rewrite_kernel(
         ws_raw = keep.tile([P, H], U8, name="ws_raw", align_bytes=64)
         wa_raw = keep.tile([P, 2 * H], U8, name="wa_raw", align_bytes=64)
         w_raw = {}
-        first = [keep.tile([P, PACK, PASS // 2], F32, name=f"first{n}", align_bytes=64) for n in range(2)]
+        wb_raw = {}
+
+        def load_wb(n, tag):
+            wb_raw[n] = keep.tile([P, PACK, QUARTER], F32, name=f"wb_raw{n}", tag=tag, align_bytes=64)
+            nc.sync.dma_start(wb_raw[n][:], wb_rows[:, :, n * QUARTER : (n + 1) * QUARTER])
+
         bias = keep.tile([P, PACK], F32, name="bias")
         warm = keep.tile([P, 1], F32, name="warm", tag="tab_w", align_bytes=64)
-        warm_out = keep.tile([P, 1], F32, name="warm_out", tag="w_raw1", align_bytes=64)
+        warm_out = keep.tile([P, 1], F32, name="warm_out")
 
         wb_rows = wb.rearrange("(p i) c -> p i c", i=PACK)
         nc.gpsimd.memset(warm[:], 0.0)
-        nc.gpsimd.memset(tab_s[:].bitcast(I32), 0)
         nc.vector.memset(ws_raw[:].bitcast(I32), 0)
         nc.sync.dma_start(pick[:], offs)
+        nc.sync.dma_start(
+            tab_s[:].bitcast(I32), tab_scales[0].bitcast(I32).unsqueeze(1).to_broadcast([16, 8, T // 4])
+        )
         nc.sync.dma_start(put[:], offs2)
-        nc.sync.dma_start(tab_s[0:P:8, :].bitcast(I32), tab_scales[0].bitcast(I32))
         nc.sync.dma_start(ws_raw[0:P:8, :].bitcast(I32), wa_scales[0].bitcast(I32))
         nc.sync.dma_start(
             ws_raw[WC_ROW:P:8, :].bitcast(I32).rearrange("q (a c) -> q a c", a=2),
             wc_scales.bitcast(I32).rearrange("a q c -> q a c"),
         )
         nc.scalar.activation(warm_out[:], warm[:], ACT.Silu)
-        nc.scalar.dma_start(wa_raw[:].bitcast(I32), wa_words[0].bitcast(I32))
-        for n in range(2):
-            nc.scalar.dma_start(first[n][:], wb_rows[:, :, n * PASS // 2 : (n + 1) * PASS // 2])
+        nc.sync.dma_start(wa_raw[:].bitcast(I32), wa_words[0].bitcast(I32))
+        load_wb(0, "wb_raw0")
+        load_wb(1, "wb_raw1")
         tab_w = keep.tile([P, T], I32, name="tab_w", align_bytes=64)
-        w_raw[1] = keep.tile([P, PACK, PASS], F32, name="w_raw1", align_bytes=64)
-        nc.scalar.dma_start(tab_w[:], tab_words[0].rearrange("p t i -> p (t i)").bitcast(I32))
-        nc.scalar.dma_start(w_raw[1][:], wb_rows[:, :, PASS : 2 * PASS])
+        nc.sync.dma_start(tab_w[:], tab_words[0].rearrange("p t i -> p (t i)").bitcast(I32))
         nc.gpsimd.dma_start(bias[:], bo.rearrange("(p i) -> p i", i=PACK))
 
         pages = {0: keep.tile([P, T2], F32, name="page0")}
@@ -77,6 +81,7 @@ def tile_list_beam_cache_rewrite_kernel(
         planes = keep.tile([P, S + H], U8, name="planes", align_bytes=64)
         v_w = keep.tile([P, S], U32, name="v_w", align_bytes=64)
         nc.vector.tensor_copy(picked_s[:], tab_s[:].indirect(pick[:]))
+        load_wb(2, "tab_s")
         nc.vector.tensor_copy(
             planes[:, S:].rearrange("p (b t g m) -> p b g t m", b=2, t=PACK, m=16),
             ws_raw[:].rearrange("p (b g m t) -> p b g t m", b=2, t=PACK, m=16),
@@ -84,35 +89,29 @@ def tile_list_beam_cache_rewrite_kernel(
         nc.vector.tensor_copy(planes[:, 0:S].bitcast(I32), picked_s[:].bitcast(I32))
         for r in range(1, 4):
             nc.sync.dma_start(planes[r:P:32, :].bitcast(I32), planes[8 * r : P : 32, :].bitcast(I32))
-        for r in range(1, 4):
-            nc.sync.dma_start(
-                planes[WC_ROW + r : P : 32, S:].bitcast(I32), planes[WC_ROW + 8 * r : P : 32, S:].bitcast(I32)
-            )
+        load_wb(3, "ws_raw")
+        wc_s = keep.tile([P, H], U8, name="wc_s", align_bytes=64)
+        nc.gpsimd.memset(wc_s[:].bitcast(I32), 0)
+        for r in range(4):
+            nc.sync.dma_start(wc_s[r:P:32, :].bitcast(I32), planes[WC_ROW + 8 * r : P : 32, S:].bitcast(I32))
         v_s = planes[:, 0:S]
         wa_s = planes[:, S:]
-        wc_s = planes[WC_ROW:, S:]
 
         wa_p = keep.tile([P, 2 * H], U8, name="wa_p", align_bytes=64)
-        wc_p = keep.tile([P, 2 * N], I32, name="wc_p", align_bytes=64)
         nc.vector.tensor_copy(
             wa_p[:].bitcast(U16).rearrange("p (b t g m) -> p b g t m", b=2, t=PACK, m=8),
             wa_raw[:].bitcast(U16).rearrange("p (b g m t) -> p b g t m", b=2, t=PACK, m=8),
         )
-        wc_raw = keep.tile([P, 2 * N], I32, name="wc_raw", tag="picked_s", align_bytes=64)
-        nc.sync.dma_start(
-            wc_raw[:].rearrange("p (a c) -> p a c", a=2),
-            wc_words.rearrange("a p c i -> p a (c i)").bitcast(I32),
-        )
-
         w_bf = [keep.tile([P, PACK * PASS], BF16, name=f"w_bf{n}", align_bytes=64) for n in range(2)]
         w_q = {}
         w_s = [keep.tile([P, PASS], U8, name=f"w_s{n}", align_bytes=64) for n in range(3)]
 
-        def round_weight(n, part):
-            ms = slice(part * P // PARTS, (part + 1) * P // PARTS)
+        def round_wb(n, part):
+            ms = slice(part * 32, (part + 1) * 32)
+            first = (n % 2) * 64 + part * 32
             nc.scalar.copy(
-                w_bf[n][:].rearrange("p (t m i) -> p m t i", t=PACK, i=PACK)[:, ms],
-                w_raw[n][:].rearrange("p i (m t) -> p m t i", t=PACK)[:, ms],
+                w_bf[n // 2][:].rearrange("p (t m i) -> p m t i", t=PACK, i=PACK)[:, first : first + 32],
+                wb_raw[n][:].rearrange("p i (m t) -> p m t i", t=PACK)[:, ms],
             )
 
         def quantise_weight(n, tag):
@@ -157,7 +156,10 @@ def tile_list_beam_cache_rewrite_kernel(
                         start=True,
                         stop=True,
                     )
-                act = ring.tile([P, JT, PACK], F32, name="act")
+                if (b, c, u) == (1, 1, HALF // JT - 1):
+                    act = keep.tile([P, JT, PACK], F32, name="last_act", tag="y00")
+                else:
+                    act = ring.tile([P, JT, PACK], F32, name="act")
                 nc.scalar.activation(act[:], gate[:].rearrange("p t j -> p j t"), ACT.Silu)
                 nc.vector.tensor_tensor(
                     h_bf[b, c][:, u * JT * PACK : (u + 1) * JT * PACK].rearrange("p (j t) -> p j t", t=PACK),
@@ -191,28 +193,54 @@ def tile_list_beam_cache_rewrite_kernel(
                 cols = slice(half * 2 * P, (half + 1) * 2 * P)
                 nc.vector.quantize_mx(out=w_q[2][:, cols].bitcast(FP8X4), scales=w_s[2][:, cols], in_=wd_bf[half][:])
 
-        for n in range(2):
-            nc.scalar.copy(
-                w_bf[0][:].rearrange("p (t m i) -> p m t i", t=PACK, i=PACK)[:, n * P // 2 : (n + 1) * P // 2],
-                first[n][:].rearrange("p i (m t) -> p m t i", t=PACK),
+        late = {}
+
+        def order_wc():
+            late["wc"] = keep.tile([P, 2 * N], I32, name="wc_p", tag="w_bf1", align_bytes=64)
+            nc.vector.tensor_copy(
+                late["wc"][:].rearrange("p (a t g m) -> p a g t m", a=2, t=PACK, m=4),
+                wc_raw[:].rearrange("p (a g m t) -> p a g t m", a=2, t=PACK, m=4),
             )
+
+        for n in range(2):
+            for part in range(2):
+                round_wb(n, part)
+        wc_raw = keep.tile([P, 2 * N], I32, name="wc_raw", tag="wb_raw1", align_bytes=64)
+        nc.sync.dma_start(
+            wc_raw[:].rearrange("p (a c) -> p a c", a=2),
+            wc_words.rearrange("a p c i -> p a (c i)").bitcast(I32),
+        )
         quantise_weight(0, "w_q0")
         gather_words(0)
         gather_words(1)
         w_raw[2] = keep.tile([P, PACK, PASS], F32, name="w_raw2", tag="tab_w", align_bytes=64)
         nc.sync.dma_start(w_raw[2][:], wd.rearrange("(p i) c -> p i c", i=PACK))
-        nc.vector.tensor_copy(
-            wc_p[:].rearrange("p (a t g m) -> p a g t m", a=2, t=PACK, m=4),
-            wc_raw[:].rearrange("p (a g m t) -> p a g t m", a=2, t=PACK, m=4),
+        for part in range(2):
+            round_wb(2, part)
+        nc.gpsimd.tensor_scalar(
+            w_bf[1][:].rearrange("p (t m i) -> p m t i", t=PACK, i=PACK)[:, P // 2 :],
+            wb_raw[3][:].rearrange("p i (m t) -> p m t i", t=PACK),
+            1.0,
+            0.0,
+            MULT,
+            ADD,
         )
-        weight = keep.tile([P, S], F32, name="weight", tag="picked_s", align_bytes=64)
+        hidden(0, 0, {})
+        weight = keep.tile([P, S], F32, name="weight", tag="ws_raw", align_bytes=64)
         nc.sync.dma_start(weight[:], wgo)
-        hidden(0, 0, {u: [lambda u=u: round_weight(1, u)] for u in range(PARTS)})
         hidden(
             0,
             1,
-            {0: [lambda: quantise_hidden(0, 0), lambda: quantise_weight(1, "h_bf00"), lambda: round_wd(0, "w_bf1")]},
+            {
+                0: [
+                    lambda: quantise_hidden(0, 0),
+                    lambda: quantise_weight(1, "h_bf00"),
+                    order_wc,
+                    lambda: round_wd(0, "wb_raw1"),
+                ]
+            },
         )
+        wc_p = late["wc"]
         hidden(1, 0, {0: [lambda: quantise_hidden(0, 1), lambda: round_wd(1, "h_bf01")]})
         hidden(1, 1, {0: [lambda: quantise_hidden(1, 0), quantise_wd]})
         quantise_hidden(1, 1)

@@ -33,6 +33,7 @@ def tile_list_beam_cache_rewrite_kernel(
     with ExitStack() as ctx:
         lists = ctx.enter_context(tc.tile_pool(name="lists", bufs=1))
         keep = ctx.enter_context(tc.tile_pool(name="keep", bufs=1))
+        shared = ctx.enter_context(tc.tile_pool(name="shared", bufs=1))
         ring = ctx.enter_context(tc.tile_pool(name="ring", bufs=4))
         psum = ctx.enter_context(tc.psum_pool(name="psum", bufs=3))
         psum_y = ctx.enter_context(tc.psum_pool(name="psum_y", bufs=2))
@@ -40,7 +41,7 @@ def tile_list_beam_cache_rewrite_kernel(
         pick = lists.tile([P, S // 16], U16, name="pick")
         put = lists.tile([P, S // 16], U16, name="put")
         tab_s = keep.tile([P, T], U8, name="tab_s", align_bytes=64)
-        ws_raw = keep.tile([P, H], U8, name="ws_raw", align_bytes=64)
+        ws_raw = shared.tile([P, H], U8, name="ws_raw", offset=8128, align_bytes=64)
         wa_raw = keep.tile([P, 2 * H], U8, name="wa_raw", align_bytes=64)
         w_raw = {}
         wb_raw = {}
@@ -89,9 +90,13 @@ def tile_list_beam_cache_rewrite_kernel(
         nc.vector.tensor_copy(planes[:, 0:S].bitcast(I32), picked_s[:].bitcast(I32))
         for r in range(1, 4):
             nc.sync.dma_start(planes[r:P:32, :].bitcast(I32), planes[8 * r : P : 32, :].bitcast(I32))
-        load_wb(3, "ws_raw")
+        load_wb(3, "picked_s")
         wc_s = keep.tile([P, H], U8, name="wc_s", align_bytes=64)
         nc.gpsimd.memset(wc_s[:].bitcast(I32), 0)
+        for i, offset in ((1, 0), (2, 8128 + 960)):
+            pages[i] = shared.tile([P, T2], F32, name=f"page{i}", offset=offset, align_bytes=64)
+            for q in range(4):
+                nc.gpsimd.memset(pages[i][:, q * HALF : (q + 1) * HALF], 0.0)
         for r in range(4):
             nc.sync.dma_start(wc_s[r:P:32, :].bitcast(I32), planes[WC_ROW + 8 * r : P : 32, S:].bitcast(I32))
         v_s = planes[:, 0:S]
@@ -129,8 +134,8 @@ def tile_list_beam_cache_rewrite_kernel(
 
         h_bf = {}
 
-        def hidden(b, c, beside):
-            h_bf[b, c] = keep.tile([P, PACK * HALF], BF16, name=f"h_bf{b}{c}", align_bytes=64)
+        def hidden(b, c, beside, tag=None):
+            h_bf[b, c] = keep.tile([P, PACK * HALF], BF16, name=f"h_bf{b}{c}", tag=tag or f"h_bf{b}{c}", align_bytes=64)
             for u in range(HALF // JT):
                 js = slice(c * HALF + u * JT, c * HALF + (u + 1) * JT)
                 gate = psum.tile([P, PACK, JT], F32, name="gate")
@@ -156,17 +161,20 @@ def tile_list_beam_cache_rewrite_kernel(
                         start=True,
                         stop=True,
                     )
-                if (b, c, u) == (1, 1, HALF // JT - 1):
-                    act = keep.tile([P, JT, PACK], F32, name="last_act", tag="y00")
+                dst = h_bf[b, c][:, u * JT * PACK : (u + 1) * JT * PACK].rearrange("p (j t) -> p j t", t=PACK)
+                if (b, c) == (1, 1):
+                    act = keep.tile([P, JT, PACK], F32, name=f"late_act{u}", align_bytes=64)
+                    up_sb = keep.tile([P, JT, PACK], F32, name=f"late_up{u}", align_bytes=64)
+                    nc.scalar.activation(act[:], gate[:].rearrange("p t j -> p j t"), ACT.Silu)
+                    nc.scalar.copy(up_sb[:], up[:].rearrange("p t j -> p j t"))
+                    nc.gpsimd.tensor_tensor(dst, up_sb[:], act[:], MULT)
                 else:
-                    act = ring.tile([P, JT, PACK], F32, name="act")
-                nc.scalar.activation(act[:], gate[:].rearrange("p t j -> p j t"), ACT.Silu)
-                nc.vector.tensor_tensor(
-                    h_bf[b, c][:, u * JT * PACK : (u + 1) * JT * PACK].rearrange("p (j t) -> p j t", t=PACK),
-                    up[:].rearrange("p t j -> p j t"),
-                    act[:],
-                    MULT,
-                )
+                    if (b, c, u) == (1, 0, 2):
+                        act = keep.tile([P, JT, PACK], F32, name="held_act", tag="w_q2", align_bytes=64)
+                    else:
+                        act = ring.tile([P, JT, PACK], F32, name="act")
+                    nc.scalar.activation(act[:], gate[:].rearrange("p t j -> p j t"), ACT.Silu)
+                    nc.vector.tensor_tensor(dst, up[:].rearrange("p t j -> p j t"), act[:], MULT)
                 for step in beside.get(u, ()):
                     step()
 
@@ -188,7 +196,7 @@ def tile_list_beam_cache_rewrite_kernel(
             )
 
         def quantise_wd():
-            w_q[2] = keep.tile([P, PASS], U32, name="w_q2", tag="h_bf10", align_bytes=64)
+            w_q[2] = keep.tile([P, PASS], U32, name="w_q2", tag="w_q2", align_bytes=64)
             for half in range(2):
                 cols = slice(half * 2 * P, (half + 1) * 2 * P)
                 nc.vector.quantize_mx(out=w_q[2][:, cols].bitcast(FP8X4), scales=w_s[2][:, cols], in_=wd_bf[half][:])
@@ -226,7 +234,7 @@ def tile_list_beam_cache_rewrite_kernel(
             ADD,
         )
         hidden(0, 0, {})
-        weight = keep.tile([P, S], F32, name="weight", tag="ws_raw", align_bytes=64)
+        weight = keep.tile([P, S], F32, name="weight", tag="picked_s", align_bytes=64)
         nc.sync.dma_start(weight[:], wgo)
         hidden(
             0,
@@ -237,15 +245,18 @@ def tile_list_beam_cache_rewrite_kernel(
                     lambda: quantise_weight(1, "h_bf00"),
                     order_wc,
                     lambda: round_wd(0, "wb_raw1"),
+                    lambda: round_wd(1, "wb_raw0"),
                 ]
             },
         )
         wc_p = late["wc"]
-        hidden(1, 0, {0: [lambda: quantise_hidden(0, 1), lambda: round_wd(1, "h_bf01")]})
-        hidden(1, 1, {0: [lambda: quantise_hidden(1, 0), quantise_wd]})
-        quantise_hidden(1, 1)
+        hidden(1, 0, {})
+        quantise_wd()
+        quantise_hidden(1, 0)
+        quantise_hidden(0, 1)
+        hidden(1, 1, {}, "h_bf10")
 
-        def result(i, c, y):
+        def total(i, c):
             cs = slice(c * HALF, (c + 1) * HALF)
             acc = psum_y.tile([P, HALF], F32, name="acc")
             nc.tensor.matmul_mx(
@@ -268,29 +279,27 @@ def tile_list_beam_cache_rewrite_kernel(
                     start=False,
                     stop=(a == 1),
                 )
-            nc.scalar.activation(y, acc[:], ACT.Identity, bias=bias[:, i : i + 1])
+            return acc
 
-        def clear_page(i, tag):
-            pages[i] = keep.tile([P, T2], F32, name=f"page{i}", tag=tag)
-            nc.gpsimd.memset(pages[i][:], 0.0)
+        def places(i, c):
+            return pages[i][:].indirect(put[:, c * HALF // 16 : (c + 1) * HALF // 16])
 
+        for i in range(2):
+            y = keep.tile([P, HALF], F32, name=f"y{i}0", tag="weighed" if i else "h_bf01", align_bytes=64)
+            nc.vector.scalar_tensor_tensor(y[:], total(i, 0)[:], bias[:, i : i + 1], weight[:, 0:HALF], ADD, MULT)
+            nc.vector.tensor_copy(places(i, 0), y[:])
+        quantise_hidden(1, 1)
+        pages[3] = keep.tile([P, T2], F32, name="page3", tag="h_bf10", align_bytes=64)
+        nc.gpsimd.memset(pages[3][:], 0.0)
+
+        def weigh_and_place(i, c, tag):
+            y = keep.tile([P, HALF], F32, name=f"y{i}{c}", tag=tag, align_bytes=64)
+            nc.scalar.activation(y[:], total(i, c)[:], ACT.Identity, bias=bias[:, i : i + 1])
+            nc.vector.tensor_tensor(places(i, c), y[:], weight[:, c * HALF : (c + 1) * HALF], MULT)
+
+        weigh_and_place(2, 0, "late_act3")
+        weigh_and_place(3, 0, "late_up3")
         out_rows = out.rearrange("(p i) t -> p i t", i=PACK)
-        for c in range(2):
-            y = keep.tile([P, HALF], F32, name=f"y0{c}")
-            result(0, c, y[:])
-            nc.vector.tensor_tensor(
-                pages[0][:].indirect(put[:, c * HALF // 16 : (c + 1) * HALF // 16]),
-                y[:],
-                weight[:, c * HALF : (c + 1) * HALF],
-                MULT,
-            )
-            clear_page(c + 1, f"y0{c}")
-        nc.sync.dma_start(out_rows[:, 0, :], pages[0][:])
-        for i in range(1, PACK):
-            y = keep.tile([P, S], F32, name=f"y{i}")
-            for c in range(2):
-                result(i, c, y[:, c * HALF : (c + 1) * HALF])
-            nc.vector.tensor_tensor(pages[i][:].indirect(put[:]), y[:], weight[:], MULT)
-            if i == 1:
-                clear_page(3, "y1")
+        for i in range(PACK):
+            weigh_and_place(i, 1, f"y{i}1")
             nc.sync.dma_start(out_rows[:, i, :], pages[i][:])

@@ -33,7 +33,6 @@ def tile_list_beam_cache_rewrite_kernel(
     with ExitStack() as ctx:
         lists = ctx.enter_context(tc.tile_pool(name="lists", bufs=1))
         keep = ctx.enter_context(tc.tile_pool(name="keep", bufs=1))
-        shared = ctx.enter_context(tc.tile_pool(name="shared", bufs=1))
         ring = ctx.enter_context(tc.tile_pool(name="ring", bufs=4))
         psum = ctx.enter_context(tc.psum_pool(name="psum", bufs=3))
         psum_y = ctx.enter_context(tc.psum_pool(name="psum_y", bufs=2))
@@ -41,7 +40,7 @@ def tile_list_beam_cache_rewrite_kernel(
         pick = lists.tile([P, S // 16], U16, name="pick")
         put = lists.tile([P, S // 16], U16, name="put")
         tab_s = keep.tile([P, T], U8, name="tab_s", align_bytes=64)
-        ws_raw = shared.tile([P, H], U8, name="ws_raw", offset=8128, align_bytes=64)
+        ws_raw = keep.tile([P, H], U8, name="ws_raw", align_bytes=64)
         wa_raw = keep.tile([P, 2 * H], U8, name="wa_raw", align_bytes=64)
         w_raw = {}
         wb_raw = {}
@@ -75,8 +74,9 @@ def tile_list_beam_cache_rewrite_kernel(
         nc.sync.dma_start(tab_w[:], tab_words[0].rearrange("p t i -> p (t i)").bitcast(I32))
         nc.gpsimd.dma_start(bias[:], bo.rearrange("(p i) -> p i", i=PACK))
 
-        pages = {0: keep.tile([P, T2], F32, name="page0")}
-        nc.vector.memset(pages[0][:], 0.0)
+        pages = {i: keep.tile([P, T2], F32, name=f"page{i}") for i in range(2)}
+        for i in range(2):
+            nc.vector.memset(pages[i][:], 0.0)
 
         picked_s = keep.tile([P, S], U8, name="picked_s", align_bytes=64)
         planes = keep.tile([P, S + H], U8, name="planes", align_bytes=64)
@@ -90,13 +90,9 @@ def tile_list_beam_cache_rewrite_kernel(
         nc.vector.tensor_copy(planes[:, 0:S].bitcast(I32), picked_s[:].bitcast(I32))
         for r in range(1, 4):
             nc.sync.dma_start(planes[r:P:32, :].bitcast(I32), planes[8 * r : P : 32, :].bitcast(I32))
-        load_wb(3, "picked_s")
+        load_wb(3, "ws_raw")
         wc_s = keep.tile([P, H], U8, name="wc_s", align_bytes=64)
         nc.gpsimd.memset(wc_s[:].bitcast(I32), 0)
-        for i, offset in ((1, 0), (2, 8128 + 960)):
-            pages[i] = shared.tile([P, T2], F32, name=f"page{i}", offset=offset, align_bytes=64)
-            for q in range(4):
-                nc.gpsimd.memset(pages[i][:, q * HALF : (q + 1) * HALF], 0.0)
         for r in range(4):
             nc.sync.dma_start(wc_s[r:P:32, :].bitcast(I32), planes[WC_ROW + 8 * r : P : 32, S:].bitcast(I32))
         v_s = planes[:, 0:S]
@@ -162,7 +158,7 @@ def tile_list_beam_cache_rewrite_kernel(
                         stop=True,
                     )
                 dst = h_bf[b, c][:, u * JT * PACK : (u + 1) * JT * PACK].rearrange("p (j t) -> p j t", t=PACK)
-                if (b, c) == (1, 1):
+                if (b, c) == (1, 1) and u != 1:
                     act = keep.tile([P, JT, PACK], F32, name=f"late_act{u}", align_bytes=64)
                     up_sb = keep.tile([P, JT, PACK], F32, name=f"late_up{u}", align_bytes=64)
                     nc.scalar.activation(act[:], gate[:].rearrange("p t j -> p j t"), ACT.Silu)
@@ -171,6 +167,8 @@ def tile_list_beam_cache_rewrite_kernel(
                 else:
                     if (b, c, u) == (1, 0, 2):
                         act = keep.tile([P, JT, PACK], F32, name="held_act", tag="w_q2", align_bytes=64)
+                    elif (b, c) == (1, 1):
+                        act = keep.tile([P, JT, PACK], F32, name="filler_act", tag="weighed", align_bytes=64)
                     else:
                         act = ring.tile([P, JT, PACK], F32, name="act")
                     nc.scalar.activation(act[:], gate[:].rearrange("p t j -> p j t"), ACT.Silu)
@@ -234,7 +232,7 @@ def tile_list_beam_cache_rewrite_kernel(
             ADD,
         )
         hidden(0, 0, {})
-        weight = keep.tile([P, S], F32, name="weight", tag="picked_s", align_bytes=64)
+        weight = keep.tile([P, S], F32, name="weight", tag="ws_raw", align_bytes=64)
         nc.sync.dma_start(weight[:], wgo)
         hidden(
             0,
@@ -245,15 +243,13 @@ def tile_list_beam_cache_rewrite_kernel(
                     lambda: quantise_weight(1, "h_bf00"),
                     order_wc,
                     lambda: round_wd(0, "wb_raw1"),
-                    lambda: round_wd(1, "wb_raw0"),
                 ]
             },
         )
         wc_p = late["wc"]
-        hidden(1, 0, {})
+        hidden(1, 0, {0: [lambda: quantise_hidden(0, 1), lambda: round_wd(1, "h_bf01")]})
         quantise_wd()
         quantise_hidden(1, 0)
-        quantise_hidden(0, 1)
         hidden(1, 1, {}, "h_bf10")
 
         def total(i, c):
@@ -284,21 +280,25 @@ def tile_list_beam_cache_rewrite_kernel(
         def places(i, c):
             return pages[i][:].indirect(put[:, c * HALF // 16 : (c + 1) * HALF // 16])
 
-        for i in range(2):
-            y = keep.tile([P, HALF], F32, name=f"y{i}0", tag="weighed" if i else "h_bf01", align_bytes=64)
-            nc.vector.scalar_tensor_tensor(y[:], total(i, 0)[:], bias[:, i : i + 1], weight[:, 0:HALF], ADD, MULT)
-            nc.vector.tensor_copy(places(i, 0), y[:])
+        weighed = keep.tile([P, HALF], F32, name="weighed", tag="weighed", align_bytes=64)
+        nc.vector.scalar_tensor_tensor(weighed[:], total(0, 0)[:], bias[:, 0:1], weight[:, 0:HALF], ADD, MULT)
+        nc.vector.tensor_copy(places(0, 0), weighed[:])
         quantise_hidden(1, 1)
-        pages[3] = keep.tile([P, T2], F32, name="page3", tag="h_bf10", align_bytes=64)
-        nc.gpsimd.memset(pages[3][:], 0.0)
+
+        def clear_page(i, tag):
+            pages[i] = keep.tile([P, T2], F32, name=f"page{i}", tag=tag, align_bytes=64)
+            nc.gpsimd.memset(pages[i][:], 0.0)
 
         def weigh_and_place(i, c, tag):
             y = keep.tile([P, HALF], F32, name=f"y{i}{c}", tag=tag, align_bytes=64)
             nc.scalar.activation(y[:], total(i, c)[:], ACT.Identity, bias=bias[:, i : i + 1])
             nc.vector.tensor_tensor(places(i, c), y[:], weight[:, c * HALF : (c + 1) * HALF], MULT)
 
-        weigh_and_place(2, 0, "late_act3")
-        weigh_and_place(3, 0, "late_up3")
+        clear_page(2, "h_bf10")
+        weigh_and_place(1, 0, "late_act3")
+        clear_page(3, "late_act3")
+        weigh_and_place(2, 0, "late_up3")
+        weigh_and_place(3, 0, "y30")
         out_rows = out.rearrange("(p i) t -> p i t", i=PACK)
         for i in range(PACK):
             weigh_and_place(i, 1, f"y{i}1")

@@ -23,7 +23,7 @@ PASS = P * PACK
 HALF = 512
 JT = 128
 QUARTER = 256
-WC_ROW = 4
+WC_ROW = 5
 
 
 def tile_list_beam_cache_rewrite_kernel(
@@ -33,6 +33,7 @@ def tile_list_beam_cache_rewrite_kernel(
     with ExitStack() as ctx:
         lists = ctx.enter_context(tc.tile_pool(name="lists", bufs=1))
         keep = ctx.enter_context(tc.tile_pool(name="keep", bufs=1))
+        shared = ctx.enter_context(tc.tile_pool(name="shared", bufs=1))
         ring = ctx.enter_context(tc.tile_pool(name="ring", bufs=4))
         psum = ctx.enter_context(tc.psum_pool(name="psum", bufs=3))
         psum_y = ctx.enter_context(tc.psum_pool(name="psum_y", bufs=2))
@@ -50,39 +51,39 @@ def tile_list_beam_cache_rewrite_kernel(
             nc.sync.dma_start(wb_raw[n][:], wb_rows[:, :, n * QUARTER : (n + 1) * QUARTER])
 
         bias = keep.tile([P, PACK], F32, name="bias")
-        warm = keep.tile([P, 1], F32, name="warm", tag="tab_w", align_bytes=64)
+        warm = keep.tile([P, 1], F32, name="warm", align_bytes=64)
         warm_out = keep.tile([P, 1], F32, name="warm_out")
 
         wb_rows = wb.rearrange("(p i) c -> p i c", i=PACK)
         nc.gpsimd.memset(warm[:], 0.0)
-        nc.vector.memset(ws_raw[:].bitcast(I32), 0)
         nc.sync.dma_start(pick[:], offs)
         nc.sync.dma_start(
             tab_s[:].bitcast(I32), tab_scales[0].bitcast(I32).unsqueeze(1).to_broadcast([16, 8, T // 4])
         )
-        nc.sync.dma_start(put[:], offs2)
-        nc.sync.dma_start(ws_raw[0:P:8, :].bitcast(I32), wa_scales[0].bitcast(I32))
         nc.sync.dma_start(
-            ws_raw[WC_ROW:P:8, :].bitcast(I32).rearrange("q (a c) -> q a c", a=2),
-            wc_scales.bitcast(I32).rearrange("a q c -> q a c"),
+            ws_raw[0:P:2, :].bitcast(I32), wa_scales[0].bitcast(I32).unsqueeze(1).to_broadcast([16, 4, H // 4])
         )
+        for a in range(2):
+            nc.sync.dma_start(
+                ws_raw[1:P:2, a * N : (a + 1) * N].bitcast(I32),
+                wc_scales[a].bitcast(I32).unsqueeze(1).to_broadcast([16, 4, N // 4]),
+            )
         nc.scalar.activation(warm_out[:], warm[:], ACT.Silu)
         nc.sync.dma_start(wa_raw[:].bitcast(I32), wa_words[0].bitcast(I32))
         load_wb(0, "wb_raw0")
         load_wb(1, "wb_raw1")
         tab_w = keep.tile([P, T], I32, name="tab_w", align_bytes=64)
         nc.sync.dma_start(tab_w[:], tab_words[0].rearrange("p t i -> p (t i)").bitcast(I32))
+        nc.sync.dma_start(put[:], offs2)
         nc.gpsimd.dma_start(bias[:], bo.rearrange("(p i) -> p i", i=PACK))
 
-        pages = {i: keep.tile([P, T2], F32, name=f"page{i}") for i in range(2)}
-        for i in range(2):
-            nc.vector.memset(pages[i][:], 0.0)
+        pages = {0: keep.tile([P, T2], F32, name="page0")}
+        nc.vector.memset(pages[0][:], 0.0)
 
-        picked_s = keep.tile([P, S], U8, name="picked_s", align_bytes=64)
+        picked_s = shared.tile([P, S], U8, name="picked_s", offset=4032, align_bytes=64)
         planes = keep.tile([P, S + H], U8, name="planes", align_bytes=64)
         v_w = keep.tile([P, S], U32, name="v_w", align_bytes=64)
         nc.vector.tensor_copy(picked_s[:], tab_s[:].indirect(pick[:]))
-        load_wb(2, "tab_s")
         nc.vector.tensor_copy(
             planes[:, S:].rearrange("p (b t g m) -> p b g t m", b=2, t=PACK, m=16),
             ws_raw[:].rearrange("p (b g m t) -> p b g t m", b=2, t=PACK, m=16),
@@ -90,11 +91,9 @@ def tile_list_beam_cache_rewrite_kernel(
         nc.vector.tensor_copy(planes[:, 0:S].bitcast(I32), picked_s[:].bitcast(I32))
         for r in range(1, 4):
             nc.sync.dma_start(planes[r:P:32, :].bitcast(I32), planes[8 * r : P : 32, :].bitcast(I32))
-        load_wb(3, "ws_raw")
-        wc_s = keep.tile([P, H], U8, name="wc_s", align_bytes=64)
-        nc.gpsimd.memset(wc_s[:].bitcast(I32), 0)
-        for r in range(4):
-            nc.sync.dma_start(wc_s[r:P:32, :].bitcast(I32), planes[WC_ROW + 8 * r : P : 32, S:].bitcast(I32))
+        for n, offset in ((2, 0), (3, 4992)):
+            wb_raw[n] = shared.tile([P, PACK, QUARTER], F32, name=f"wb_raw{n}", offset=offset, align_bytes=64)
+            nc.sync.dma_start(wb_raw[n][:], wb_rows[:, :, n * QUARTER : (n + 1) * QUARTER])
         v_s = planes[:, 0:S]
         wa_s = planes[:, S:]
 
@@ -217,22 +216,38 @@ def tile_list_beam_cache_rewrite_kernel(
             wc_words.rearrange("a p c i -> p a (c i)").bitcast(I32),
         )
         quantise_weight(0, "w_q0")
+        spare = psum_y.tile([P, HALF], F32, name="acc")
+        for k in range(3):
+            nc.tensor.matmul_mx(
+                out=spare[:],
+                lhsT=w_q[0][:, 0:P].bitcast(FP8X4),
+                lhsT_scale=w_s[0][:, 0:P],
+                rhs=w_q[0][:].bitcast(FP8X4),
+                rhs_scale=w_s[0][:],
+                start=True,
+                stop=True,
+            )
+        pages[1] = keep.tile([P, T2], F32, name="page1", tag="w_bf0", align_bytes=64)
+        nc.gpsimd.memset(pages[1][:], 0.0)
+        wc_s = keep.tile([P, H], U8, name="wc_s", tag="wb_raw0", align_bytes=64)
+        nc.gpsimd.memset(wc_s[:].bitcast(I32), 0)
+        for r in range(4):
+            nc.sync.dma_start(wc_s[r:P:32, :].bitcast(I32), planes[WC_ROW + 8 * r : P : 32, S:].bitcast(I32))
         gather_words(0)
         gather_words(1)
         w_raw[2] = keep.tile([P, PACK, PASS], F32, name="w_raw2", tag="tab_w", align_bytes=64)
         nc.sync.dma_start(w_raw[2][:], wd.rearrange("(p i) c -> p i c", i=PACK))
-        for part in range(2):
-            round_wb(2, part)
-        nc.gpsimd.tensor_scalar(
-            w_bf[1][:].rearrange("p (t m i) -> p m t i", t=PACK, i=PACK)[:, P // 2 :],
-            wb_raw[3][:].rearrange("p i (m t) -> p m t i", t=PACK),
-            1.0,
-            0.0,
-            MULT,
-            ADD,
-        )
+        for n in (2, 3):
+            nc.gpsimd.tensor_scalar(
+                w_bf[1][:].rearrange("p (t m i) -> p m t i", t=PACK, i=PACK)[:, (n - 2) * 64 : (n - 1) * 64],
+                wb_raw[n][:].rearrange("p i (m t) -> p m t i", t=PACK),
+                1.0,
+                0.0,
+                MULT,
+                ADD,
+            )
         hidden(0, 0, {})
-        weight = keep.tile([P, S], F32, name="weight", tag="ws_raw", align_bytes=64)
+        weight = shared.tile([P, S], F32, name="weight", offset=4992, align_bytes=64)
         nc.sync.dma_start(weight[:], wgo)
         hidden(
             0,

@@ -72,7 +72,7 @@ def tile_list_beam_cache_rewrite_kernel(
         nc.sync.dma_start(wa_raw[:].bitcast(I32), wa_words[0].bitcast(I32))
         load_wb(0, "wb_raw0")
         load_wb(1, "wb_raw1")
-        tab_w = keep.tile([P, T], I32, name="tab_w", align_bytes=64)
+        tab_w = shared.tile([P, T], I32, name="tab_w", offset=9216 + 8128, align_bytes=64)
         nc.sync.dma_start(tab_w[:], tab_words[0].rearrange("p t i -> p (t i)").bitcast(I32))
         nc.sync.dma_start(put[:], offs2)
         nc.gpsimd.dma_start(bias[:], bo.rearrange("(p i) -> p i", i=PACK))
@@ -102,7 +102,7 @@ def tile_list_beam_cache_rewrite_kernel(
             wa_p[:].bitcast(U16).rearrange("p (b t g m) -> p b g t m", b=2, t=PACK, m=8),
             wa_raw[:].bitcast(U16).rearrange("p (b g m t) -> p b g t m", b=2, t=PACK, m=8),
         )
-        w_bf = [keep.tile([P, PACK * PASS], BF16, name=f"w_bf{n}", align_bytes=64) for n in range(2)]
+        w_bf = {0: keep.tile([P, PACK * PASS], BF16, name="w_bf0", align_bytes=64)}
         w_q = {}
         w_s = [keep.tile([P, PASS], U8, name=f"w_s{n}", align_bytes=64) for n in range(3)]
 
@@ -157,17 +157,19 @@ def tile_list_beam_cache_rewrite_kernel(
                         stop=True,
                     )
                 dst = h_bf[b, c][:, u * JT * PACK : (u + 1) * JT * PACK].rearrange("p (j t) -> p j t", t=PACK)
-                if (b, c) == (1, 1) and u != 1:
-                    act = keep.tile([P, JT, PACK], F32, name=f"late_act{u}", align_bytes=64)
-                    up_sb = keep.tile([P, JT, PACK], F32, name=f"late_up{u}", align_bytes=64)
+                if b == 1 and u == 0:
+                    act = keep.tile([P, JT, PACK], F32, name=f"late_act{c}", align_bytes=64)
+                    up_sb = keep.tile([P, JT, PACK], F32, name=f"late_up{c}", align_bytes=64)
                     nc.scalar.activation(act[:], gate[:].rearrange("p t j -> p j t"), ACT.Silu)
                     nc.scalar.copy(up_sb[:], up[:].rearrange("p t j -> p j t"))
                     nc.gpsimd.tensor_tensor(dst, up_sb[:], act[:], MULT)
                 else:
                     if (b, c, u) == (1, 0, 2):
                         act = keep.tile([P, JT, PACK], F32, name="held_act", tag="w_q2", align_bytes=64)
-                    elif (b, c) == (1, 1):
-                        act = keep.tile([P, JT, PACK], F32, name="filler_act", tag="weighed", align_bytes=64)
+                    elif (b, c, u) == (0, 1, 2):
+                        act = keep.tile([P, JT, PACK], F32, name="held_act", tag="wc_p", align_bytes=64)
+                    elif (b, c, u) == (1, 1, 3):
+                        act = keep.tile([P, JT, PACK], F32, name="last_act", tag="y00", align_bytes=64)
                     else:
                         act = ring.tile([P, JT, PACK], F32, name="act")
                     nc.scalar.activation(act[:], gate[:].rearrange("p t j -> p j t"), ACT.Silu)
@@ -182,15 +184,16 @@ def tile_list_beam_cache_rewrite_kernel(
         wd_bf = {}
 
         def round_wd(half, tag):
-            wd_bf[half] = keep.tile([P, 2 * PASS], BF16, name=f"wd_bf{half}", tag=tag, align_bytes=64)
-            nc.gpsimd.tensor_scalar(
-                wd_bf[half][:].rearrange("p (t m i) -> p m t i", t=2, i=PACK),
-                w_raw[2][:].rearrange("p i (m t) -> p m t i", t=PACK)[:, :, 2 * half : 2 * half + 2],
-                1.0,
-                0.0,
-                MULT,
-                ADD,
-            )
+            if half == 0:
+                wd_bf[half] = shared.tile([P, 2 * PASS], BF16, name="wd_bf0", offset=9216 + 8128 + 8192, align_bytes=64)
+            else:
+                wd_bf[half] = keep.tile([P, 2 * PASS], BF16, name="wd_bf1", align_bytes=64)
+            dst = wd_bf[half][:].rearrange("p (t m i) -> p m t i", t=2, i=PACK)
+            src = w_raw[2][:].rearrange("p i (m t) -> p m t i", t=PACK)[:, :, 2 * half : 2 * half + 2]
+            if half == 0:
+                nc.gpsimd.tensor_scalar(dst, src, 1.0, 0.0, MULT, ADD)
+            else:
+                nc.scalar.copy(dst, src)
 
         def quantise_wd():
             w_q[2] = keep.tile([P, PASS], U32, name="w_q2", tag="w_q2", align_bytes=64)
@@ -201,7 +204,7 @@ def tile_list_beam_cache_rewrite_kernel(
         late = {}
 
         def order_wc():
-            late["wc"] = keep.tile([P, 2 * N], I32, name="wc_p", tag="w_bf1", align_bytes=64)
+            late["wc"] = keep.tile([P, 2 * N], I32, name="wc_p", tag="wc_p", align_bytes=64)
             nc.vector.tensor_copy(
                 late["wc"][:].rearrange("p (a t g m) -> p a g t m", a=2, t=PACK, m=4),
                 wc_raw[:].rearrange("p (a g m t) -> p a g t m", a=2, t=PACK, m=4),
@@ -227,16 +230,15 @@ def tile_list_beam_cache_rewrite_kernel(
                 start=True,
                 stop=True,
             )
-        pages[1] = keep.tile([P, T2], F32, name="page1", tag="w_bf0", align_bytes=64)
-        nc.gpsimd.memset(pages[1][:], 0.0)
         wc_s = keep.tile([P, H], U8, name="wc_s", tag="wb_raw0", align_bytes=64)
         nc.gpsimd.memset(wc_s[:].bitcast(I32), 0)
         for r in range(4):
             nc.sync.dma_start(wc_s[r:P:32, :].bitcast(I32), planes[WC_ROW + 8 * r : P : 32, S:].bitcast(I32))
         gather_words(0)
         gather_words(1)
-        w_raw[2] = keep.tile([P, PACK, PASS], F32, name="w_raw2", tag="tab_w", align_bytes=64)
+        w_raw[2] = shared.tile([P, PACK, PASS], F32, name="w_raw2", offset=9216, align_bytes=64)
         nc.sync.dma_start(w_raw[2][:], wd.rearrange("(p i) c -> p i c", i=PACK))
+        w_bf[1] = shared.tile([P, PACK * PASS], BF16, name="w_bf1", offset=9216 + 8128 + 8128, align_bytes=64)
         for n in (2, 3):
             nc.gpsimd.tensor_scalar(
                 w_bf[1][:].rearrange("p (t m i) -> p m t i", t=PACK, i=PACK)[:, (n - 2) * 64 : (n - 1) * 64],
@@ -256,16 +258,18 @@ def tile_list_beam_cache_rewrite_kernel(
                 0: [
                     lambda: quantise_hidden(0, 0),
                     lambda: quantise_weight(1, "h_bf00"),
-                    order_wc,
-                    lambda: round_wd(0, "wb_raw1"),
+                    lambda: round_wd(0, "w_bf1"),
                 ]
             },
         )
+        order_wc()
         wc_p = late["wc"]
-        hidden(1, 0, {0: [lambda: quantise_hidden(0, 1), lambda: round_wd(1, "h_bf01")]})
+        quantise_hidden(0, 1)
+        hidden(1, 0, {1: [lambda: round_wd(1, "wd_bf1")]}, "h_bf01")
         quantise_wd()
         quantise_hidden(1, 0)
-        hidden(1, 1, {}, "h_bf10")
+        hidden(1, 1, {}, "h_bf01")
+        quantise_hidden(1, 1)
 
         def total(i, c):
             cs = slice(c * HALF, (c + 1) * HALF)
@@ -292,29 +296,30 @@ def tile_list_beam_cache_rewrite_kernel(
                 )
             return acc
 
-        def places(i, c):
-            return pages[i][:].indirect(put[:, c * HALF // 16 : (c + 1) * HALF // 16])
-
-        weighed = keep.tile([P, HALF], F32, name="weighed", tag="weighed", align_bytes=64)
-        nc.vector.scalar_tensor_tensor(weighed[:], total(0, 0)[:], bias[:, 0:1], weight[:, 0:HALF], ADD, MULT)
-        nc.vector.tensor_copy(places(0, 0), weighed[:])
-        quantise_hidden(1, 1)
+        def result(i, c, y):
+            nc.scalar.activation(y, total(i, c)[:], ACT.Identity, bias=bias[:, i : i + 1])
 
         def clear_page(i, tag):
             pages[i] = keep.tile([P, T2], F32, name=f"page{i}", tag=tag, align_bytes=64)
             nc.gpsimd.memset(pages[i][:], 0.0)
 
-        def weigh_and_place(i, c, tag):
-            y = keep.tile([P, HALF], F32, name=f"y{i}{c}", tag=tag, align_bytes=64)
-            nc.scalar.activation(y[:], total(i, c)[:], ACT.Identity, bias=bias[:, i : i + 1])
-            nc.vector.tensor_tensor(places(i, c), y[:], weight[:, c * HALF : (c + 1) * HALF], MULT)
-
-        clear_page(2, "h_bf10")
-        weigh_and_place(1, 0, "late_act3")
-        clear_page(3, "late_act3")
-        weigh_and_place(2, 0, "late_up3")
-        weigh_and_place(3, 0, "y30")
         out_rows = out.rearrange("(p i) t -> p i t", i=PACK)
-        for i in range(PACK):
-            weigh_and_place(i, 1, f"y{i}1")
+        for c in range(2):
+            y = keep.tile([P, HALF], F32, name=f"y0{c}", align_bytes=64)
+            result(0, c, y[:])
+            nc.vector.tensor_tensor(
+                pages[0][:].indirect(put[:, c * HALF // 16 : (c + 1) * HALF // 16]),
+                y[:],
+                weight[:, c * HALF : (c + 1) * HALF],
+                MULT,
+            )
+            clear_page(c + 1, "h_bf01" if c == 0 else "y00")
+        nc.sync.dma_start(out_rows[:, 0, :], pages[0][:])
+        for i in range(1, PACK):
+            y = keep.tile([P, S], F32, name=f"y{i}", align_bytes=64)
+            for c in range(2):
+                result(i, c, y[:, c * HALF : (c + 1) * HALF])
+            nc.vector.tensor_tensor(pages[i][:].indirect(put[:]), y[:], weight[:], MULT)
+            if i == 1:
+                clear_page(3, "y01")
             nc.sync.dma_start(out_rows[:, i, :], pages[i][:])

@@ -24,6 +24,9 @@ HALF = 512
 JT = 128
 QUARTER = 256
 WC_ROW = 5
+AHEAD = 2
+ON_GPSIMD = ((0, 1, 3), (1, 1, 3))
+ORDER = [(0, 0, u) for u in range(4)] + [(1, 0, u) for u in range(4)] + [(0, 1, u) for u in (3, 0, 1, 2)]
 
 
 def tile_list_beam_cache_rewrite_kernel(
@@ -34,8 +37,8 @@ def tile_list_beam_cache_rewrite_kernel(
         lists = ctx.enter_context(tc.tile_pool(name="lists", bufs=1))
         keep = ctx.enter_context(tc.tile_pool(name="keep", bufs=1))
         shared = ctx.enter_context(tc.tile_pool(name="shared", bufs=1))
-        ring = ctx.enter_context(tc.tile_pool(name="ring", bufs=4))
-        psum = ctx.enter_context(tc.psum_pool(name="psum", bufs=3))
+        psum_g = ctx.enter_context(tc.psum_pool(name="psum_g", bufs=2))
+        psum_u = ctx.enter_context(tc.psum_pool(name="psum_u", bufs=4))
         psum_y = ctx.enter_context(tc.psum_pool(name="psum_y", bufs=2))
 
         pick = lists.tile([P, S // 16], U16, name="pick")
@@ -43,18 +46,14 @@ def tile_list_beam_cache_rewrite_kernel(
         tab_s = keep.tile([P, T], U8, name="tab_s", align_bytes=64)
         ws_raw = keep.tile([P, H], U8, name="ws_raw", align_bytes=64)
         wa_raw = keep.tile([P, 2 * H], U8, name="wa_raw", align_bytes=64)
-        w_raw = {}
-        wb_raw = {}
-
-        def load_wb(n, tag):
-            wb_raw[n] = keep.tile([P, PACK, QUARTER], F32, name=f"wb_raw{n}", tag=tag, align_bytes=64)
-            nc.sync.dma_start(wb_raw[n][:], wb_rows[:, :, n * QUARTER : (n + 1) * QUARTER])
-
+        tab_w = keep.tile([P, T], I32, name="tab_w", align_bytes=64)
         bias = keep.tile([P, PACK], F32, name="bias")
         warm = keep.tile([P, 1], F32, name="warm", align_bytes=64)
         warm_out = keep.tile([P, 1], F32, name="warm_out")
-
+        wc_s = keep.tile([P, H], U8, name="wc_s", align_bytes=64)
+        wb_raw = {}
         wb_rows = wb.rearrange("(p i) c -> p i c", i=PACK)
+
         nc.gpsimd.memset(warm[:], 0.0)
         nc.sync.dma_start(pick[:], offs)
         nc.sync.dma_start(
@@ -70,30 +69,43 @@ def tile_list_beam_cache_rewrite_kernel(
             )
         nc.scalar.activation(warm_out[:], warm[:], ACT.Silu)
         nc.sync.dma_start(wa_raw[:].bitcast(I32), wa_words[0].bitcast(I32))
-        load_wb(0, "wb_raw0")
-        load_wb(1, "wb_raw1")
-        tab_w = shared.tile([P, T], I32, name="tab_w", offset=9216 + 8128, align_bytes=64)
+        for n in range(2):
+            wb_raw[n] = keep.tile([P, PACK, QUARTER], F32, name=f"wb_raw{n}", align_bytes=64)
+            nc.sync.dma_start(wb_raw[n][:], wb_rows[:, :, n * QUARTER : (n + 1) * QUARTER])
         nc.sync.dma_start(tab_w[:], tab_words[0].rearrange("p t i -> p (t i)").bitcast(I32))
         nc.sync.dma_start(put[:], offs2)
+
+        pages = {0: keep.tile([P, T2], F32, name="page0", align_bytes=64)}
+        nc.vector.memset(pages[0][:, 0 : T2 // 2], 0.0)
+        nc.gpsimd.memset(pages[0][:, T2 // 2 :], 0.0)
+        nc.gpsimd.memset(wc_s[:].bitcast(I32), 0)
         nc.gpsimd.dma_start(bias[:], bo.rearrange("(p i) -> p i", i=PACK))
 
-        pages = {0: keep.tile([P, T2], F32, name="page0")}
-        nc.vector.memset(pages[0][:], 0.0)
-
-        picked_s = shared.tile([P, S], U8, name="picked_s", offset=4032, align_bytes=64)
+        picked_s = shared.tile([P, 24576], U8, name="picked_s", offset=0, align_bytes=64)
         planes = keep.tile([P, S + H], U8, name="planes", align_bytes=64)
         v_w = keep.tile([P, S], U32, name="v_w", align_bytes=64)
-        nc.vector.tensor_copy(picked_s[:], tab_s[:].indirect(pick[:]))
+        nc.vector.tensor_copy(picked_s[:, 0:S], tab_s[:].indirect(pick[:]))
         nc.vector.tensor_copy(
             planes[:, S:].rearrange("p (b t g m) -> p b g t m", b=2, t=PACK, m=16),
             ws_raw[:].rearrange("p (b g m t) -> p b g t m", b=2, t=PACK, m=16),
         )
-        nc.vector.tensor_copy(planes[:, 0:S].bitcast(I32), picked_s[:].bitcast(I32))
+        nc.vector.tensor_copy(planes[:, 0:S].bitcast(I32), picked_s[:, 0:S].bitcast(I32))
         for r in range(1, 4):
             nc.sync.dma_start(planes[r:P:32, :].bitcast(I32), planes[8 * r : P : 32, :].bitcast(I32))
-        for n, offset in ((2, 0), (3, 4992)):
+        for n, offset in ((2, 0), (3, 20480)):
             wb_raw[n] = shared.tile([P, PACK, QUARTER], F32, name=f"wb_raw{n}", offset=offset, align_bytes=64)
             nc.sync.dma_start(wb_raw[n][:], wb_rows[:, :, n * QUARTER : (n + 1) * QUARTER])
+        wc_raw = shared.tile([P, 2 * N], I32, name="wc_raw", offset=4096, align_bytes=64)
+        nc.sync.dma_start(
+            wc_raw[:].rearrange("p (a c) -> p a c", a=2),
+            wc_words.rearrange("a p c i -> p a (c i)").bitcast(I32),
+        )
+        wd_raw = shared.tile([P, PACK, PASS], F32, name="wd_raw", offset=8192, align_bytes=64)
+        nc.sync.dma_start(wd_raw[:], wd.rearrange("(p i) c -> p i c", i=PACK))
+        weight = shared.tile([P, S], F32, name="weight", offset=16384, align_bytes=64)
+        nc.sync.dma_start(weight[:], wgo)
+        for r in range(4):
+            nc.sync.dma_start(wc_s[r:P:32, :].bitcast(I32), planes[WC_ROW + 8 * r : P : 32, S:].bitcast(I32))
         v_s = planes[:, 0:S]
         wa_s = planes[:, S:]
 
@@ -102,123 +114,17 @@ def tile_list_beam_cache_rewrite_kernel(
             wa_p[:].bitcast(U16).rearrange("p (b t g m) -> p b g t m", b=2, t=PACK, m=8),
             wa_raw[:].bitcast(U16).rearrange("p (b g m t) -> p b g t m", b=2, t=PACK, m=8),
         )
-        w_bf = {0: keep.tile([P, PACK * PASS], BF16, name="w_bf0", align_bytes=64)}
-        w_q = {}
+        w_q = [keep.tile([P, PASS], U32, name=f"w_q{n}", align_bytes=64) for n in range(2)]
         w_s = [keep.tile([P, PASS], U8, name=f"w_s{n}", align_bytes=64) for n in range(3)]
-
-        def round_wb(n, part):
-            ms = slice(part * 32, (part + 1) * 32)
-            first = (n % 2) * 64 + part * 32
-            nc.scalar.copy(
-                w_bf[n // 2][:].rearrange("p (t m i) -> p m t i", t=PACK, i=PACK)[:, first : first + 32],
-                wb_raw[n][:].rearrange("p i (m t) -> p m t i", t=PACK)[:, ms],
-            )
-
-        def quantise_weight(n, tag):
-            w_q[n] = keep.tile([P, PASS], U32, name=f"w_q{n}", tag=tag, align_bytes=64)
-            nc.vector.quantize_mx(out=w_q[n][:].bitcast(FP8X4), scales=w_s[n][:], in_=w_bf[n][:])
-
-        def gather_words(c):
-            nc.vector.tensor_copy(
-                v_w[:, c * HALF : (c + 1) * HALF],
-                tab_w[:].bitcast(U32).indirect(pick[:, c * HALF // 16 : (c + 1) * HALF // 16]),
-            )
-
-        h_q = [keep.tile([P, S], U32, name=f"h_q{b}", align_bytes=64) for b in range(2)]
-        h_s = [keep.tile([P, S], U8, name=f"h_s{b}", align_bytes=64) for b in range(2)]
-
-        h_bf = {}
-
-        def hidden(b, c, beside, tag=None):
-            h_bf[b, c] = keep.tile([P, PACK * HALF], BF16, name=f"h_bf{b}{c}", tag=tag or f"h_bf{b}{c}", align_bytes=64)
-            for u in range(HALF // JT):
-                js = slice(c * HALF + u * JT, c * HALF + (u + 1) * JT)
-                gate = psum.tile([P, PACK, JT], F32, name="gate")
-                up = psum.tile([P, PACK, JT], F32, name="up")
-                for t in range(PACK):
-                    col = b * PASS + t * P
-                    nc.tensor.matmul_mx(
-                        out=gate[:, t, :],
-                        lhsT=wa_p[:, 2 * col : 2 * (col + P)].bitcast(FP4X4),
-                        lhsT_scale=wa_s[:, col : col + P],
-                        rhs=v_w[:, js].bitcast(FP8X4),
-                        rhs_scale=v_s[:, js],
-                        start=True,
-                        stop=True,
-                    )
-                for t in range(PACK):
-                    nc.tensor.matmul_mx(
-                        out=up[:, t, :],
-                        lhsT=w_q[b][:, t * P : (t + 1) * P].bitcast(FP8X4),
-                        lhsT_scale=w_s[b][:, t * P : (t + 1) * P],
-                        rhs=v_w[:, js].bitcast(FP8X4),
-                        rhs_scale=v_s[:, js],
-                        start=True,
-                        stop=True,
-                    )
-                dst = h_bf[b, c][:, u * JT * PACK : (u + 1) * JT * PACK].rearrange("p (j t) -> p j t", t=PACK)
-                if b == 1 and u == 0:
-                    act = keep.tile([P, JT, PACK], F32, name=f"late_act{c}", align_bytes=64)
-                    up_sb = keep.tile([P, JT, PACK], F32, name=f"late_up{c}", align_bytes=64)
-                    nc.scalar.activation(act[:], gate[:].rearrange("p t j -> p j t"), ACT.Silu)
-                    nc.scalar.copy(up_sb[:], up[:].rearrange("p t j -> p j t"))
-                    nc.gpsimd.tensor_tensor(dst, up_sb[:], act[:], MULT)
-                else:
-                    if (b, c, u) == (1, 0, 2):
-                        act = keep.tile([P, JT, PACK], F32, name="held_act", tag="w_q2", align_bytes=64)
-                    elif (b, c, u) == (0, 1, 2):
-                        act = keep.tile([P, JT, PACK], F32, name="held_act", tag="wc_p", align_bytes=64)
-                    elif (b, c, u) == (1, 1, 3):
-                        act = keep.tile([P, JT, PACK], F32, name="last_act", tag="y00", align_bytes=64)
-                    else:
-                        act = ring.tile([P, JT, PACK], F32, name="act")
-                    nc.scalar.activation(act[:], gate[:].rearrange("p t j -> p j t"), ACT.Silu)
-                    nc.vector.tensor_tensor(dst, up[:].rearrange("p t j -> p j t"), act[:], MULT)
-                for step in beside.get(u, ()):
-                    step()
-
-        def quantise_hidden(b, c):
-            cs = slice(c * HALF, (c + 1) * HALF)
-            nc.vector.quantize_mx(out=h_q[b][:, cs].bitcast(FP8X4), scales=h_s[b][:, cs], in_=h_bf[b, c][:])
-
-        wd_bf = {}
-
-        def round_wd(half, tag):
-            if half == 0:
-                wd_bf[half] = shared.tile([P, 2 * PASS], BF16, name="wd_bf0", offset=9216 + 8128 + 8192, align_bytes=64)
-            else:
-                wd_bf[half] = keep.tile([P, 2 * PASS], BF16, name="wd_bf1", align_bytes=64)
-            dst = wd_bf[half][:].rearrange("p (t m i) -> p m t i", t=2, i=PACK)
-            src = w_raw[2][:].rearrange("p i (m t) -> p m t i", t=PACK)[:, :, 2 * half : 2 * half + 2]
-            if half == 0:
-                nc.gpsimd.tensor_scalar(dst, src, 1.0, 0.0, MULT, ADD)
-            else:
-                nc.scalar.copy(dst, src)
-
-        def quantise_wd():
-            w_q[2] = keep.tile([P, PASS], U32, name="w_q2", tag="w_q2", align_bytes=64)
-            for half in range(2):
-                cols = slice(half * 2 * P, (half + 1) * 2 * P)
-                nc.vector.quantize_mx(out=w_q[2][:, cols].bitcast(FP8X4), scales=w_s[2][:, cols], in_=wd_bf[half][:])
-
-        late = {}
-
-        def order_wc():
-            late["wc"] = keep.tile([P, 2 * N], I32, name="wc_p", tag="wc_p", align_bytes=64)
-            nc.vector.tensor_copy(
-                late["wc"][:].rearrange("p (a t g m) -> p a g t m", a=2, t=PACK, m=4),
-                wc_raw[:].rearrange("p (a g m t) -> p a g t m", a=2, t=PACK, m=4),
-            )
-
+        first_bf = keep.tile([P, PACK * PASS], BF16, name="first_bf", align_bytes=64)
         for n in range(2):
             for part in range(2):
-                round_wb(n, part)
-        wc_raw = keep.tile([P, 2 * N], I32, name="wc_raw", tag="wb_raw1", align_bytes=64)
-        nc.sync.dma_start(
-            wc_raw[:].rearrange("p (a c) -> p a c", a=2),
-            wc_words.rearrange("a p c i -> p a (c i)").bitcast(I32),
-        )
-        quantise_weight(0, "w_q0")
+                first = n * 64 + part * 32
+                nc.scalar.copy(
+                    first_bf[:].rearrange("p (t m i) -> p m t i", t=PACK, i=PACK)[:, first : first + 32],
+                    wb_raw[n][:].rearrange("p i (m t) -> p m t i", t=PACK)[:, part * 32 : (part + 1) * 32],
+                )
+        nc.vector.quantize_mx(out=w_q[0][:].bitcast(FP8X4), scales=w_s[0][:], in_=first_bf[:])
         spare = psum_y.tile([P, HALF], F32, name="acc")
         for k in range(3):
             nc.tensor.matmul_mx(
@@ -230,96 +136,178 @@ def tile_list_beam_cache_rewrite_kernel(
                 start=True,
                 stop=True,
             )
-        wc_s = keep.tile([P, H], U8, name="wc_s", tag="wb_raw0", align_bytes=64)
-        nc.gpsimd.memset(wc_s[:].bitcast(I32), 0)
-        for r in range(4):
-            nc.sync.dma_start(wc_s[r:P:32, :].bitcast(I32), planes[WC_ROW + 8 * r : P : 32, S:].bitcast(I32))
-        gather_words(0)
-        gather_words(1)
-        w_raw[2] = shared.tile([P, PACK, PASS], F32, name="w_raw2", offset=9216, align_bytes=64)
-        nc.sync.dma_start(w_raw[2][:], wd.rearrange("(p i) c -> p i c", i=PACK))
-        w_bf[1] = shared.tile([P, PACK * PASS], BF16, name="w_bf1", offset=9216 + 8128 + 8128, align_bytes=64)
+        for c in range(2):
+            nc.vector.tensor_copy(
+                v_w[:, c * HALF : (c + 1) * HALF],
+                tab_w[:].bitcast(U32).indirect(pick[:, c * HALF // 16 : (c + 1) * HALF // 16]),
+            )
+
+        second_bf = keep.tile([P, PACK * PASS], BF16, name="second_bf", tag="tab_w", align_bytes=64)
         for n in (2, 3):
             nc.gpsimd.tensor_scalar(
-                w_bf[1][:].rearrange("p (t m i) -> p m t i", t=PACK, i=PACK)[:, (n - 2) * 64 : (n - 1) * 64],
+                second_bf[:].rearrange("p (t m i) -> p m t i", t=PACK, i=PACK)[:, (n - 2) * 64 : (n - 1) * 64],
                 wb_raw[n][:].rearrange("p i (m t) -> p m t i", t=PACK),
                 1.0,
                 0.0,
                 MULT,
                 ADD,
             )
-        hidden(0, 0, {})
-        weight = shared.tile([P, S], F32, name="weight", offset=4992, align_bytes=64)
-        nc.sync.dma_start(weight[:], wgo)
-        hidden(
-            0,
-            1,
-            {
-                0: [
-                    lambda: quantise_hidden(0, 0),
-                    lambda: quantise_weight(1, "h_bf00"),
-                    lambda: round_wd(0, "w_bf1"),
-                ]
-            },
-        )
-        order_wc()
-        wc_p = late["wc"]
-        quantise_hidden(0, 1)
-        hidden(1, 0, {1: [lambda: round_wd(1, "wd_bf1")]}, "h_bf01")
-        quantise_wd()
-        quantise_hidden(1, 0)
-        hidden(1, 1, {}, "h_bf01")
-        quantise_hidden(1, 1)
 
-        def total(i, c):
+        h_q = {}
+        h_s = [keep.tile([P, S], U8, name=f"h_s{b}", align_bytes=64) for b in range(2)]
+        h_bf = {}
+        act = {}
+
+        def gate(b, c, u):
+            js = slice(c * HALF + u * JT, c * HALF + (u + 1) * JT)
+            if (b, c) == (1, 1):
+                bank = psum_y.tile([P, PACK, JT], F32, name="late_gate", tag="acc")
+            else:
+                bank = psum_g.tile([P, PACK, JT], F32, name="gate")
+            for t in range(PACK):
+                col = b * PASS + t * P
+                nc.tensor.matmul_mx(
+                    out=bank[:, t, :],
+                    lhsT=wa_p[:, 2 * col : 2 * (col + P)].bitcast(FP4X4),
+                    lhsT_scale=wa_s[:, col : col + P],
+                    rhs=v_w[:, js].bitcast(FP8X4),
+                    rhs_scale=v_s[:, js],
+                    start=True,
+                    stop=True,
+                )
+            act[b, c, u] = keep.tile([P, JT, PACK], F32, name=f"act{b}{c}{u}", align_bytes=64)
+            nc.scalar.activation(act[b, c, u][:], bank[:].rearrange("p t j -> p j t"), ACT.Silu)
+
+        def product(b, c, u):
+            js = slice(c * HALF + u * JT, c * HALF + (u + 1) * JT)
+            if (b, c, u) == (1, 1, 3):
+                up = psum_y.tile([P, PACK, JT], F32, name="late_up", tag="acc")
+            else:
+                up = psum_u.tile([P, PACK, JT], F32, name="up")
+            for t in range(PACK):
+                nc.tensor.matmul_mx(
+                    out=up[:, t, :],
+                    lhsT=w_q[b][:, t * P : (t + 1) * P].bitcast(FP8X4),
+                    lhsT_scale=w_s[b][:, t * P : (t + 1) * P],
+                    rhs=v_w[:, js].bitcast(FP8X4),
+                    rhs_scale=v_s[:, js],
+                    start=True,
+                    stop=True,
+                )
+            dst = h_bf[b, c][:, u * JT * PACK : (u + 1) * JT * PACK].rearrange("p (j t) -> p j t", t=PACK)
+            if (b, c, u) in ON_GPSIMD:
+                up_sb = keep.tile([P, JT, PACK], F32, name=f"up_sb{b}", align_bytes=64)
+                nc.scalar.copy(up_sb[:], up[:].rearrange("p t j -> p j t"))
+                nc.gpsimd.tensor_tensor(dst, up_sb[:], act[b, c, u][:], MULT)
+            else:
+                nc.vector.tensor_tensor(dst, up[:].rearrange("p t j -> p j t"), act[b, c, u][:], MULT)
+
+        def quantise_hidden(b, c, codes):
+            h_q[b, c] = codes
+            cs = slice(c * HALF, (c + 1) * HALF)
+            nc.vector.quantize_mx(out=codes[:].bitcast(FP8X4), scales=h_s[b][:, cs], in_=h_bf[b, c][:])
+
+        wd_bf = {}
+        late = {}
+
+        def first_group():
+            nc.vector.quantize_mx(out=w_q[1][:].bitcast(FP8X4), scales=w_s[1][:], in_=second_bf[:])
+            quantise_hidden(0, 0, shared.tile([P, HALF], U32, name="h_q00", offset=20480, align_bytes=64))
+            late["wc"] = shared.tile([P, 2 * N], I32, name="wc_p", offset=22528, align_bytes=64)
+            nc.vector.tensor_copy(
+                late["wc"][:].rearrange("p (a t g m) -> p a g t m", a=2, t=PACK, m=4),
+                wc_raw[:].rearrange("p (a g m t) -> p a g t m", a=2, t=PACK, m=4),
+            )
+            for half in range(2):
+                wd_bf[half] = shared.tile(
+                    [P, 2 * PASS], BF16, name=f"wd_bf{half}", offset=4096 + 2048 * half, align_bytes=64
+                )
+                dst = wd_bf[half][:].rearrange("p (t m i) -> p m t i", t=2, i=PACK)
+                src = wd_raw[:].rearrange("p i (m t) -> p m t i", t=PACK)[:, :, 2 * half : 2 * half + 2]
+                if half == 0:
+                    nc.gpsimd.tensor_scalar(dst, src, 1.0, 0.0, MULT, ADD)
+                else:
+                    nc.scalar.copy(dst, src)
+
+        def second_group():
+            late["wd"] = keep.tile([P, PASS], U32, name="wd_q", tag="act102", align_bytes=64)
+            for half in range(2):
+                cols = slice(half * 2 * P, (half + 1) * 2 * P)
+                nc.vector.quantize_mx(
+                    out=late["wd"][:, cols].bitcast(FP8X4), scales=w_s[2][:, cols], in_=wd_bf[half][:]
+                )
+            quantise_hidden(1, 0, keep.tile([P, HALF], U32, name="h_q10", align_bytes=64))
+
+        def result(i, c, y):
             cs = slice(c * HALF, (c + 1) * HALF)
             acc = psum_y.tile([P, HALF], F32, name="acc")
-            nc.tensor.matmul_mx(
-                out=acc[:],
-                lhsT=w_q[2][:, i * P : (i + 1) * P].bitcast(FP8X4),
-                lhsT_scale=w_s[2][:, i * P : (i + 1) * P],
-                rhs=v_w[:, cs].bitcast(FP8X4),
-                rhs_scale=v_s[:, cs],
-                start=True,
-                stop=False,
-            )
             for a in range(2):
                 col = a * N + i * P
                 nc.tensor.matmul_mx(
                     out=acc[:],
-                    lhsT=wc_p[:, col : col + P].bitcast(FP8X4),
+                    lhsT=late["wc"][:, col : col + P].bitcast(FP8X4),
                     lhsT_scale=wc_s[:, col : col + P],
-                    rhs=h_q[a][:, cs].bitcast(FP8X4),
+                    rhs=h_q[a, c][:].bitcast(FP8X4),
                     rhs_scale=h_s[a][:, cs],
-                    start=False,
+                    start=(a == 0),
                     stop=(a == 1),
                 )
-            return acc
-
-        def result(i, c, y):
-            nc.scalar.activation(y, total(i, c)[:], ACT.Identity, bias=bias[:, i : i + 1])
+                if a == 0:
+                    nc.tensor.matmul_mx(
+                        out=acc[:],
+                        lhsT=late["wd"][:, i * P : (i + 1) * P].bitcast(FP8X4),
+                        lhsT_scale=w_s[2][:, i * P : (i + 1) * P],
+                        rhs=v_w[:, cs].bitcast(FP8X4),
+                        rhs_scale=v_s[:, cs],
+                        start=False,
+                        stop=False,
+                    )
+            nc.scalar.activation(y, acc[:], ACT.Identity, bias=bias[:, i : i + 1])
 
         def clear_page(i, tag):
             pages[i] = keep.tile([P, T2], F32, name=f"page{i}", tag=tag, align_bytes=64)
             nc.gpsimd.memset(pages[i][:], 0.0)
 
         out_rows = out.rearrange("(p i) t -> p i t", i=PACK)
-        for c in range(2):
-            y = keep.tile([P, HALF], F32, name=f"y0{c}", align_bytes=64)
-            result(0, c, y[:])
+
+        def place(i, c, tag):
+            y = keep.tile([P, HALF], F32, name=f"y{i}{c}", tag=tag, align_bytes=64)
+            result(i, c, y[:])
             nc.vector.tensor_tensor(
-                pages[0][:].indirect(put[:, c * HALF // 16 : (c + 1) * HALF // 16]),
+                pages[i][:].indirect(put[:, c * HALF // 16 : (c + 1) * HALF // 16]),
                 y[:],
                 weight[:, c * HALF : (c + 1) * HALF],
                 MULT,
             )
-            clear_page(c + 1, "h_bf01" if c == 0 else "y00")
-        nc.sync.dma_start(out_rows[:, 0, :], pages[0][:])
-        for i in range(1, PACK):
-            y = keep.tile([P, S], F32, name=f"y{i}", align_bytes=64)
-            for c in range(2):
-                result(i, c, y[:, c * HALF : (c + 1) * HALF])
-            nc.vector.tensor_tensor(pages[i][:].indirect(put[:]), y[:], weight[:], MULT)
-            if i == 1:
-                clear_page(3, "y01")
-            nc.sync.dma_start(out_rows[:, i, :], pages[i][:])
+            if c == 1:
+                nc.sync.dma_start(out_rows[:, i, :], pages[i][:])
+
+        for b in range(2):
+            h_bf[b, 0] = keep.tile([P, PACK * HALF], BF16, name=f"h_bf{b}0", align_bytes=64)
+        h_bf[0, 1] = keep.tile([P, PACK * HALF], BF16, name="h_bf01", align_bytes=64)
+        for k in range(AHEAD):
+            gate(*ORDER[k])
+        for k, tile in enumerate(ORDER):
+            product(*tile)
+            if k + AHEAD < len(ORDER):
+                gate(*ORDER[k + AHEAD])
+            if tile == (0, 0, 3):
+                first_group()
+            if tile == (1, 0, 3):
+                second_group()
+        clear_page(1, "act012")
+        place(0, 0, "act011")
+        clear_page(2, "act011")
+        place(1, 0, "y10")
+        for u in range(4):
+            gate(1, 1, u)
+        clear_page(3, "y10")
+        place(2, 0, "y20")
+        h_bf[1, 1] = keep.tile([P, PACK * HALF], BF16, name="h_bf11", tag="y20", align_bytes=64)
+        for u in (3, 0, 1, 2):
+            product(1, 1, u)
+        quantise_hidden(0, 1, keep.tile([P, HALF], U32, name="h_q01", tag="act110", align_bytes=64))
+        quantise_hidden(1, 1, keep.tile([P, HALF], U32, name="h_q11", align_bytes=64))
+        place(3, 0, "act111")
+        for i in range(PACK):
+            place(i, 1, f"y{i}1")

@@ -69,10 +69,10 @@ def tile_list_beam_cache_rewrite_kernel(
             )
         nc.scalar.activation(warm_out[:], warm[:], ACT.Silu)
         nc.sync.dma_start(wa_raw[:].bitcast(I32), wa_words[0].bitcast(I32))
+        nc.sync.dma_start(tab_w[:], tab_words[0].rearrange("p t i -> p (t i)").bitcast(I32))
         for n in range(2):
             wb_raw[n] = keep.tile([P, PACK, QUARTER], F32, name=f"wb_raw{n}", align_bytes=64)
             nc.sync.dma_start(wb_raw[n][:], wb_rows[:, :, n * QUARTER : (n + 1) * QUARTER])
-        nc.sync.dma_start(tab_w[:], tab_words[0].rearrange("p t i -> p (t i)").bitcast(I32))
         nc.sync.dma_start(put[:], offs2)
 
         pages = {0: keep.tile([P, T2], F32, name="page0", align_bytes=64)}
@@ -102,10 +102,10 @@ def tile_list_beam_cache_rewrite_kernel(
         )
         wd_raw = shared.tile([P, PACK, PASS], F32, name="wd_raw", offset=8192, align_bytes=64)
         nc.sync.dma_start(wd_raw[:], wd.rearrange("(p i) c -> p i c", i=PACK))
-        weight = shared.tile([P, S], F32, name="weight", offset=16384, align_bytes=64)
-        nc.sync.dma_start(weight[:], wgo)
         for r in range(4):
             nc.sync.dma_start(wc_s[r:P:32, :].bitcast(I32), planes[WC_ROW + 8 * r : P : 32, S:].bitcast(I32))
+        weight = shared.tile([P, S], F32, name="weight", offset=16384, align_bytes=64)
+        nc.sync.dma_start(weight[:], wgo)
         v_s = planes[:, 0:S]
         wa_s = planes[:, S:]
 
@@ -116,33 +116,36 @@ def tile_list_beam_cache_rewrite_kernel(
         )
         w_q = [keep.tile([P, PASS], U32, name=f"w_q{n}", align_bytes=64) for n in range(2)]
         w_s = [keep.tile([P, PASS], U8, name=f"w_s{n}", align_bytes=64) for n in range(3)]
-        first_bf = keep.tile([P, PACK * PASS], BF16, name="first_bf", align_bytes=64)
-        for n in range(2):
-            for part in range(2):
-                first = n * 64 + part * 32
-                nc.scalar.copy(
-                    first_bf[:].rearrange("p (t m i) -> p m t i", t=PACK, i=PACK)[:, first : first + 32],
-                    wb_raw[n][:].rearrange("p i (m t) -> p m t i", t=PACK)[:, part * 32 : (part + 1) * 32],
-                )
-        nc.vector.quantize_mx(out=w_q[0][:].bitcast(FP8X4), scales=w_s[0][:], in_=first_bf[:])
-        spare = psum_y.tile([P, HALF], F32, name="acc")
-        for k in range(3):
-            nc.tensor.matmul_mx(
-                out=spare[:],
-                lhsT=w_q[0][:, 0:P].bitcast(FP8X4),
-                lhsT_scale=w_s[0][:, 0:P],
-                rhs=w_q[0][:].bitcast(FP8X4),
-                rhs_scale=w_s[0][:],
-                start=True,
-                stop=True,
-            )
         for c in range(2):
             nc.vector.tensor_copy(
                 v_w[:, c * HALF : (c + 1) * HALF],
                 tab_w[:].bitcast(U32).indirect(pick[:, c * HALF // 16 : (c + 1) * HALF // 16]),
             )
+        spare = psum_y.tile([P, HALF], F32, name="acc")
+        for k in range(3):
+            nc.tensor.matmul_mx(
+                out=spare[:],
+                lhsT=wa_p[:, 0 : 2 * P].bitcast(FP4X4),
+                lhsT_scale=ws_raw[:, 0:P],
+                rhs=v_w[:, 0:HALF].bitcast(FP8X4),
+                rhs_scale=ws_raw[:, 0:HALF],
+                start=True,
+                stop=True,
+            )
+        first_bf = [keep.tile([P, 2 * PASS], BF16, name=f"first_bf{pair}", align_bytes=64) for pair in range(2)]
+        for n in range(2):
+            for pair in range(2):
+                dst = first_bf[pair][:].rearrange("p (t m i) -> p m t i", t=2, i=PACK)[:, n * 64 : (n + 1) * 64]
+                src = wb_raw[n][:].rearrange("p i (m t) -> p m t i", t=PACK)[:, :, 2 * pair : 2 * pair + 2]
+                if (n, pair) == (1, 1):
+                    nc.vector.tensor_copy(dst, src)
+                else:
+                    nc.scalar.copy(dst, src)
+        for pair in (1, 0):
+            cols = slice(pair * 2 * P, (pair + 1) * 2 * P)
+            nc.vector.quantize_mx(out=w_q[0][:, cols].bitcast(FP8X4), scales=w_s[0][:, cols], in_=first_bf[pair][:])
 
-        second_bf = keep.tile([P, PACK * PASS], BF16, name="second_bf", tag="tab_w", align_bytes=64)
+        second_bf = keep.tile([P, PACK * PASS], BF16, name="second_bf", tag="first_bf0", align_bytes=64)
         for n in (2, 3):
             nc.gpsimd.tensor_scalar(
                 second_bf[:].rearrange("p (t m i) -> p m t i", t=PACK, i=PACK)[:, (n - 2) * 64 : (n - 1) * 64],

@@ -48,13 +48,11 @@ def tile_list_beam_cache_rewrite_kernel(
         wa_raw = keep.tile([P, 2 * H], U8, name="wa_raw", align_bytes=64)
         tab_w = keep.tile([P, T], I32, name="tab_w", align_bytes=64)
         bias = keep.tile([P, PACK], F32, name="bias")
-        warm = keep.tile([P, 1], F32, name="warm", align_bytes=64)
         warm_out = keep.tile([P, 1], F32, name="warm_out")
         wc_s = keep.tile([P, H], U8, name="wc_s", align_bytes=64)
         wb_raw = {}
         wb_rows = wb.rearrange("(p i) c -> p i c", i=PACK)
 
-        nc.gpsimd.memset(warm[:], 0.0)
         nc.sync.dma_start(pick[:], offs)
         nc.sync.dma_start(
             tab_s[:].bitcast(I32), tab_scales[0].bitcast(I32).unsqueeze(1).to_broadcast([16, 8, T // 4])
@@ -67,7 +65,6 @@ def tile_list_beam_cache_rewrite_kernel(
                 ws_raw[1:P:2, a * N : (a + 1) * N].bitcast(I32),
                 wc_scales[a].bitcast(I32).unsqueeze(1).to_broadcast([16, 4, N // 4]),
             )
-        nc.scalar.activation(warm_out[:], warm[:], ACT.Silu)
         nc.sync.dma_start(wa_raw[:].bitcast(I32), wa_words[0].bitcast(I32))
         nc.sync.dma_start(tab_w[:], tab_words[0].rearrange("p t i -> p (t i)").bitcast(I32))
         for n in range(2):
@@ -78,6 +75,7 @@ def tile_list_beam_cache_rewrite_kernel(
         pages = {0: keep.tile([P, T2], F32, name="page0", align_bytes=64)}
         nc.vector.memset(pages[0][:, 0 : T2 // 2], 0.0)
         nc.gpsimd.memset(pages[0][:, T2 // 2 :], 0.0)
+        nc.scalar.activation(warm_out[:], pages[0][:, 0:1], ACT.Silu)
         nc.gpsimd.memset(wc_s[:].bitcast(I32), 0)
         nc.gpsimd.dma_start(bias[:], bo.rearrange("(p i) -> p i", i=PACK))
 
@@ -120,17 +118,6 @@ def tile_list_beam_cache_rewrite_kernel(
             nc.vector.tensor_copy(
                 v_w[:, c * HALF : (c + 1) * HALF],
                 tab_w[:].bitcast(U32).indirect(pick[:, c * HALF // 16 : (c + 1) * HALF // 16]),
-            )
-        spare = psum_y.tile([P, HALF], F32, name="acc")
-        for k in range(3):
-            nc.tensor.matmul_mx(
-                out=spare[:],
-                lhsT=wa_p[:, 0 : 2 * P].bitcast(FP4X4),
-                lhsT_scale=ws_raw[:, 0:P],
-                rhs=v_w[:, 0:HALF].bitcast(FP8X4),
-                rhs_scale=ws_raw[:, 0:HALF],
-                start=True,
-                stop=True,
             )
         first_bf = [keep.tile([P, 2 * PASS], BF16, name=f"first_bf{pair}", align_bytes=64) for pair in range(2)]
         for n in range(2):
@@ -187,7 +174,7 @@ def tile_list_beam_cache_rewrite_kernel(
                 up = psum_y.tile([P, PACK, JT], F32, name="late_up", tag="acc")
             else:
                 up = psum_u.tile([P, PACK, JT], F32, name="up")
-            for t in range(PACK):
+            for t in (2, 3, 0, 1):
                 nc.tensor.matmul_mx(
                     out=up[:, t, :],
                     lhsT=w_q[b][:, t * P : (t + 1) * P].bitcast(FP8X4),

@@ -252,7 +252,9 @@ def tile_list_beam_cache_rewrite_kernel(
                         start=False,
                         stop=False,
                     )
-            nc.scalar.activation(y, acc[:], ACT.Identity, bias=bias[:, i : i + 1])
+            if y is not None:
+                nc.scalar.activation(y, acc[:], ACT.Identity, bias=bias[:, i : i + 1])
+            return acc[:]
 
         def clear_page(i, tag):
             pages[i] = keep.tile([P, T2], F32, name=f"page{i}", tag=tag, align_bytes=64)
@@ -271,6 +273,18 @@ def tile_list_beam_cache_rewrite_kernel(
             )
             if c == 1:
                 nc.sync.dma_start(out_rows[:, i, :], pages[i][:])
+
+        def place_by_copy(i):
+            cs = slice(HALF, S)
+            weighed = keep.tile([P, HALF], F32, name=f"weighed{i}", tag="weighed", bufs=2, align_bytes=64)
+            if i == 0:
+                nc.vector.scalar_tensor_tensor(weighed[:], result(i, 1, None), bias[:, 0:1], weight[:, cs], ADD, MULT)
+            else:
+                y = keep.tile([P, HALF], F32, name=f"y{i}1", align_bytes=64)
+                result(i, 1, y[:])
+                nc.gpsimd.tensor_tensor(weighed[:], y[:], weight[:, cs], MULT)
+            nc.vector.tensor_copy(pages[i][:].indirect(put[:, HALF // 16 : S // 16]), weighed[:])
+            nc.sync.dma_start(out_rows[:, i, :], pages[i][:])
 
         for b in range(2):
             h_bf[b, 0] = keep.tile([P, PACK * HALF], BF16, name=f"h_bf{b}0", align_bytes=64)
@@ -300,4 +314,4 @@ def tile_list_beam_cache_rewrite_kernel(
         quantise_hidden(1, 1, keep.tile([P, HALF], U32, name="h_q11", align_bytes=64))
         place(3, 0, "act111")
         for i in range(PACK):
-            place(i, 1, f"y{i}1")
+            place_by_copy(i)

@@ -24,9 +24,15 @@ HALF = 512
 JT = 128
 QUARTER = 256
 WC_ROW = 5
-AHEAD = 2
-ON_GPSIMD = ((0, 1, 3), (1, 1, 3))
-ORDER = [(0, 0, u) for u in range(4)] + [(1, 0, u) for u in range(4)] + [(0, 1, u) for u in (3, 0, 1, 2)]
+PARTS = (slice(0, 512), slice(512, 768), slice(768, 1024))
+BANK = 2048
+ROOM = 2048
+WC_ROOM = 4096
+LATE_ROOM = 32768
+R0, R2, R1, R3 = (WC_ROOM + n * ROOM for n in range(1, 5))
+Y0, Y1, Y2, Y3 = (LATE_ROOM + n * ROOM for n in range(4))
+ACT_ROOM = {(0, 4): R0, (0, 5): R1}
+UP_ROOM = {(0, 4): R2, (0, 5): Y0, (1, 4): Y1, (1, 6): Y2, (1, 7): Y3}
 
 
 def tile_list_beam_cache_rewrite_kernel(
@@ -37,9 +43,7 @@ def tile_list_beam_cache_rewrite_kernel(
         lists = ctx.enter_context(tc.tile_pool(name="lists", bufs=1))
         keep = ctx.enter_context(tc.tile_pool(name="keep", bufs=1))
         shared = ctx.enter_context(tc.tile_pool(name="shared", bufs=1))
-        psum_g = ctx.enter_context(tc.psum_pool(name="psum_g", bufs=2))
-        psum_u = ctx.enter_context(tc.psum_pool(name="psum_u", bufs=4))
-        psum_y = ctx.enter_context(tc.psum_pool(name="psum_y", bufs=2))
+        psum = ctx.enter_context(tc.psum_pool(name="psum", bufs=1))
 
         pick = lists.tile([P, S // 16], U16, name="pick")
         put = lists.tile([P, S // 16], U16, name="put")
@@ -47,8 +51,6 @@ def tile_list_beam_cache_rewrite_kernel(
         ws_raw = keep.tile([P, H], U8, name="ws_raw", align_bytes=64)
         wa_raw = keep.tile([P, 2 * H], U8, name="wa_raw", align_bytes=64)
         tab_w = keep.tile([P, T], I32, name="tab_w", align_bytes=64)
-        bias = keep.tile([P, PACK], F32, name="bias")
-        warm_out = keep.tile([P, 1], F32, name="warm_out")
         wc_s = keep.tile([P, H], U8, name="wc_s", align_bytes=64)
         wb_raw = {}
         wb_rows = wb.rearrange("(p i) c -> p i c", i=PACK)
@@ -71,17 +73,20 @@ def tile_list_beam_cache_rewrite_kernel(
             wb_raw[n] = keep.tile([P, PACK, QUARTER], F32, name=f"wb_raw{n}", align_bytes=64)
             nc.sync.dma_start(wb_raw[n][:], wb_rows[:, :, n * QUARTER : (n + 1) * QUARTER])
         nc.sync.dma_start(put[:], offs2)
+        bias = keep.tile([P, PACK], F32, name="bias")
+        nc.sync.dma_start(bias[:], bo.rearrange("(p i) -> p i", i=PACK))
 
-        pages = {0: keep.tile([P, T2], F32, name="page0", align_bytes=64)}
-        nc.vector.memset(pages[0][:, 0 : T2 // 2], 0.0)
-        nc.gpsimd.memset(pages[0][:, T2 // 2 :], 0.0)
-        nc.scalar.activation(warm_out[:], pages[0][:, 0:1], ACT.Silu)
+        pages = {i: keep.tile([P, T2], F32, name=f"page{i}", align_bytes=64) for i in range(3)}
+        nc.gpsimd.memset(pages[0][:], 0.0)
+        warm = keep.tile([P, 2], F32, name="warm")
+        nc.vector.memset(warm[:, 0:1], 0.0)
+        nc.scalar.activation(warm[:, 1:2], warm[:, 0:1], ACT.Silu)
+        nc.vector.memset(pages[1][:], 0.0)
+        nc.gpsimd.memset(pages[2][:], 0.0)
         nc.gpsimd.memset(wc_s[:].bitcast(I32), 0)
-        nc.gpsimd.dma_start(bias[:], bo.rearrange("(p i) -> p i", i=PACK))
 
-        picked_s = shared.tile([P, 24576], U8, name="picked_s", offset=0, align_bytes=64)
+        picked_s = shared.tile([P, 32768], U8, name="picked_s", offset=0, align_bytes=64)
         planes = keep.tile([P, S + H], U8, name="planes", align_bytes=64)
-        v_w = keep.tile([P, S], U32, name="v_w", align_bytes=64)
         nc.vector.tensor_copy(picked_s[:, 0:S], tab_s[:].indirect(pick[:]))
         nc.vector.tensor_copy(
             planes[:, S:].rearrange("p (b t g m) -> p b g t m", b=2, t=PACK, m=16),
@@ -93,32 +98,43 @@ def tile_list_beam_cache_rewrite_kernel(
         for n, offset in ((2, 0), (3, 20480)):
             wb_raw[n] = shared.tile([P, PACK, QUARTER], F32, name=f"wb_raw{n}", offset=offset, align_bytes=64)
             nc.sync.dma_start(wb_raw[n][:], wb_rows[:, :, n * QUARTER : (n + 1) * QUARTER])
+        for r in range(4):
+            nc.sync.dma_start(wc_s[r:P:32, :].bitcast(I32), planes[WC_ROW + 8 * r : P : 32, S:].bitcast(I32))
+        wd_raw = shared.tile([P, PACK, PASS], F32, name="wd_raw", offset=8192, align_bytes=64)
+        nc.sync.dma_start(wd_raw[:], wd.rearrange("(p i) c -> p i c", i=PACK))
+        weight = shared.tile([P, S], F32, name="weight", offset=16384, align_bytes=64)
+        nc.sync.dma_start(weight[:, 0:HALF], wgo[:, 0:HALF])
         wc_raw = shared.tile([P, 2 * N], I32, name="wc_raw", offset=4096, align_bytes=64)
         nc.sync.dma_start(
             wc_raw[:].rearrange("p (a c) -> p a c", a=2),
             wc_words.rearrange("a p c i -> p a (c i)").bitcast(I32),
         )
-        wd_raw = shared.tile([P, PACK, PASS], F32, name="wd_raw", offset=8192, align_bytes=64)
-        nc.sync.dma_start(wd_raw[:], wd.rearrange("(p i) c -> p i c", i=PACK))
-        for r in range(4):
-            nc.sync.dma_start(wc_s[r:P:32, :].bitcast(I32), planes[WC_ROW + 8 * r : P : 32, S:].bitcast(I32))
-        weight = shared.tile([P, S], F32, name="weight", offset=16384, align_bytes=64)
-        nc.sync.dma_start(weight[:], wgo)
+        nc.sync.dma_start(weight[:, HALF:], wgo[:, HALF:])
+        pages[3] = shared.tile([P, T2], F32, name="page3", offset=24576, align_bytes=64)
+        nc.gpsimd.memset(pages[3][:], 0.0)
         v_s = planes[:, 0:S]
         wa_s = planes[:, S:]
 
         wa_p = keep.tile([P, 2 * H], U8, name="wa_p", align_bytes=64)
-        nc.vector.tensor_copy(
+        nc.scalar.copy(
             wa_p[:].bitcast(U16).rearrange("p (b t g m) -> p b g t m", b=2, t=PACK, m=8),
             wa_raw[:].bitcast(U16).rearrange("p (b g m t) -> p b g t m", b=2, t=PACK, m=8),
         )
         w_q = [keep.tile([P, PASS], U32, name=f"w_q{n}", align_bytes=64) for n in range(2)]
         w_s = [keep.tile([P, PASS], U8, name=f"w_s{n}", align_bytes=64) for n in range(3)]
-        for c in range(2):
-            nc.vector.tensor_copy(
-                v_w[:, c * HALF : (c + 1) * HALF],
-                tab_w[:].bitcast(U32).indirect(pick[:, c * HALF // 16 : (c + 1) * HALF // 16]),
-            )
+        v_w = {}
+
+        def gather_words(k, tag):
+            js = PARTS[k]
+            v_w[k] = keep.tile([P, js.stop - js.start], U32, name=f"v_w{k}", tag=tag, align_bytes=64)
+            nc.vector.tensor_copy(v_w[k][:], tab_w[:].bitcast(U32).indirect(pick[:, js.start // 16 : js.stop // 16]))
+
+        def words(first, width):
+            k = max(n for n in range(len(PARTS)) if PARTS[n].start <= first)
+            return v_w[k][:, first - PARTS[k].start : first - PARTS[k].start + width].bitcast(FP8X4)
+
+        gather_words(0, "v_w0")
+        gather_words(1, "v_w1")
         first_bf = [keep.tile([P, 2 * PASS], BF16, name=f"first_bf{pair}", align_bytes=64) for pair in range(2)]
         for n in range(2):
             for pair in range(2):
@@ -132,186 +148,220 @@ def tile_list_beam_cache_rewrite_kernel(
             cols = slice(pair * 2 * P, (pair + 1) * 2 * P)
             nc.vector.quantize_mx(out=w_q[0][:, cols].bitcast(FP8X4), scales=w_s[0][:, cols], in_=first_bf[pair][:])
 
+        gather_words(2, "first_bf1")
         second_bf = keep.tile([P, PACK * PASS], BF16, name="second_bf", tag="first_bf0", align_bytes=64)
         for n in (2, 3):
-            nc.gpsimd.tensor_scalar(
-                second_bf[:].rearrange("p (t m i) -> p m t i", t=PACK, i=PACK)[:, (n - 2) * 64 : (n - 1) * 64],
-                wb_raw[n][:].rearrange("p i (m t) -> p m t i", t=PACK),
-                1.0,
-                0.0,
-                MULT,
-                ADD,
-            )
+            dst = second_bf[:].rearrange("p (t m i) -> p m t i", t=PACK, i=PACK)[:, (n - 2) * 64 : (n - 1) * 64]
+            src = wb_raw[n][:].rearrange("p i (m t) -> p m t i", t=PACK)
+            nc.gpsimd.tensor_scalar(dst, src, 1.0, 0.0, MULT, ADD)
 
-        h_q = {}
-        h_s = [keep.tile([P, S], U8, name=f"h_s{b}", align_bytes=64) for b in range(2)]
-        h_bf = {}
         act = {}
+        h_q = {}
+        h_s = {}
+        late = {}
 
-        def gate(b, c, u):
-            js = slice(c * HALF + u * JT, c * HALF + (u + 1) * JT)
-            if (b, c) == (1, 1):
-                bank = psum_y.tile([P, PACK, JT], F32, name="late_gate", tag="acc")
-            else:
-                bank = psum_g.tile([P, PACK, JT], F32, name="gate")
+        def gate(b, u):
+            js = slice(u * JT, (u + 1) * JT)
+            bank = psum.tile([P, PACK, JT], F32, name=f"gate{b}{u}", offset=(u % 2) * BANK)
             for t in range(PACK):
                 col = b * PASS + t * P
                 nc.tensor.matmul_mx(
                     out=bank[:, t, :],
                     lhsT=wa_p[:, 2 * col : 2 * (col + P)].bitcast(FP4X4),
                     lhsT_scale=wa_s[:, col : col + P],
-                    rhs=v_w[:, js].bitcast(FP8X4),
+                    rhs=words(js.start, js.stop - js.start),
                     rhs_scale=v_s[:, js],
                     start=True,
                     stop=True,
                 )
-            act[b, c, u] = keep.tile([P, JT, PACK], F32, name=f"act{b}{c}{u}", align_bytes=64)
-            nc.scalar.activation(act[b, c, u][:], bank[:].rearrange("p t j -> p j t"), ACT.Silu)
-
-        def product(b, c, u):
-            js = slice(c * HALF + u * JT, c * HALF + (u + 1) * JT)
-            if (b, c, u) == (1, 1, 3):
-                up = psum_y.tile([P, PACK, JT], F32, name="late_up", tag="acc")
+            if (b, u) in ACT_ROOM:
+                act[b, u] = shared.tile([P, JT, PACK], F32, name=f"act{b}{u}", offset=ACT_ROOM[b, u], align_bytes=64)
             else:
-                up = psum_u.tile([P, PACK, JT], F32, name="up")
+                act[b, u] = keep.tile([P, JT, PACK], F32, name=f"act{b}{u}", align_bytes=64)
+            nc.scalar.activation(act[b, u][:], bank[:].rearrange("p t j -> p j t"), ACT.Silu)
+
+        up_sb = {}
+
+        def up_tile(b, u):
+            js = slice(u * JT, (u + 1) * JT)
+            bank = 2 + u % 3 if u < 4 else 3 + u % 2
+            up = psum.tile([P, PACK, JT], F32, name=f"up{b}{u}", offset=bank * BANK)
             for t in (2, 3, 0, 1):
                 nc.tensor.matmul_mx(
                     out=up[:, t, :],
                     lhsT=w_q[b][:, t * P : (t + 1) * P].bitcast(FP8X4),
                     lhsT_scale=w_s[b][:, t * P : (t + 1) * P],
-                    rhs=v_w[:, js].bitcast(FP8X4),
+                    rhs=words(js.start, JT),
                     rhs_scale=v_s[:, js],
                     start=True,
                     stop=True,
                 )
-            dst = h_bf[b, c][:, u * JT * PACK : (u + 1) * JT * PACK].rearrange("p (j t) -> p j t", t=PACK)
-            if (b, c, u) in ON_GPSIMD:
-                up_sb = keep.tile([P, JT, PACK], F32, name=f"up_sb{b}", align_bytes=64)
-                nc.scalar.copy(up_sb[:], up[:].rearrange("p t j -> p j t"))
-                nc.gpsimd.tensor_tensor(dst, up_sb[:], act[b, c, u][:], MULT)
+            return up[:].rearrange("p t j -> p j t")
+
+        def hidden_slice(h_bf, u, first):
+            return h_bf[:, (u - first) * PASS : (u - first + 1) * PASS].rearrange("p (j t) -> p j t", t=PACK)
+
+        def product(b, u, h_bf, first):
+            nc.vector.tensor_tensor(hidden_slice(h_bf, u, first), up_tile(b, u), act[b, u][:], MULT)
+
+        def stage(b, u):
+            gate(b, u)
+            if (b, u) in UP_ROOM:
+                up_sb[b, u] = shared.tile([P, JT, PACK], F32, name=f"up_sb{b}{u}", offset=UP_ROOM[b, u], align_bytes=64)
             else:
-                nc.vector.tensor_tensor(dst, up[:].rearrange("p t j -> p j t"), act[b, c, u][:], MULT)
+                up_sb[b, u] = keep.tile([P, JT, PACK], F32, name=f"up_sb{b}{u}", align_bytes=64)
+            nc.scalar.copy(up_sb[b, u][:], up_tile(b, u))
 
-        def quantise_hidden(b, c, codes):
-            h_q[b, c] = codes
-            cs = slice(c * HALF, (c + 1) * HALF)
-            nc.vector.quantize_mx(out=codes[:].bitcast(FP8X4), scales=h_s[b][:, cs], in_=h_bf[b, c][:])
+        def hidden_tile(k, b, width):
+            if k > 0 and b == 0:
+                return shared.tile([P, PACK * width], BF16, name=f"h_bf{k}0", offset=WC_ROOM, align_bytes=64)
+            return keep.tile([P, PACK * width], BF16, name=f"h_bf{k}{b}", tag=f"h_bf{b}", align_bytes=64)
 
-        wd_bf = {}
-        late = {}
+        def hidden(k, first):
+            h_bf = []
+            for b in range(2):
+                h_bf.append(hidden_tile(k, b, QUARTER))
+                for u in (first, first + 1):
+                    nc.gpsimd.tensor_tensor(hidden_slice(h_bf[b], u, first), up_sb[b, u][:], act[b, u][:], MULT)
+            return h_bf
 
-        def first_group():
-            nc.vector.quantize_mx(out=w_q[1][:].bitcast(FP8X4), scales=w_s[1][:], in_=second_bf[:])
-            quantise_hidden(0, 0, shared.tile([P, HALF], U32, name="h_q00", offset=20480, align_bytes=64))
-            late["wc"] = shared.tile([P, 2 * N], I32, name="wc_p", offset=22528, align_bytes=64)
-            nc.vector.tensor_copy(
-                late["wc"][:].rearrange("p (a t g m) -> p a g t m", a=2, t=PACK, m=4),
-                wc_raw[:].rearrange("p (a g m t) -> p a g t m", a=2, t=PACK, m=4),
-            )
-            for half in range(2):
-                wd_bf[half] = shared.tile(
-                    [P, 2 * PASS], BF16, name=f"wd_bf{half}", offset=4096 + 2048 * half, align_bytes=64
-                )
-                dst = wd_bf[half][:].rearrange("p (t m i) -> p m t i", t=2, i=PACK)
-                src = wd_raw[:].rearrange("p i (m t) -> p m t i", t=PACK)[:, :, 2 * half : 2 * half + 2]
-                if half == 0:
-                    nc.gpsimd.tensor_scalar(dst, src, 1.0, 0.0, MULT, ADD)
-                else:
-                    nc.scalar.copy(dst, src)
+        def quantise_rows(k, b, h_bf, codes_tag, scales_tag):
+            width = PARTS[k].stop - PARTS[k].start
+            h_q[k, b] = keep.tile([P, width], U32, name=f"h_q{k}{b}", tag=codes_tag, align_bytes=64)
+            h_s[k, b] = keep.tile([P, width], U8, name=f"h_s{k}{b}", tag=scales_tag, align_bytes=64)
+            nc.vector.quantize_mx(out=h_q[k, b][:].bitcast(FP8X4), scales=h_s[k, b][:], in_=h_bf[:])
 
-        def second_group():
-            late["wd"] = keep.tile([P, PASS], U32, name="wd_q", tag="act102", align_bytes=64)
-            for half in range(2):
-                cols = slice(half * 2 * P, (half + 1) * 2 * P)
-                nc.vector.quantize_mx(
-                    out=late["wd"][:, cols].bitcast(FP8X4), scales=w_s[2][:, cols], in_=wd_bf[half][:]
-                )
-            quantise_hidden(1, 0, keep.tile([P, HALF], U32, name="h_q10", align_bytes=64))
+        def quantise_hidden(k, h_bf, codes_tag, scales_tag):
+            quantise_rows(k, 0, h_bf[0], codes_tag, scales_tag)
+            quantise_rows(k, 1, h_bf[1], f"h_q{k}1", f"h_s{k}1")
 
-        def result(i, c, y):
-            cs = slice(c * HALF, (c + 1) * HALF)
-            acc = psum_y.tile([P, HALF], F32, name="acc")
-            for a in range(2):
-                col = a * N + i * P
+        def sums(k, rows, bank):
+            js = PARTS[k]
+            width = js.stop - js.start
+            acc = psum.tile([P, len(rows), width], F32, name=f"acc{k}{rows[0]}", offset=bank * BANK)
+            for n, i in enumerate(rows):
                 nc.tensor.matmul_mx(
-                    out=acc[:],
-                    lhsT=late["wc"][:, col : col + P].bitcast(FP8X4),
-                    lhsT_scale=wc_s[:, col : col + P],
-                    rhs=h_q[a, c][:].bitcast(FP8X4),
-                    rhs_scale=h_s[a][:, cs],
-                    start=(a == 0),
-                    stop=(a == 1),
+                    out=acc[:, n, :],
+                    lhsT=late["wd"][:, i * P : (i + 1) * P].bitcast(FP8X4),
+                    lhsT_scale=w_s[2][:, i * P : (i + 1) * P],
+                    rhs=words(js.start, width),
+                    rhs_scale=v_s[:, js],
+                    start=(n == 0),
+                    stop=False,
                 )
-                if a == 0:
+            for n, i in enumerate(rows):
+                for a in range(2):
+                    col = a * N + i * P
                     nc.tensor.matmul_mx(
-                        out=acc[:],
-                        lhsT=late["wd"][:, i * P : (i + 1) * P].bitcast(FP8X4),
-                        lhsT_scale=w_s[2][:, i * P : (i + 1) * P],
-                        rhs=v_w[:, cs].bitcast(FP8X4),
-                        rhs_scale=v_s[:, cs],
+                        out=acc[:, n, :],
+                        lhsT=late["wc"][:, col : col + P].bitcast(FP8X4),
+                        lhsT_scale=wc_s[:, col : col + P],
+                        rhs=h_q[k, a][:].bitcast(FP8X4),
+                        rhs_scale=h_s[k, a][:],
                         start=False,
-                        stop=False,
+                        stop=(n == len(rows) - 1 and a == 1),
                     )
-            if y is not None:
-                nc.scalar.activation(y, acc[:], ACT.Identity, bias=bias[:, i : i + 1])
-            return acc[:]
+            return {i: acc[:, n, :] for n, i in enumerate(rows)}
 
-        def clear_page(i, tag):
-            pages[i] = keep.tile([P, T2], F32, name=f"page{i}", tag=tag, align_bytes=64)
-            nc.gpsimd.memset(pages[i][:], 0.0)
+        def result_tile(name, width, tag=""):
+            return keep.tile([P, width], F32, name=name, tag=tag or name, align_bytes=64)
+
+        def weigh_on_vector(k, i, acc, tag=""):
+            weighed = result_tile(f"weighed{k}{i}", PARTS[k].stop - PARTS[k].start, tag)
+            nc.vector.scalar_tensor_tensor(weighed[:], acc, bias[:, i : i + 1], weight[:, PARTS[k]], ADD, MULT)
+            return weighed
+
+        def add_bias(i, acc, dst):
+            nc.scalar.activation(dst, acc, ACT.Identity, bias=bias[:, i : i + 1])
+
+        def weigh_on_gpsimd(k, i, acc, room):
+            width = PARTS[k].stop - PARTS[k].start
+            y = shared.tile([P, width], F32, name=f"y{k}{i}", offset=room, align_bytes=64)
+            add_bias(i, acc, y[:])
+            weighed = result_tile(f"weighed{k}{i}", width)
+            nc.gpsimd.tensor_tensor(weighed[:], y[:], weight[:, PARTS[k]], MULT)
+            return weighed
+
+        def window(i, js):
+            return pages[i][:].indirect(put[:, js.start // 16 : js.stop // 16])
+
+        def scatter(i, k, weighed):
+            nc.vector.tensor_copy(window(i, PARTS[k]), weighed[:])
 
         out_rows = out.rearrange("(p i) t -> p i t", i=PACK)
 
-        def place(i, c, tag):
-            y = keep.tile([P, HALF], F32, name=f"y{i}{c}", tag=tag, align_bytes=64)
-            result(i, c, y[:])
-            nc.vector.tensor_tensor(
-                pages[i][:].indirect(put[:, c * HALF // 16 : (c + 1) * HALF // 16]),
-                y[:],
-                weight[:, c * HALF : (c + 1) * HALF],
-                MULT,
-            )
-            if c == 1:
-                nc.sync.dma_start(out_rows[:, i, :], pages[i][:])
-
-        def place_by_copy(i):
-            cs = slice(HALF, S)
-            weighed = keep.tile([P, HALF], F32, name=f"weighed{i}", tag="weighed", bufs=2, align_bytes=64)
-            if i == 0:
-                nc.vector.scalar_tensor_tensor(weighed[:], result(i, 1, None), bias[:, 0:1], weight[:, cs], ADD, MULT)
-            else:
-                y = keep.tile([P, HALF], F32, name=f"y{i}1", align_bytes=64)
-                result(i, 1, y[:])
-                nc.gpsimd.tensor_tensor(weighed[:], y[:], weight[:, cs], MULT)
-            nc.vector.tensor_copy(pages[i][:].indirect(put[:, HALF // 16 : S // 16]), weighed[:])
+        def scatter_last(i, js, y):
+            nc.vector.tensor_tensor(window(i, js), y[:], weight[:, js], MULT)
             nc.sync.dma_start(out_rows[:, i, :], pages[i][:])
 
-        for b in range(2):
-            h_bf[b, 0] = keep.tile([P, PACK * HALF], BF16, name=f"h_bf{b}0", align_bytes=64)
-        h_bf[0, 1] = keep.tile([P, PACK * HALF], BF16, name="h_bf01", align_bytes=64)
-        for k in range(AHEAD):
-            gate(*ORDER[k])
-        for k, tile in enumerate(ORDER):
-            product(*tile)
-            if k + AHEAD < len(ORDER):
-                gate(*ORDER[k + AHEAD])
-            if tile == (0, 0, 3):
-                first_group()
-            if tile == (1, 0, 3):
-                second_group()
-        clear_page(1, "act012")
-        place(0, 0, "act011")
-        clear_page(2, "act011")
-        place(1, 0, "y10")
+        h_bf = [hidden_tile(0, b, HALF) for b in range(2)]
         for u in range(4):
-            gate(1, 1, u)
-        clear_page(3, "y10")
-        place(2, 0, "y20")
-        h_bf[1, 1] = keep.tile([P, PACK * HALF], BF16, name="h_bf11", tag="y20", align_bytes=64)
-        for u in (3, 0, 1, 2):
-            product(1, 1, u)
-        quantise_hidden(0, 1, keep.tile([P, HALF], U32, name="h_q01", tag="act110", align_bytes=64))
-        quantise_hidden(1, 1, keep.tile([P, HALF], U32, name="h_q11", align_bytes=64))
-        place(3, 0, "act111")
-        for i in range(PACK):
-            place_by_copy(i)
+            gate(0, u)
+        for u in range(4):
+            product(0, u, h_bf[0], 0)
+            gate(1, u)
+        nc.vector.quantize_mx(out=w_q[1][:].bitcast(FP8X4), scales=w_s[1][:], in_=second_bf[:])
+        quantise_rows(0, 0, h_bf[0], "first_bf0", "h_s00")
+        for u in range(4):
+            product(1, u, h_bf[1], 0)
+        late["wc"] = keep.tile([P, 2 * N], I32, name="wc_p", align_bytes=64)
+        nc.scalar.copy(
+            late["wc"][:].bitcast(U32).rearrange("p (a t g m) -> p a g t m", a=2, t=PACK, m=4),
+            wc_raw[:].bitcast(U32).rearrange("p (a g m t) -> p a g t m", a=2, t=PACK, m=4),
+        )
+        wd_bf = {
+            0: keep.tile([P, 2 * PASS], BF16, name="wd_bf0", tag="h_bf0", align_bytes=64),
+            1: shared.tile([P, 2 * PASS], BF16, name="wd_bf1", offset=WC_ROOM, align_bytes=64),
+        }
+        for half in range(2):
+            dst = wd_bf[half][:].rearrange("p (t m i) -> p m t i", t=2, i=PACK)
+            src = wd_raw[:].rearrange("p i (m t) -> p m t i", t=PACK)[:, :, 2 * half : 2 * half + 2]
+            if half == 0:
+                nc.gpsimd.tensor_scalar(dst, src, 1.0, 0.0, MULT, ADD)
+            else:
+                nc.scalar.copy(dst, src)
+        late["wd"] = keep.tile([P, PASS], U32, name="wd_q", align_bytes=64)
+
+        def quantise_wd(half):
+            cols = slice(half * 2 * P, (half + 1) * 2 * P)
+            nc.vector.quantize_mx(out=late["wd"][:, cols].bitcast(FP8X4), scales=w_s[2][:, cols], in_=wd_bf[half][:])
+
+        quantise_wd(0)
+        quantise_rows(0, 1, h_bf[1], "h_q01", "h_bf0")
+        quantise_wd(1)
+
+        first = weigh_on_vector(0, 0, sums(0, (0,), 5)[0])
+        second = weigh_on_gpsimd(0, 1, sums(0, (1,), 6)[1], Y0)
+        third = weigh_on_gpsimd(0, 3, sums(0, (3,), 2)[3], Y1)
+        held = sums(0, (2,), 7)[2]
+        scatter(0, 0, first)
+        scatter(1, 0, second)
+        scatter(3, 0, third)
+        for tile in ((0, 4), (0, 5), (1, 4), (0, 6), (0, 7), (1, 5)):
+            stage(*tile)
+        quantise_hidden(1, hidden(1, 4), "act15", "weighed03")
+
+        scatter(2, 0, weigh_on_vector(0, 2, held, "h_bf1"))
+        acc = sums(1, (0, 1), 5)
+        first = weigh_on_gpsimd(1, 0, acc[0], Y2)
+        second = weigh_on_gpsimd(1, 1, acc[1], Y3)
+        y_wide = result_tile("y_wide", HALF)
+        add_bias(2, sums(1, (2,), 6)[2], y_wide[:, 0:QUARTER])
+        held = sums(1, (3,), 2)[3]
+        scatter(0, 1, first)
+        scatter(1, 1, second)
+        for tile in ((1, 6), (1, 7)):
+            stage(*tile)
+        quantise_hidden(2, hidden(2, 6), "act17", "weighed11")
+
+        scatter(3, 1, weigh_on_vector(1, 3, held, "h_bf1"))
+        for rows, bank in (((0,), 5), ((1,), 6), ((3, 2), 7)):
+            acc = sums(2, rows, bank)
+            for i in rows:
+                if i == 2:
+                    add_bias(i, acc[i], y_wide[:, QUARTER:])
+                    scatter_last(i, slice(HALF, S), y_wide)
+                else:
+                    y = result_tile(f"y2{i}", QUARTER)
+                    add_bias(i, acc[i], y[:])
+                    scatter_last(i, PARTS[2], y)

@@ -27,12 +27,13 @@ WC_ROW = 5
 PARTS = (slice(0, 512), slice(512, 768), slice(768, 1024))
 BANK = 2048
 ROOM = 2048
-WC_ROOM = 4096
-LATE_ROOM = 32768
-R0, R2, R1, R3 = (WC_ROOM + n * ROOM for n in range(1, 5))
+WC_ROOM = 12288
+HIDDEN_ROOM = {(0, 1): 7168, (1, 0): 8192, (2, 0): 8192, (1, 1): 10240}
+LATE_ROOM = 40960
+R0, R1 = (WC_ROOM + n * ROOM for n in range(2))
 Y0, Y1, Y2, Y3 = (LATE_ROOM + n * ROOM for n in range(4))
-ACT_ROOM = {(0, 4): R0, (0, 5): R1}
-UP_ROOM = {(0, 4): R2, (0, 5): Y0, (1, 4): Y1, (1, 6): Y2, (1, 7): Y3}
+ACT_ROOM = {(0, 5): R0, (1, 4): R1}
+UP_ROOM = {(0, 5): Y0, (1, 6): Y2, (1, 7): Y3}
 
 
 def tile_list_beam_cache_rewrite_kernel(
@@ -76,16 +77,16 @@ def tile_list_beam_cache_rewrite_kernel(
         bias = keep.tile([P, PACK], F32, name="bias")
         nc.sync.dma_start(bias[:], bo.rearrange("(p i) -> p i", i=PACK))
 
-        pages = {i: keep.tile([P, T2], F32, name=f"page{i}", align_bytes=64) for i in range(3)}
-        nc.gpsimd.memset(pages[0][:], 0.0)
+        pages = {i: keep.tile([P, T2], F32, name=f"page{i}", align_bytes=64) for i in range(2)}
+        nc.gpsimd.memset(wc_s[:].bitcast(I32), 0)
+        nc.gpsimd.memset(pages[1][:, 0:HALF], 0.0)
         warm = keep.tile([P, 2], F32, name="warm")
         nc.vector.memset(warm[:, 0:1], 0.0)
         nc.scalar.activation(warm[:, 1:2], warm[:, 0:1], ACT.Silu)
-        nc.vector.memset(pages[1][:], 0.0)
-        nc.gpsimd.memset(pages[2][:], 0.0)
-        nc.gpsimd.memset(wc_s[:].bitcast(I32), 0)
+        nc.vector.memset(pages[0][:], 0.0)
+        nc.vector.memset(pages[1][:, HALF:], 0.0)
 
-        picked_s = shared.tile([P, 32768], U8, name="picked_s", offset=0, align_bytes=64)
+        picked_s = shared.tile([P, LATE_ROOM], U8, name="picked_s", offset=0, align_bytes=64)
         planes = keep.tile([P, S + H], U8, name="planes", align_bytes=64)
         nc.vector.tensor_copy(picked_s[:, 0:S], tab_s[:].indirect(pick[:]))
         nc.vector.tensor_copy(
@@ -95,22 +96,22 @@ def tile_list_beam_cache_rewrite_kernel(
         nc.vector.tensor_copy(planes[:, 0:S].bitcast(I32), picked_s[:, 0:S].bitcast(I32))
         for r in range(1, 4):
             nc.sync.dma_start(planes[r:P:32, :].bitcast(I32), planes[8 * r : P : 32, :].bitcast(I32))
-        for n, offset in ((2, 0), (3, 20480)):
+        for n, offset in ((2, 0), (3, 28672)):
             wb_raw[n] = shared.tile([P, PACK, QUARTER], F32, name=f"wb_raw{n}", offset=offset, align_bytes=64)
             nc.sync.dma_start(wb_raw[n][:], wb_rows[:, :, n * QUARTER : (n + 1) * QUARTER])
         for r in range(4):
             nc.sync.dma_start(wc_s[r:P:32, :].bitcast(I32), planes[WC_ROW + 8 * r : P : 32, S:].bitcast(I32))
-        wd_raw = shared.tile([P, PACK, PASS], F32, name="wd_raw", offset=8192, align_bytes=64)
+        wd_raw = shared.tile([P, PACK, PASS], F32, name="wd_raw", offset=16384, align_bytes=64)
         nc.sync.dma_start(wd_raw[:], wd.rearrange("(p i) c -> p i c", i=PACK))
-        weight = shared.tile([P, S], F32, name="weight", offset=16384, align_bytes=64)
+        weight = shared.tile([P, S], F32, name="weight", offset=24576, align_bytes=64)
         nc.sync.dma_start(weight[:, 0:HALF], wgo[:, 0:HALF])
-        wc_raw = shared.tile([P, 2 * N], I32, name="wc_raw", offset=4096, align_bytes=64)
+        wc_raw = shared.tile([P, 2 * N], I32, name="wc_raw", offset=WC_ROOM, align_bytes=64)
         nc.sync.dma_start(
             wc_raw[:].rearrange("p (a c) -> p a c", a=2),
             wc_words.rearrange("a p c i -> p a (c i)").bitcast(I32),
         )
         nc.sync.dma_start(weight[:, HALF:], wgo[:, HALF:])
-        pages[3] = shared.tile([P, T2], F32, name="page3", offset=24576, align_bytes=64)
+        pages[3] = shared.tile([P, T2], F32, name="page3", offset=32768, align_bytes=64)
         nc.gpsimd.memset(pages[3][:], 0.0)
         v_s = planes[:, 0:S]
         wa_s = planes[:, S:]
@@ -184,7 +185,7 @@ def tile_list_beam_cache_rewrite_kernel(
 
         def up_tile(b, u):
             js = slice(u * JT, (u + 1) * JT)
-            bank = 2 + u % 3 if u < 4 else 3 + u % 2
+            bank = 2 + u % 3 if u < 4 else 4 - u % 2
             up = psum.tile([P, PACK, JT], F32, name=f"up{b}{u}", offset=bank * BANK)
             for t in (2, 3, 0, 1):
                 nc.tensor.matmul_mx(
@@ -213,16 +214,15 @@ def tile_list_beam_cache_rewrite_kernel(
             nc.scalar.copy(up_sb[b, u][:], up_tile(b, u))
 
         def hidden_tile(k, b, width):
-            if k > 0 and b == 0:
-                return shared.tile([P, PACK * width], BF16, name=f"h_bf{k}0", offset=WC_ROOM, align_bytes=64)
-            return keep.tile([P, PACK * width], BF16, name=f"h_bf{k}{b}", tag=f"h_bf{b}", align_bytes=64)
+            if (k, b) in HIDDEN_ROOM:
+                return shared.tile([P, PACK * width], BF16, name=f"h_bf{k}{b}", offset=HIDDEN_ROOM[k, b], align_bytes=64)
+            return keep.tile([P, PACK * width], BF16, name=f"h_bf{k}{b}", align_bytes=64)
 
-        def hidden(k, first):
-            h_bf = []
+        def hidden(h_bf, first):
             for b in range(2):
-                h_bf.append(hidden_tile(k, b, QUARTER))
                 for u in (first, first + 1):
-                    nc.gpsimd.tensor_tensor(hidden_slice(h_bf[b], u, first), up_sb[b, u][:], act[b, u][:], MULT)
+                    if (b, u) in up_sb:
+                        nc.gpsimd.tensor_tensor(hidden_slice(h_bf[b], u, first), up_sb[b, u][:], act[b, u][:], MULT)
             return h_bf
 
         def quantise_rows(k, b, h_bf, codes_tag, scales_tag):
@@ -254,7 +254,7 @@ def tile_list_beam_cache_rewrite_kernel(
                     col = a * N + i * P
                     nc.tensor.matmul_mx(
                         out=acc[:, n, :],
-                        lhsT=late["wc"][:, col : col + P].bitcast(FP8X4),
+                        lhsT=late["wc"][:, (2 * i + a) * P : (2 * i + a + 1) * P].bitcast(FP8X4),
                         lhsT_scale=wc_s[:, col : col + P],
                         rhs=h_q[k, a][:].bitcast(FP8X4),
                         rhs_scale=h_s[k, a][:],
@@ -267,7 +267,10 @@ def tile_list_beam_cache_rewrite_kernel(
             return keep.tile([P, width], F32, name=name, tag=tag or name, align_bytes=64)
 
         def weigh_on_vector(k, i, acc, tag=""):
-            weighed = result_tile(f"weighed{k}{i}", PARTS[k].stop - PARTS[k].start, tag)
+            if (k, i) == (0, 2):
+                weighed = shared.tile([P, HALF], F32, name="weighed02", offset=HIDDEN_ROOM[1, 1], align_bytes=64)
+            else:
+                weighed = result_tile(f"weighed{k}{i}", PARTS[k].stop - PARTS[k].start, tag)
             nc.vector.scalar_tensor_tensor(weighed[:], acc, bias[:, i : i + 1], weight[:, PARTS[k]], ADD, MULT)
             return weighed
 
@@ -304,14 +307,10 @@ def tile_list_beam_cache_rewrite_kernel(
         quantise_rows(0, 0, h_bf[0], "first_bf0", "h_s00")
         for u in range(4):
             product(1, u, h_bf[1], 0)
-        late["wc"] = keep.tile([P, 2 * N], I32, name="wc_p", align_bytes=64)
-        nc.scalar.copy(
-            late["wc"][:].bitcast(U32).rearrange("p (a t g m) -> p a g t m", a=2, t=PACK, m=4),
-            wc_raw[:].bitcast(U32).rearrange("p (a g m t) -> p a g t m", a=2, t=PACK, m=4),
-        )
+        gate(0, 4)
         wd_bf = {
-            0: keep.tile([P, 2 * PASS], BF16, name="wd_bf0", tag="h_bf0", align_bytes=64),
-            1: shared.tile([P, 2 * PASS], BF16, name="wd_bf1", offset=WC_ROOM, align_bytes=64),
+            0: keep.tile([P, 2 * PASS], BF16, name="wd_bf0", tag="h_bf00", align_bytes=64),
+            1: keep.tile([P, 2 * PASS], BF16, name="wd_bf1", align_bytes=64),
         }
         for half in range(2):
             dst = wd_bf[half][:].rearrange("p (t m i) -> p m t i", t=2, i=PACK)
@@ -320,6 +319,14 @@ def tile_list_beam_cache_rewrite_kernel(
                 nc.gpsimd.tensor_scalar(dst, src, 1.0, 0.0, MULT, ADD)
             else:
                 nc.scalar.copy(dst, src)
+        late["wc"] = keep.tile([P, 2 * N], U32, name="wc_p", align_bytes=64)
+        for half in range(2):
+            nc.scalar.copy(
+                late["wc"][:, half * N : (half + 1) * N].rearrange("p (t a g m) -> p a g t m", a=2, t=2, m=4),
+                wc_raw[:].bitcast(U32).rearrange("p (a g m t) -> p a g t m", a=2, t=PACK, m=4)[
+                    :, :, :, 2 * half : 2 * half + 2
+                ],
+            )
         late["wd"] = keep.tile([P, PASS], U32, name="wd_q", align_bytes=64)
 
         def quantise_wd(half):
@@ -327,35 +334,39 @@ def tile_list_beam_cache_rewrite_kernel(
             nc.vector.quantize_mx(out=late["wd"][:, cols].bitcast(FP8X4), scales=w_s[2][:, cols], in_=wd_bf[half][:])
 
         quantise_wd(0)
-        quantise_rows(0, 1, h_bf[1], "h_q01", "h_bf0")
         quantise_wd(1)
+        quantise_rows(0, 1, h_bf[1], "wd_bf1", "h_bf00")
+        pages[2] = shared.tile([P, T2], F32, name="page2", offset=0, align_bytes=64)
+        nc.gpsimd.memset(pages[2][:], 0.0)
+        h_bf = [hidden_tile(1, b, QUARTER) for b in range(2)]
+        product(0, 4, h_bf[0], 4)
 
         first = weigh_on_vector(0, 0, sums(0, (0,), 5)[0])
-        second = weigh_on_gpsimd(0, 1, sums(0, (1,), 6)[1], Y0)
-        third = weigh_on_gpsimd(0, 3, sums(0, (3,), 2)[3], Y1)
-        held = sums(0, (2,), 7)[2]
+        second = weigh_on_gpsimd(0, 1, sums(0, (1,), 2)[1], Y0)
+        third = weigh_on_gpsimd(0, 3, sums(0, (3,), 5)[3], Y1)
+        held = sums(0, (2,), 2)[2]
         scatter(0, 0, first)
         scatter(1, 0, second)
         scatter(3, 0, third)
-        for tile in ((0, 4), (0, 5), (1, 4), (0, 6), (0, 7), (1, 5)):
+        for tile in ((0, 5), (1, 4), (0, 6), (0, 7), (1, 5)):
             stage(*tile)
-        quantise_hidden(1, hidden(1, 4), "act15", "weighed03")
+        quantise_hidden(1, hidden(h_bf, 4), "act15", "weighed03")
 
-        scatter(2, 0, weigh_on_vector(0, 2, held, "h_bf1"))
+        scatter(2, 0, weigh_on_vector(0, 2, held))
         acc = sums(1, (0, 1), 5)
         first = weigh_on_gpsimd(1, 0, acc[0], Y2)
         second = weigh_on_gpsimd(1, 1, acc[1], Y3)
         y_wide = result_tile("y_wide", HALF)
         add_bias(2, sums(1, (2,), 6)[2], y_wide[:, 0:QUARTER])
-        held = sums(1, (3,), 2)[3]
+        held = sums(1, (3,), 7)[3]
         scatter(0, 1, first)
         scatter(1, 1, second)
         for tile in ((1, 6), (1, 7)):
             stage(*tile)
-        quantise_hidden(2, hidden(2, 6), "act17", "weighed11")
+        quantise_hidden(2, hidden([hidden_tile(2, b, QUARTER) for b in range(2)], 6), "act17", "weighed11")
 
-        scatter(3, 1, weigh_on_vector(1, 3, held, "h_bf1"))
-        for rows, bank in (((0,), 5), ((1,), 6), ((3, 2), 7)):
+        scatter(3, 1, weigh_on_vector(1, 3, held, "h_bf21"))
+        for rows, bank in (((0,), 5), ((1,), 6), ((3, 2), 2)):
             acc = sums(2, rows, bank)
             for i in rows:
                 if i == 2:

@@ -28,12 +28,12 @@ PARTS = (slice(0, 512), slice(512, 768), slice(768, 1024))
 BANK = 2048
 ROOM = 2048
 WC_ROOM = 12288
-HIDDEN_ROOM = {(0, 1): 7168, (1, 0): 8192, (2, 0): 8192, (1, 1): 10240}
+HIDDEN_ROOM = {(0, 1): 7168, (1, 0): 8192, (2, 0): 8192, (1, 1): 10240, (2, 1): 10240}
 LATE_ROOM = 40960
 R0, R1 = (WC_ROOM + n * ROOM for n in range(2))
 Y0, Y1, Y2, Y3 = (LATE_ROOM + n * ROOM for n in range(4))
 ACT_ROOM = {(0, 5): R0, (1, 4): R1}
-UP_ROOM = {(0, 5): Y0, (1, 6): Y2, (1, 7): Y3}
+UP_ROOM = {(0, 5): Y0, (1, 7): Y3}
 
 
 def tile_list_beam_cache_rewrite_kernel(
@@ -77,14 +77,15 @@ def tile_list_beam_cache_rewrite_kernel(
         bias = keep.tile([P, PACK], F32, name="bias")
         nc.sync.dma_start(bias[:], bo.rearrange("(p i) -> p i", i=PACK))
 
-        pages = {i: keep.tile([P, T2], F32, name=f"page{i}", align_bytes=64) for i in range(2)}
+        pages = {i: keep.tile([P, T2], F32, name=f"page{i}", align_bytes=64) for i in range(3)}
         nc.gpsimd.memset(wc_s[:].bitcast(I32), 0)
-        nc.gpsimd.memset(pages[1][:, 0:HALF], 0.0)
+        nc.gpsimd.memset(pages[1][:], 0.0)
+        nc.gpsimd.memset(pages[2][:], 0.0)
         warm = keep.tile([P, 2], F32, name="warm")
         nc.vector.memset(warm[:, 0:1], 0.0)
         nc.scalar.activation(warm[:, 1:2], warm[:, 0:1], ACT.Silu)
-        nc.vector.memset(pages[0][:], 0.0)
-        nc.vector.memset(pages[1][:, HALF:], 0.0)
+        nc.vector.memset(pages[0][:, 0 : T2 // 2 - 1], 0.0)
+        nc.vector.memset(pages[0][:, T2 // 2 - 1 :], 0.0)
 
         picked_s = shared.tile([P, LATE_ROOM], U8, name="picked_s", offset=0, align_bytes=64)
         planes = keep.tile([P, S + H], U8, name="planes", align_bytes=64)
@@ -218,12 +219,8 @@ def tile_list_beam_cache_rewrite_kernel(
                 return shared.tile([P, PACK * width], BF16, name=f"h_bf{k}{b}", offset=HIDDEN_ROOM[k, b], align_bytes=64)
             return keep.tile([P, PACK * width], BF16, name=f"h_bf{k}{b}", align_bytes=64)
 
-        def hidden(h_bf, first):
-            for b in range(2):
-                for u in (first, first + 1):
-                    if (b, u) in up_sb:
-                        nc.gpsimd.tensor_tensor(hidden_slice(h_bf[b], u, first), up_sb[b, u][:], act[b, u][:], MULT)
-            return h_bf
+        def multiply(b, u, h_bf, first):
+            nc.gpsimd.tensor_tensor(hidden_slice(h_bf, u, first), up_sb[b, u][:], act[b, u][:], MULT)
 
         def quantise_rows(k, b, h_bf, codes_tag, scales_tag):
             width = PARTS[k].stop - PARTS[k].start
@@ -267,10 +264,7 @@ def tile_list_beam_cache_rewrite_kernel(
             return keep.tile([P, width], F32, name=name, tag=tag or name, align_bytes=64)
 
         def weigh_on_vector(k, i, acc, tag=""):
-            if (k, i) == (0, 2):
-                weighed = shared.tile([P, HALF], F32, name="weighed02", offset=HIDDEN_ROOM[1, 1], align_bytes=64)
-            else:
-                weighed = result_tile(f"weighed{k}{i}", PARTS[k].stop - PARTS[k].start, tag)
+            weighed = result_tile(f"weighed{k}{i}", PARTS[k].stop - PARTS[k].start, tag)
             nc.vector.scalar_tensor_tensor(weighed[:], acc, bias[:, i : i + 1], weight[:, PARTS[k]], ADD, MULT)
             return weighed
 
@@ -336,37 +330,55 @@ def tile_list_beam_cache_rewrite_kernel(
         quantise_wd(0)
         quantise_wd(1)
         quantise_rows(0, 1, h_bf[1], "wd_bf1", "h_bf00")
-        pages[2] = shared.tile([P, T2], F32, name="page2", offset=0, align_bytes=64)
-        nc.gpsimd.memset(pages[2][:], 0.0)
         h_bf = [hidden_tile(1, b, QUARTER) for b in range(2)]
         product(0, 4, h_bf[0], 4)
 
         first = weigh_on_vector(0, 0, sums(0, (0,), 5)[0])
         second = weigh_on_gpsimd(0, 1, sums(0, (1,), 2)[1], Y0)
         third = weigh_on_gpsimd(0, 3, sums(0, (3,), 5)[3], Y1)
-        held = sums(0, (2,), 2)[2]
+        y_held = result_tile("y02", HALF)
+        add_bias(2, sums(0, (2,), 2)[2], y_held[:])
         scatter(0, 0, first)
         scatter(1, 0, second)
         scatter(3, 0, third)
-        for tile in ((0, 5), (1, 4), (0, 6), (0, 7), (1, 5)):
+        for tile in ((0, 5), (1, 4), (0, 6), (0, 7), (1, 6), (1, 5)):
             stage(*tile)
-        quantise_hidden(1, hidden(h_bf, 4), "act15", "weighed03")
+        early_bf = keep.tile([P, PASS], BF16, name="early_bf", align_bytes=64)
+        multiply(0, 5, h_bf[0], 4)
+        multiply(1, 4, h_bf[1], 4)
+        multiply(0, 6, early_bf, 6)
+        multiply(1, 5, h_bf[1], 4)
+        held = result_tile("weighed02", HALF, "up_sb15")
+        nc.gpsimd.tensor_tensor(held[:], y_held[:], weight[:, PARTS[0]], MULT)
+        quantise_hidden(1, h_bf, "act15", "weighed03")
 
-        scatter(2, 0, weigh_on_vector(0, 2, held))
+        scatter(2, 0, held)
         acc = sums(1, (0, 1), 5)
         first = weigh_on_gpsimd(1, 0, acc[0], Y2)
         second = weigh_on_gpsimd(1, 1, acc[1], Y3)
         y_wide = result_tile("y_wide", HALF)
         add_bias(2, sums(1, (2,), 6)[2], y_wide[:, 0:QUARTER])
-        held = sums(1, (3,), 7)[3]
+        y_held = result_tile("y13", QUARTER)
+        add_bias(3, sums(1, (3,), 7)[3], y_held[:])
         scatter(0, 1, first)
         scatter(1, 1, second)
-        for tile in ((1, 6), (1, 7)):
-            stage(*tile)
-        quantise_hidden(2, hidden([hidden_tile(2, b, QUARTER) for b in range(2)], 6), "act17", "weighed11")
+        stage(1, 7)
+        late_bf = hidden_tile(2, 0, JT)
+        h_bf = hidden_tile(2, 1, QUARTER)
+        multiply(0, 7, late_bf, 7)
+        multiply(1, 6, h_bf, 6)
+        multiply(1, 7, h_bf, 6)
+        held = shared.tile([P, QUARTER], F32, name="weighed13", offset=Y3, align_bytes=64)
+        nc.gpsimd.tensor_tensor(held[:], y_held[:], weight[:, PARTS[1]], MULT)
+        h_q[2, 0] = keep.tile([P, QUARTER], U32, name="h_q20", tag="act17", align_bytes=64)
+        h_s[2, 0] = keep.tile([P, QUARTER], U8, name="h_s20", tag="weighed11", align_bytes=64)
+        for n, tile in enumerate((early_bf, late_bf)):
+            cols = slice(n * JT, (n + 1) * JT)
+            nc.vector.quantize_mx(out=h_q[2, 0][:, cols].bitcast(FP8X4), scales=h_s[2, 0][:, cols], in_=tile[:])
+        quantise_rows(2, 1, h_bf, "h_q21", "h_s21")
 
-        scatter(3, 1, weigh_on_vector(1, 3, held, "h_bf21"))
-        for rows, bank in (((0,), 5), ((1,), 6), ((3, 2), 2)):
+        scatter(3, 1, held)
+        for rows, bank in (((0,), 5), ((1,), 6), ((3, 2), 5)):
             acc = sums(2, rows, bank)
             for i in rows:
                 if i == 2:

@@ -21,19 +21,26 @@ P = 128
 PACK = 4
 PASS = P * PACK
 HALF = 512
-JT = 128
 QUARTER = 256
+JT = 128
 WC_ROW = 5
+
 PARTS = (slice(0, 512), slice(512, 768), slice(768, 1024))
+
 BANK = 2048
 ROOM = 2048
+
+WB_ROOM = {2: 0, 3: 28672}
+WC_SCALE_ROOM = 4096
 WC_ROOM = 12288
-HIDDEN_ROOM = {(0, 1): 7168, (1, 0): 8192, (2, 0): 8192, (1, 1): 10240, (2, 1): 10240}
+WD_ROOM = 16384
+WEIGHT_ROOM = 24576
+PAGE_ROOM = 32768
 LATE_ROOM = 40960
-R0, R1 = (WC_ROOM + n * ROOM for n in range(2))
-Y0, Y1, Y2, Y3 = (LATE_ROOM + n * ROOM for n in range(4))
-ACT_ROOM = {(0, 5): R0, (1, 4): R1}
-UP_ROOM = {(0, 5): Y0, (1, 7): Y3}
+HIDDEN_ROOM = {(0, 1): 7168, (1, 0): 8192, (2, 0): 8192, (1, 1): 10240, (2, 1): 10240}
+RESULT_ROOM = {key: LATE_ROOM + n * ROOM for n, key in enumerate(((0, 1), (0, 3), (1, 0), (1, 1)))}
+ACT_ROOM = {(0, 5): WC_ROOM, (1, 4): WC_ROOM + ROOM}
+UP_ROOM = {(0, 5): RESULT_ROOM[0, 1], (1, 7): RESULT_ROOM[1, 0]}
 
 
 def tile_list_beam_cache_rewrite_kernel(
@@ -52,7 +59,6 @@ def tile_list_beam_cache_rewrite_kernel(
         ws_raw = keep.tile([P, H], U8, name="ws_raw", align_bytes=64)
         wa_raw = keep.tile([P, 2 * H], U8, name="wa_raw", align_bytes=64)
         tab_w = keep.tile([P, T], I32, name="tab_w", align_bytes=64)
-        wc_s = keep.tile([P, H], U8, name="wc_s", align_bytes=64)
         wb_raw = {}
         wb_rows = wb.rearrange("(p i) c -> p i c", i=PACK)
 
@@ -78,7 +84,6 @@ def tile_list_beam_cache_rewrite_kernel(
         nc.sync.dma_start(bias[:], bo.rearrange("(p i) -> p i", i=PACK))
 
         pages = {i: keep.tile([P, T2], F32, name=f"page{i}", align_bytes=64) for i in range(3)}
-        nc.gpsimd.memset(wc_s[:].bitcast(I32), 0)
         nc.gpsimd.memset(pages[1][:], 0.0)
         nc.gpsimd.memset(pages[2][:], 0.0)
         warm = keep.tile([P, 2], F32, name="warm")
@@ -97,14 +102,16 @@ def tile_list_beam_cache_rewrite_kernel(
         nc.vector.tensor_copy(planes[:, 0:S].bitcast(I32), picked_s[:, 0:S].bitcast(I32))
         for r in range(1, 4):
             nc.sync.dma_start(planes[r:P:32, :].bitcast(I32), planes[8 * r : P : 32, :].bitcast(I32))
-        for n, offset in ((2, 0), (3, 28672)):
+        for n, offset in WB_ROOM.items():
             wb_raw[n] = shared.tile([P, PACK, QUARTER], F32, name=f"wb_raw{n}", offset=offset, align_bytes=64)
             nc.sync.dma_start(wb_raw[n][:], wb_rows[:, :, n * QUARTER : (n + 1) * QUARTER])
+        wc_s = shared.tile([P, H], U8, name="wc_s", offset=WC_SCALE_ROOM, align_bytes=64)
+        nc.gpsimd.memset(wc_s[:].bitcast(I32), 0)
         for r in range(4):
             nc.sync.dma_start(wc_s[r:P:32, :].bitcast(I32), planes[WC_ROW + 8 * r : P : 32, S:].bitcast(I32))
-        wd_raw = shared.tile([P, PACK, PASS], F32, name="wd_raw", offset=16384, align_bytes=64)
+        wd_raw = shared.tile([P, PACK, PASS], F32, name="wd_raw", offset=WD_ROOM, align_bytes=64)
         nc.sync.dma_start(wd_raw[:], wd.rearrange("(p i) c -> p i c", i=PACK))
-        weight = shared.tile([P, S], F32, name="weight", offset=24576, align_bytes=64)
+        weight = shared.tile([P, S], F32, name="weight", offset=WEIGHT_ROOM, align_bytes=64)
         nc.sync.dma_start(weight[:, 0:HALF], wgo[:, 0:HALF])
         wc_raw = shared.tile([P, 2 * N], I32, name="wc_raw", offset=WC_ROOM, align_bytes=64)
         nc.sync.dma_start(
@@ -112,7 +119,7 @@ def tile_list_beam_cache_rewrite_kernel(
             wc_words.rearrange("a p c i -> p a (c i)").bitcast(I32),
         )
         nc.sync.dma_start(weight[:, HALF:], wgo[:, HALF:])
-        pages[3] = shared.tile([P, T2], F32, name="page3", offset=32768, align_bytes=64)
+        pages[3] = shared.tile([P, T2], F32, name="page3", offset=PAGE_ROOM, align_bytes=64)
         nc.gpsimd.memset(pages[3][:], 0.0)
         v_s = planes[:, 0:S]
         wa_s = planes[:, S:]
@@ -122,8 +129,9 @@ def tile_list_beam_cache_rewrite_kernel(
             wa_p[:].bitcast(U16).rearrange("p (b t g m) -> p b g t m", b=2, t=PACK, m=8),
             wa_raw[:].bitcast(U16).rearrange("p (b g m t) -> p b g t m", b=2, t=PACK, m=8),
         )
-        w_q = [keep.tile([P, PASS], U32, name=f"w_q{n}", align_bytes=64) for n in range(2)]
-        w_s = [keep.tile([P, PASS], U8, name=f"w_s{n}", align_bytes=64) for n in range(3)]
+        wb_q = [keep.tile([P, PASS], U32, name=f"wb_q{b}", align_bytes=64) for b in range(2)]
+        wb_s = [keep.tile([P, PASS], U8, name=f"wb_s{b}", align_bytes=64) for b in range(2)]
+        wd_s = keep.tile([P, PASS], U8, name="wd_s", align_bytes=64)
         v_w = {}
 
         def gather_words(k, tag):
@@ -148,7 +156,7 @@ def tile_list_beam_cache_rewrite_kernel(
                     nc.scalar.copy(dst, src)
         for pair in (1, 0):
             cols = slice(pair * 2 * P, (pair + 1) * 2 * P)
-            nc.vector.quantize_mx(out=w_q[0][:, cols].bitcast(FP8X4), scales=w_s[0][:, cols], in_=first_bf[pair][:])
+            nc.vector.quantize_mx(out=wb_q[0][:, cols].bitcast(FP8X4), scales=wb_s[0][:, cols], in_=first_bf[pair][:])
 
         gather_words(2, "first_bf1")
         second_bf = keep.tile([P, PACK * PASS], BF16, name="second_bf", tag="first_bf0", align_bytes=64)
@@ -158,9 +166,9 @@ def tile_list_beam_cache_rewrite_kernel(
             nc.gpsimd.tensor_scalar(dst, src, 1.0, 0.0, MULT, ADD)
 
         act = {}
+        up_sb = {}
         h_q = {}
         h_s = {}
-        late = {}
 
         def gate(b, u):
             js = slice(u * JT, (u + 1) * JT)
@@ -171,7 +179,7 @@ def tile_list_beam_cache_rewrite_kernel(
                     out=bank[:, t, :],
                     lhsT=wa_p[:, 2 * col : 2 * (col + P)].bitcast(FP4X4),
                     lhsT_scale=wa_s[:, col : col + P],
-                    rhs=words(js.start, js.stop - js.start),
+                    rhs=words(js.start, JT),
                     rhs_scale=v_s[:, js],
                     start=True,
                     stop=True,
@@ -182,8 +190,6 @@ def tile_list_beam_cache_rewrite_kernel(
                 act[b, u] = keep.tile([P, JT, PACK], F32, name=f"act{b}{u}", align_bytes=64)
             nc.scalar.activation(act[b, u][:], bank[:].rearrange("p t j -> p j t"), ACT.Silu)
 
-        up_sb = {}
-
         def up_tile(b, u):
             js = slice(u * JT, (u + 1) * JT)
             bank = 2 + u % 3 if u < 4 else 4 - u % 2
@@ -191,8 +197,8 @@ def tile_list_beam_cache_rewrite_kernel(
             for t in (2, 3, 0, 1):
                 nc.tensor.matmul_mx(
                     out=up[:, t, :],
-                    lhsT=w_q[b][:, t * P : (t + 1) * P].bitcast(FP8X4),
-                    lhsT_scale=w_s[b][:, t * P : (t + 1) * P],
+                    lhsT=wb_q[b][:, t * P : (t + 1) * P].bitcast(FP8X4),
+                    lhsT_scale=wb_s[b][:, t * P : (t + 1) * P],
                     rhs=words(js.start, JT),
                     rhs_scale=v_s[:, js],
                     start=True,
@@ -203,7 +209,7 @@ def tile_list_beam_cache_rewrite_kernel(
         def hidden_slice(h_bf, u, first):
             return h_bf[:, (u - first) * PASS : (u - first + 1) * PASS].rearrange("p (j t) -> p j t", t=PACK)
 
-        def product(b, u, h_bf, first):
+        def multiply_on_vector(b, u, h_bf, first):
             nc.vector.tensor_tensor(hidden_slice(h_bf, u, first), up_tile(b, u), act[b, u][:], MULT)
 
         def stage(b, u):
@@ -219,7 +225,7 @@ def tile_list_beam_cache_rewrite_kernel(
                 return shared.tile([P, PACK * width], BF16, name=f"h_bf{k}{b}", offset=HIDDEN_ROOM[k, b], align_bytes=64)
             return keep.tile([P, PACK * width], BF16, name=f"h_bf{k}{b}", align_bytes=64)
 
-        def multiply(b, u, h_bf, first):
+        def multiply_on_gpsimd(b, u, h_bf, first):
             nc.gpsimd.tensor_tensor(hidden_slice(h_bf, u, first), up_sb[b, u][:], act[b, u][:], MULT)
 
         def quantise_rows(k, b, h_bf, codes_tag, scales_tag):
@@ -228,10 +234,6 @@ def tile_list_beam_cache_rewrite_kernel(
             h_s[k, b] = keep.tile([P, width], U8, name=f"h_s{k}{b}", tag=scales_tag, align_bytes=64)
             nc.vector.quantize_mx(out=h_q[k, b][:].bitcast(FP8X4), scales=h_s[k, b][:], in_=h_bf[:])
 
-        def quantise_hidden(k, h_bf, codes_tag, scales_tag):
-            quantise_rows(k, 0, h_bf[0], codes_tag, scales_tag)
-            quantise_rows(k, 1, h_bf[1], f"h_q{k}1", f"h_s{k}1")
-
         def sums(k, rows, bank):
             js = PARTS[k]
             width = js.stop - js.start
@@ -239,8 +241,8 @@ def tile_list_beam_cache_rewrite_kernel(
             for n, i in enumerate(rows):
                 nc.tensor.matmul_mx(
                     out=acc[:, n, :],
-                    lhsT=late["wd"][:, i * P : (i + 1) * P].bitcast(FP8X4),
-                    lhsT_scale=w_s[2][:, i * P : (i + 1) * P],
+                    lhsT=wd_q[:, i * P : (i + 1) * P].bitcast(FP8X4),
+                    lhsT_scale=wd_s[:, i * P : (i + 1) * P],
                     rhs=words(js.start, width),
                     rhs_scale=v_s[:, js],
                     start=(n == 0),
@@ -251,7 +253,7 @@ def tile_list_beam_cache_rewrite_kernel(
                     col = a * N + i * P
                     nc.tensor.matmul_mx(
                         out=acc[:, n, :],
-                        lhsT=late["wc"][:, (2 * i + a) * P : (2 * i + a + 1) * P].bitcast(FP8X4),
+                        lhsT=wc_p[:, (2 * i + a) * P : (2 * i + a + 1) * P].bitcast(FP8X4),
                         lhsT_scale=wc_s[:, col : col + P],
                         rhs=h_q[k, a][:].bitcast(FP8X4),
                         rhs_scale=h_s[k, a][:],
@@ -263,17 +265,12 @@ def tile_list_beam_cache_rewrite_kernel(
         def result_tile(name, width, tag=""):
             return keep.tile([P, width], F32, name=name, tag=tag or name, align_bytes=64)
 
-        def weigh_on_vector(k, i, acc, tag=""):
-            weighed = result_tile(f"weighed{k}{i}", PARTS[k].stop - PARTS[k].start, tag)
-            nc.vector.scalar_tensor_tensor(weighed[:], acc, bias[:, i : i + 1], weight[:, PARTS[k]], ADD, MULT)
-            return weighed
-
         def add_bias(i, acc, dst):
             nc.scalar.activation(dst, acc, ACT.Identity, bias=bias[:, i : i + 1])
 
-        def weigh_on_gpsimd(k, i, acc, room):
+        def weigh_on_gpsimd(k, i, acc):
             width = PARTS[k].stop - PARTS[k].start
-            y = shared.tile([P, width], F32, name=f"y{k}{i}", offset=room, align_bytes=64)
+            y = shared.tile([P, width], F32, name=f"y{k}{i}", offset=RESULT_ROOM[k, i], align_bytes=64)
             add_bias(i, acc, y[:])
             weighed = result_tile(f"weighed{k}{i}", width)
             nc.gpsimd.tensor_tensor(weighed[:], y[:], weight[:, PARTS[k]], MULT)
@@ -285,22 +282,19 @@ def tile_list_beam_cache_rewrite_kernel(
         def scatter(i, k, weighed):
             nc.vector.tensor_copy(window(i, PARTS[k]), weighed[:])
 
-        out_rows = out.rearrange("(p i) t -> p i t", i=PACK)
-
-        def scatter_last(i, js, y):
+        def weigh_and_scatter(i, js, y):
             nc.vector.tensor_tensor(window(i, js), y[:], weight[:, js], MULT)
-            nc.sync.dma_start(out_rows[:, i, :], pages[i][:])
 
         h_bf = [hidden_tile(0, b, HALF) for b in range(2)]
         for u in range(4):
             gate(0, u)
         for u in range(4):
-            product(0, u, h_bf[0], 0)
+            multiply_on_vector(0, u, h_bf[0], 0)
             gate(1, u)
-        nc.vector.quantize_mx(out=w_q[1][:].bitcast(FP8X4), scales=w_s[1][:], in_=second_bf[:])
+        nc.vector.quantize_mx(out=wb_q[1][:].bitcast(FP8X4), scales=wb_s[1][:], in_=second_bf[:])
         quantise_rows(0, 0, h_bf[0], "first_bf0", "h_s00")
         for u in range(4):
-            product(1, u, h_bf[1], 0)
+            multiply_on_vector(1, u, h_bf[1], 0)
         gate(0, 4)
         wd_bf = {
             0: keep.tile([P, 2 * PASS], BF16, name="wd_bf0", tag="h_bf00", align_bytes=64),
@@ -313,29 +307,28 @@ def tile_list_beam_cache_rewrite_kernel(
                 nc.gpsimd.tensor_scalar(dst, src, 1.0, 0.0, MULT, ADD)
             else:
                 nc.scalar.copy(dst, src)
-        late["wc"] = keep.tile([P, 2 * N], U32, name="wc_p", align_bytes=64)
+        wc_p = keep.tile([P, 2 * N], U32, name="wc_p", align_bytes=64)
         for half in range(2):
             nc.scalar.copy(
-                late["wc"][:, half * N : (half + 1) * N].rearrange("p (t a g m) -> p a g t m", a=2, t=2, m=4),
+                wc_p[:, half * N : (half + 1) * N].rearrange("p (t a g m) -> p a g t m", a=2, t=2, m=4),
                 wc_raw[:].bitcast(U32).rearrange("p (a g m t) -> p a g t m", a=2, t=PACK, m=4)[
                     :, :, :, 2 * half : 2 * half + 2
                 ],
             )
-        late["wd"] = keep.tile([P, PASS], U32, name="wd_q", align_bytes=64)
-
-        def quantise_wd(half):
+        wd_q = keep.tile([P, PASS], U32, name="wd_q", align_bytes=64)
+        for half in range(2):
             cols = slice(half * 2 * P, (half + 1) * 2 * P)
-            nc.vector.quantize_mx(out=late["wd"][:, cols].bitcast(FP8X4), scales=w_s[2][:, cols], in_=wd_bf[half][:])
-
-        quantise_wd(0)
-        quantise_wd(1)
+            nc.vector.quantize_mx(out=wd_q[:, cols].bitcast(FP8X4), scales=wd_s[:, cols], in_=wd_bf[half][:])
         quantise_rows(0, 1, h_bf[1], "wd_bf1", "h_bf00")
         h_bf = [hidden_tile(1, b, QUARTER) for b in range(2)]
-        product(0, 4, h_bf[0], 4)
+        multiply_on_vector(0, 4, h_bf[0], 4)
 
-        first = weigh_on_vector(0, 0, sums(0, (0,), 5)[0])
-        second = weigh_on_gpsimd(0, 1, sums(0, (1,), 2)[1], Y0)
-        third = weigh_on_gpsimd(0, 3, sums(0, (3,), 5)[3], Y1)
+        first = result_tile("weighed00", HALF)
+        nc.vector.scalar_tensor_tensor(
+            first[:], sums(0, (0,), 5)[0], bias[:, 0:1], weight[:, PARTS[0]], ADD, MULT
+        )
+        second = weigh_on_gpsimd(0, 1, sums(0, (1,), 2)[1])
+        third = weigh_on_gpsimd(0, 3, sums(0, (3,), 5)[3])
         y_held = result_tile("y02", HALF)
         add_bias(2, sums(0, (2,), 2)[2], y_held[:])
         scatter(0, 0, first)
@@ -344,47 +337,49 @@ def tile_list_beam_cache_rewrite_kernel(
         for tile in ((0, 5), (1, 4), (0, 6), (0, 7), (1, 6), (1, 5)):
             stage(*tile)
         early_bf = keep.tile([P, PASS], BF16, name="early_bf", align_bytes=64)
-        multiply(0, 5, h_bf[0], 4)
-        multiply(1, 4, h_bf[1], 4)
-        multiply(0, 6, early_bf, 6)
-        multiply(1, 5, h_bf[1], 4)
+        multiply_on_gpsimd(0, 5, h_bf[0], 4)
+        multiply_on_gpsimd(1, 4, h_bf[1], 4)
+        multiply_on_gpsimd(0, 6, early_bf, 6)
+        multiply_on_gpsimd(1, 5, h_bf[1], 4)
         held = result_tile("weighed02", HALF, "up_sb15")
         nc.gpsimd.tensor_tensor(held[:], y_held[:], weight[:, PARTS[0]], MULT)
-        quantise_hidden(1, h_bf, "act15", "weighed03")
+        quantise_rows(1, 0, h_bf[0], "act15", "weighed03")
+        quantise_rows(1, 1, h_bf[1], "h_q11", "h_s11")
 
         scatter(2, 0, held)
         acc = sums(1, (0, 1), 5)
-        first = weigh_on_gpsimd(1, 0, acc[0], Y2)
-        second = weigh_on_gpsimd(1, 1, acc[1], Y3)
+        first = weigh_on_gpsimd(1, 0, acc[0])
+        second = weigh_on_gpsimd(1, 1, acc[1])
         y_wide = result_tile("y_wide", HALF)
         add_bias(2, sums(1, (2,), 6)[2], y_wide[:, 0:QUARTER])
-        y_held = result_tile("y13", QUARTER)
-        add_bias(3, sums(1, (3,), 7)[3], y_held[:])
+        acc_held = sums(1, (3,), 7)[3]
         scatter(0, 1, first)
         scatter(1, 1, second)
         stage(1, 7)
         late_bf = hidden_tile(2, 0, JT)
-        h_bf = hidden_tile(2, 1, QUARTER)
-        multiply(0, 7, late_bf, 7)
-        multiply(1, 6, h_bf, 6)
-        multiply(1, 7, h_bf, 6)
-        held = shared.tile([P, QUARTER], F32, name="weighed13", offset=Y3, align_bytes=64)
-        nc.gpsimd.tensor_tensor(held[:], y_held[:], weight[:, PARTS[1]], MULT)
+        last_bf = hidden_tile(2, 1, QUARTER)
+        multiply_on_gpsimd(0, 7, late_bf, 7)
+        multiply_on_gpsimd(1, 6, last_bf, 6)
+        multiply_on_gpsimd(1, 7, last_bf, 6)
+        y_cover = shared.tile([P, QUARTER], F32, name="y13", offset=UP_ROOM[1, 7], align_bytes=64)
+        add_bias(3, acc_held, y_cover[:])
         h_q[2, 0] = keep.tile([P, QUARTER], U32, name="h_q20", tag="act17", align_bytes=64)
         h_s[2, 0] = keep.tile([P, QUARTER], U8, name="h_s20", tag="weighed11", align_bytes=64)
         for n, tile in enumerate((early_bf, late_bf)):
             cols = slice(n * JT, (n + 1) * JT)
             nc.vector.quantize_mx(out=h_q[2, 0][:, cols].bitcast(FP8X4), scales=h_s[2, 0][:, cols], in_=tile[:])
-        quantise_rows(2, 1, h_bf, "h_q21", "h_s21")
+        quantise_rows(2, 1, last_bf, "h_q21", "h_s21")
+        weigh_and_scatter(3, PARTS[1], y_cover)
 
-        scatter(3, 1, held)
+        out_rows = out.rearrange("(p i) t -> p i t", i=PACK)
         for rows, bank in (((0,), 5), ((1,), 6), ((3, 2), 5)):
             acc = sums(2, rows, bank)
             for i in rows:
                 if i == 2:
                     add_bias(i, acc[i], y_wide[:, QUARTER:])
-                    scatter_last(i, slice(HALF, S), y_wide)
+                    weigh_and_scatter(i, slice(HALF, S), y_wide)
                 else:
                     y = result_tile(f"y2{i}", QUARTER)
                     add_bias(i, acc[i], y[:])
-                    scatter_last(i, PARTS[2], y)
+                    weigh_and_scatter(i, PARTS[2], y)
+                nc.sync.dma_start(out_rows[:, i, :], pages[i][:])

@@ -20,27 +20,33 @@ ADD = mybir.AluOpType.add
 P = 128
 PACK = 4
 PASS = P * PACK
-HALF = 512
 QUARTER = 256
 JT = 128
-WC_ROW = 5
-
-PARTS = (slice(0, 512), slice(512, 768), slice(768, 1024))
-
+WC_ROW = 4
 BANK = 2048
-ROOM = 2048
 
-WB_ROOM = {2: 0, 3: 28672}
-WC_SCALE_ROOM = 4096
-WC_ROOM = 12288
-WD_ROOM = 16384
-WEIGHT_ROOM = 24576
-PAGE_ROOM = 32768
-LATE_ROOM = 40960
-HIDDEN_ROOM = {(0, 1): 7168, (1, 0): 8192, (2, 0): 8192, (1, 1): 10240, (2, 1): 10240}
-RESULT_ROOM = {key: LATE_ROOM + n * ROOM for n, key in enumerate(((0, 1), (0, 3), (1, 0), (1, 1)))}
-ACT_ROOM = {(0, 5): WC_ROOM, (1, 4): WC_ROOM + ROOM}
-UP_ROOM = {(0, 5): RESULT_ROOM[0, 1], (1, 7): RESULT_ROOM[1, 0]}
+FIRST, FILL, SECOND, LAST = slice(0, 384), slice(384, 512), slice(512, 768), slice(768, 1024)
+WORD_RUNS = (slice(0, 512), SECOND, LAST)
+CLEAR_CUT = 1728
+HELD = 640
+
+ROOM_SIZES = (
+    ("wb2", 4096),
+    ("wb3", 4096),
+    ("wc_s", 1024),
+    ("wd", 8192),
+    ("wc", 4096),
+    ("weight", 4096),
+    ("page3", 8192),
+    ("wb1", 4096),
+    ("wb_bf", 4096),
+    ("first_h", 4096),
+    ("late_h", 4096),
+    ("up", 2048),
+    ("y02", 2048),
+    ("act15", 2048),
+)
+ROOM = {name: sum(size for other, size in ROOM_SIZES[:n]) for n, (name, own) in enumerate(ROOM_SIZES)}
 
 
 def tile_list_beam_cache_rewrite_kernel(
@@ -53,47 +59,51 @@ def tile_list_beam_cache_rewrite_kernel(
         shared = ctx.enter_context(tc.tile_pool(name="shared", bufs=1))
         psum = ctx.enter_context(tc.psum_pool(name="psum", bufs=1))
 
+        def own(name, shape, dtype):
+            return keep.tile(shape, dtype, name=name, align_bytes=64)
+
+        def tenant(name, shape, dtype, room, at=0):
+            return shared.tile(shape, dtype, name=name, offset=ROOM[room] + at, align_bytes=64)
+
         pick = lists.tile([P, S // 16], U16, name="pick")
         put = lists.tile([P, S // 16], U16, name="put")
-        tab_s = keep.tile([P, T], U8, name="tab_s", align_bytes=64)
-        ws_raw = keep.tile([P, H], U8, name="ws_raw", align_bytes=64)
-        wa_raw = keep.tile([P, 2 * H], U8, name="wa_raw", align_bytes=64)
-        tab_w = keep.tile([P, T], I32, name="tab_w", align_bytes=64)
-        wb_raw = {}
+        tab_s = own("tab_s", [P, T], U8)
+        ws_raw = own("ws_raw", [P, H], U8)
+        wa_raw = own("wa_raw", [P, 2 * H], U8)
+        tab_w = own("tab_w", [P, T], I32)
         wb_rows = wb.rearrange("(p i) c -> p i c", i=PACK)
 
+        nc.gpsimd.memset(ws_raw[:].bitcast(I32), 0)
         nc.sync.dma_start(pick[:], offs)
         nc.sync.dma_start(
             tab_s[:].bitcast(I32), tab_scales[0].bitcast(I32).unsqueeze(1).to_broadcast([16, 8, T // 4])
         )
+        nc.sync.dma_start(ws_raw[0:P:8, :].bitcast(I32), wa_scales[0].bitcast(I32))
         nc.sync.dma_start(
-            ws_raw[0:P:2, :].bitcast(I32), wa_scales[0].bitcast(I32).unsqueeze(1).to_broadcast([16, 4, H // 4])
+            ws_raw[WC_ROW:P:8, :].bitcast(I32).rearrange("q (a c) -> q a c", a=2),
+            wc_scales.bitcast(I32).rearrange("a q c -> q a c"),
         )
-        for a in range(2):
-            nc.sync.dma_start(
-                ws_raw[1:P:2, a * N : (a + 1) * N].bitcast(I32),
-                wc_scales[a].bitcast(I32).unsqueeze(1).to_broadcast([16, 4, N // 4]),
-            )
         nc.sync.dma_start(wa_raw[:].bitcast(I32), wa_words[0].bitcast(I32))
         nc.sync.dma_start(tab_w[:], tab_words[0].rearrange("p t i -> p (t i)").bitcast(I32))
+        wb_raw = {0: own("wb_raw0", [P, PACK, QUARTER], F32), 1: tenant("wb_raw1", [P, PACK, QUARTER], F32, "wb1")}
         for n in range(2):
-            wb_raw[n] = keep.tile([P, PACK, QUARTER], F32, name=f"wb_raw{n}", align_bytes=64)
             nc.sync.dma_start(wb_raw[n][:], wb_rows[:, :, n * QUARTER : (n + 1) * QUARTER])
         nc.sync.dma_start(put[:], offs2)
-        bias = keep.tile([P, PACK], F32, name="bias")
+        bias = own("bias", [P, PACK], F32)
         nc.sync.dma_start(bias[:], bo.rearrange("(p i) -> p i", i=PACK))
 
-        pages = {i: keep.tile([P, T2], F32, name=f"page{i}", align_bytes=64) for i in range(3)}
+        pages = {i: own(f"page{i}", [P, T2], F32) for i in range(3)}
         nc.gpsimd.memset(pages[1][:], 0.0)
         nc.gpsimd.memset(pages[2][:], 0.0)
-        warm = keep.tile([P, 2], F32, name="warm")
+        nc.gpsimd.memset(pages[0][:, CLEAR_CUT:], 0.0)
+        warm = own("warm", [P, 2], F32)
         nc.vector.memset(warm[:, 0:1], 0.0)
         nc.scalar.activation(warm[:, 1:2], warm[:, 0:1], ACT.Silu)
-        nc.vector.memset(pages[0][:, 0 : T2 // 2 - 1], 0.0)
-        nc.vector.memset(pages[0][:, T2 // 2 - 1 :], 0.0)
+        nc.vector.memset(pages[0][:, 0 : CLEAR_CUT // 2 - 1], 0.0)
+        nc.vector.memset(pages[0][:, CLEAR_CUT // 2 - 1 : CLEAR_CUT], 0.0)
 
-        picked_s = shared.tile([P, LATE_ROOM], U8, name="picked_s", offset=0, align_bytes=64)
-        planes = keep.tile([P, S + H], U8, name="planes", align_bytes=64)
+        picked_s = tenant("picked_s", [P, ROOM["wb1"]], U8, "wb2")
+        planes = own("planes", [P, S + H], U8)
         nc.vector.tensor_copy(picked_s[:, 0:S], tab_s[:].indirect(pick[:]))
         nc.vector.tensor_copy(
             planes[:, S:].rearrange("p (b t g m) -> p b g t m", b=2, t=PACK, m=16),
@@ -102,284 +112,294 @@ def tile_list_beam_cache_rewrite_kernel(
         nc.vector.tensor_copy(planes[:, 0:S].bitcast(I32), picked_s[:, 0:S].bitcast(I32))
         for r in range(1, 4):
             nc.sync.dma_start(planes[r:P:32, :].bitcast(I32), planes[8 * r : P : 32, :].bitcast(I32))
-        for n, offset in WB_ROOM.items():
-            wb_raw[n] = shared.tile([P, PACK, QUARTER], F32, name=f"wb_raw{n}", offset=offset, align_bytes=64)
+        for n in (2, 3):
+            wb_raw[n] = tenant(f"wb_raw{n}", [P, PACK, QUARTER], F32, f"wb{n}")
             nc.sync.dma_start(wb_raw[n][:], wb_rows[:, :, n * QUARTER : (n + 1) * QUARTER])
-        wc_s = shared.tile([P, H], U8, name="wc_s", offset=WC_SCALE_ROOM, align_bytes=64)
+        wc_s = tenant("wc_s", [P, H], U8, "wc_s")
         nc.gpsimd.memset(wc_s[:].bitcast(I32), 0)
         for r in range(4):
             nc.sync.dma_start(wc_s[r:P:32, :].bitcast(I32), planes[WC_ROW + 8 * r : P : 32, S:].bitcast(I32))
-        wd_raw = shared.tile([P, PACK, PASS], F32, name="wd_raw", offset=WD_ROOM, align_bytes=64)
+        wd_raw = tenant("wd_raw", [P, PACK, PASS], F32, "wd")
         nc.sync.dma_start(wd_raw[:], wd.rearrange("(p i) c -> p i c", i=PACK))
-        weight = shared.tile([P, S], F32, name="weight", offset=WEIGHT_ROOM, align_bytes=64)
-        nc.sync.dma_start(weight[:, 0:HALF], wgo[:, 0:HALF])
-        wc_raw = shared.tile([P, 2 * N], I32, name="wc_raw", offset=WC_ROOM, align_bytes=64)
+        wc_raw = tenant("wc_raw", [P, 2 * N], I32, "wc")
         nc.sync.dma_start(
             wc_raw[:].rearrange("p (a c) -> p a c", a=2),
             wc_words.rearrange("a p c i -> p a (c i)").bitcast(I32),
         )
-        nc.sync.dma_start(weight[:, HALF:], wgo[:, HALF:])
-        pages[3] = shared.tile([P, T2], F32, name="page3", offset=PAGE_ROOM, align_bytes=64)
+        weight = tenant("weight", [P, S], F32, "weight")
+        nc.sync.dma_start(weight[:], wgo)
+        pages[3] = tenant("page3", [P, T2], F32, "page3")
         nc.gpsimd.memset(pages[3][:], 0.0)
         v_s = planes[:, 0:S]
         wa_s = planes[:, S:]
 
-        wa_p = keep.tile([P, 2 * H], U8, name="wa_p", align_bytes=64)
+        wa_p = own("wa_p", [P, 2 * H], U8)
         nc.scalar.copy(
             wa_p[:].bitcast(U16).rearrange("p (b t g m) -> p b g t m", b=2, t=PACK, m=8),
             wa_raw[:].bitcast(U16).rearrange("p (b g m t) -> p b g t m", b=2, t=PACK, m=8),
         )
-        wb_q = [keep.tile([P, PASS], U32, name=f"wb_q{b}", align_bytes=64) for b in range(2)]
-        wb_s = [keep.tile([P, PASS], U8, name=f"wb_s{b}", align_bytes=64) for b in range(2)]
-        wd_s = keep.tile([P, PASS], U8, name="wd_s", align_bytes=64)
+        wb_q = [own(f"wb_q{b}", [P, PASS], U32) for b in range(2)]
+        wb_s = [own(f"wb_s{b}", [P, PASS], U8) for b in range(2)]
         v_w = {}
 
-        def gather_words(k, tag):
-            js = PARTS[k]
-            v_w[k] = keep.tile([P, js.stop - js.start], U32, name=f"v_w{k}", tag=tag, align_bytes=64)
-            nc.vector.tensor_copy(v_w[k][:], tab_w[:].bitcast(U32).indirect(pick[:, js.start // 16 : js.stop // 16]))
+        def gather_words(k, tile):
+            js = WORD_RUNS[k]
+            v_w[k] = tile
+            nc.vector.tensor_copy(tile[:], tab_w[:].bitcast(U32).indirect(pick[:, js.start // 16 : js.stop // 16]))
 
-        def words(first, width):
-            k = max(n for n in range(len(PARTS)) if PARTS[n].start <= first)
-            return v_w[k][:, first - PARTS[k].start : first - PARTS[k].start + width].bitcast(FP8X4)
+        def words(js):
+            k = max(n for n in range(len(WORD_RUNS)) if WORD_RUNS[n].start <= js.start)
+            first = WORD_RUNS[k].start
+            return v_w[k][:, js.start - first : js.stop - first].bitcast(FP8X4)
 
-        gather_words(0, "v_w0")
-        gather_words(1, "v_w1")
-        first_bf = [keep.tile([P, 2 * PASS], BF16, name=f"first_bf{pair}", align_bytes=64) for pair in range(2)]
+        def quantise(codes, scales, values):
+            nc.vector.quantize_mx(out=codes.bitcast(FP8X4), scales=scales, in_=values)
+
+        gather_words(0, own("v_w0", [P, 512], U32))
+        gather_words(1, own("v_w1", [P, QUARTER], U32))
+        first_bf = [tenant(f"first_bf{pair}", [P, 2 * PASS], BF16, "wb_bf", pair * 2048) for pair in range(2)]
         for n in range(2):
             for pair in range(2):
                 dst = first_bf[pair][:].rearrange("p (t m i) -> p m t i", t=2, i=PACK)[:, n * 64 : (n + 1) * 64]
                 src = wb_raw[n][:].rearrange("p i (m t) -> p m t i", t=PACK)[:, :, 2 * pair : 2 * pair + 2]
-                if (n, pair) == (1, 1):
+                if (n, pair) == (1, 0):
                     nc.vector.tensor_copy(dst, src)
                 else:
                     nc.scalar.copy(dst, src)
         for pair in (1, 0):
             cols = slice(pair * 2 * P, (pair + 1) * 2 * P)
-            nc.vector.quantize_mx(out=wb_q[0][:, cols].bitcast(FP8X4), scales=wb_s[0][:, cols], in_=first_bf[pair][:])
-
-        gather_words(2, "first_bf1")
-        second_bf = keep.tile([P, PACK * PASS], BF16, name="second_bf", tag="first_bf0", align_bytes=64)
+            quantise(wb_q[0][:, cols], wb_s[0][:, cols], first_bf[pair][:])
+        gather_words(2, tenant("v_w2", [P, QUARTER], U32, "wb1"))
+        second_bf = tenant("second_bf", [P, PACK * PASS], BF16, "wb_bf")
         for n in (2, 3):
             dst = second_bf[:].rearrange("p (t m i) -> p m t i", t=PACK, i=PACK)[:, (n - 2) * 64 : (n - 1) * 64]
             src = wb_raw[n][:].rearrange("p i (m t) -> p m t i", t=PACK)
             nc.gpsimd.tensor_scalar(dst, src, 1.0, 0.0, MULT, ADD)
 
         act = {}
-        up_sb = {}
-        h_q = {}
-        h_s = {}
 
-        def gate(b, u):
+        def gate(b, u, bank, tile=None):
             js = slice(u * JT, (u + 1) * JT)
-            bank = psum.tile([P, PACK, JT], F32, name=f"gate{b}{u}", offset=(u % 2) * BANK)
+            acc = psum.tile([P, PACK, JT], F32, name=f"gate{b}{u}", offset=bank * BANK)
             for t in range(PACK):
                 col = b * PASS + t * P
                 nc.tensor.matmul_mx(
-                    out=bank[:, t, :],
+                    out=acc[:, t, :],
                     lhsT=wa_p[:, 2 * col : 2 * (col + P)].bitcast(FP4X4),
                     lhsT_scale=wa_s[:, col : col + P],
-                    rhs=words(js.start, JT),
+                    rhs=words(js),
                     rhs_scale=v_s[:, js],
                     start=True,
                     stop=True,
                 )
-            if (b, u) in ACT_ROOM:
-                act[b, u] = shared.tile([P, JT, PACK], F32, name=f"act{b}{u}", offset=ACT_ROOM[b, u], align_bytes=64)
-            else:
-                act[b, u] = keep.tile([P, JT, PACK], F32, name=f"act{b}{u}", align_bytes=64)
-            nc.scalar.activation(act[b, u][:], bank[:].rearrange("p t j -> p j t"), ACT.Silu)
+            act[b, u] = own(f"act{b}{u}", [P, JT, PACK], F32) if tile is None else tile
+            nc.scalar.activation(act[b, u][:], acc[:].rearrange("p t j -> p j t"), ACT.Silu)
 
-        def up_tile(b, u):
+        def up_tile(b, u, bank):
             js = slice(u * JT, (u + 1) * JT)
-            bank = 2 + u % 3 if u < 4 else 4 - u % 2
             up = psum.tile([P, PACK, JT], F32, name=f"up{b}{u}", offset=bank * BANK)
             for t in (2, 3, 0, 1):
                 nc.tensor.matmul_mx(
                     out=up[:, t, :],
                     lhsT=wb_q[b][:, t * P : (t + 1) * P].bitcast(FP8X4),
                     lhsT_scale=wb_s[b][:, t * P : (t + 1) * P],
-                    rhs=words(js.start, JT),
+                    rhs=words(js),
                     rhs_scale=v_s[:, js],
                     start=True,
                     stop=True,
                 )
             return up[:].rearrange("p t j -> p j t")
 
-        def hidden_slice(h_bf, u, first):
-            return h_bf[:, (u - first) * PASS : (u - first + 1) * PASS].rearrange("p (j t) -> p j t", t=PACK)
+        def hidden(h_bf, n):
+            return h_bf[:, n * PASS : (n + 1) * PASS].rearrange("p (j t) -> p j t", t=PACK)
 
-        def multiply_on_vector(b, u, h_bf, first):
-            nc.vector.tensor_tensor(hidden_slice(h_bf, u, first), up_tile(b, u), act[b, u][:], MULT)
+        def multiply_on_vector(b, u, bank, dst):
+            nc.vector.tensor_tensor(dst, up_tile(b, u, bank), act[b, u][:], MULT)
 
-        def stage(b, u):
-            gate(b, u)
-            if (b, u) in UP_ROOM:
-                up_sb[b, u] = shared.tile([P, JT, PACK], F32, name=f"up_sb{b}{u}", offset=UP_ROOM[b, u], align_bytes=64)
-            else:
-                up_sb[b, u] = keep.tile([P, JT, PACK], F32, name=f"up_sb{b}{u}", align_bytes=64)
-            nc.scalar.copy(up_sb[b, u][:], up_tile(b, u))
+        up_sb = {}
 
-        def hidden_tile(k, b, width):
-            if (k, b) in HIDDEN_ROOM:
-                return shared.tile([P, PACK * width], BF16, name=f"h_bf{k}{b}", offset=HIDDEN_ROOM[k, b], align_bytes=64)
-            return keep.tile([P, PACK * width], BF16, name=f"h_bf{k}{b}", align_bytes=64)
+        def stage_up(b, u, room):
+            up_sb[b, u] = tenant(f"up_sb{b}{u}", [P, JT, PACK], F32, room)
+            nc.scalar.copy(up_sb[b, u][:], up_tile(b, u, 6 + u % 2))
 
-        def multiply_on_gpsimd(b, u, h_bf, first):
-            nc.gpsimd.tensor_tensor(hidden_slice(h_bf, u, first), up_sb[b, u][:], act[b, u][:], MULT)
+        def multiply_on_gpsimd(b, u, dst):
+            nc.gpsimd.tensor_tensor(dst, up_sb[b, u][:], act[b, u][:], MULT)
 
-        def quantise_rows(k, b, h_bf, codes_tag, scales_tag):
-            width = PARTS[k].stop - PARTS[k].start
-            h_q[k, b] = keep.tile([P, width], U32, name=f"h_q{k}{b}", tag=codes_tag, align_bytes=64)
-            h_s[k, b] = keep.tile([P, width], U8, name=f"h_s{k}{b}", tag=scales_tag, align_bytes=64)
-            nc.vector.quantize_mx(out=h_q[k, b][:].bitcast(FP8X4), scales=h_s[k, b][:], in_=h_bf[:])
+        h_q = {}
 
-        def sums(k, rows, bank):
-            js = PARTS[k]
-            width = js.stop - js.start
-            acc = psum.tile([P, len(rows), width], F32, name=f"acc{k}{rows[0]}", offset=bank * BANK)
-            for n, i in enumerate(rows):
-                nc.tensor.matmul_mx(
-                    out=acc[:, n, :],
-                    lhsT=wd_q[:, i * P : (i + 1) * P].bitcast(FP8X4),
-                    lhsT_scale=wd_s[:, i * P : (i + 1) * P],
-                    rhs=words(js.start, width),
-                    rhs_scale=v_s[:, js],
-                    start=(n == 0),
-                    stop=False,
-                )
-            for n, i in enumerate(rows):
+        def sum_of(i, runs, bank):
+            first = runs[0].start
+            acc = psum.tile([P, runs[-1].stop - first], F32, name=f"acc{i}_{first}", offset=bank * BANK)
+            passes = []
+            for js in runs:
+                passes.append((js, wd_q[:, i * P : (i + 1) * P], wd_s[:, i * P : (i + 1) * P], words(js), v_s[:, js]))
+            for js in runs:
                 for a in range(2):
-                    col = a * N + i * P
-                    nc.tensor.matmul_mx(
-                        out=acc[:, n, :],
-                        lhsT=wc_p[:, (2 * i + a) * P : (2 * i + a + 1) * P].bitcast(FP8X4),
-                        lhsT_scale=wc_s[:, col : col + P],
-                        rhs=h_q[k, a][:].bitcast(FP8X4),
-                        rhs_scale=h_s[k, a][:],
-                        start=False,
-                        stop=(n == len(rows) - 1 and a == 1),
-                    )
-            return {i: acc[:, n, :] for n, i in enumerate(rows)}
-
-        def result_tile(name, width, tag=""):
-            return keep.tile([P, width], F32, name=name, tag=tag or name, align_bytes=64)
+                    codes, scales = h_q[js.start, a]
+                    lhs = wc_p[i // 2][:, (2 * (i % 2) + a) * P : (2 * (i % 2) + a + 1) * P]
+                    passes.append((js, lhs, wc_s[:, a * N + i * P : a * N + (i + 1) * P], codes.bitcast(FP8X4), scales))
+            for n, (js, lhs, lhs_s, rhs, rhs_s) in enumerate(passes):
+                nc.tensor.matmul_mx(
+                    out=acc[:, js.start - first : js.stop - first],
+                    lhsT=lhs.bitcast(FP8X4),
+                    lhsT_scale=lhs_s,
+                    rhs=rhs,
+                    rhs_scale=rhs_s,
+                    start=(n == 0),
+                    stop=(n == len(passes) - 1),
+                )
+            return acc
 
         def add_bias(i, acc, dst):
             nc.scalar.activation(dst, acc, ACT.Identity, bias=bias[:, i : i + 1])
 
-        def weigh_on_gpsimd(k, i, acc):
-            width = PARTS[k].stop - PARTS[k].start
-            y = shared.tile([P, width], F32, name=f"y{k}{i}", offset=RESULT_ROOM[k, i], align_bytes=64)
-            add_bias(i, acc, y[:])
-            weighed = result_tile(f"weighed{k}{i}", width)
-            nc.gpsimd.tensor_tensor(weighed[:], y[:], weight[:, PARTS[k]], MULT)
-            return weighed
+        def weigh_on_gpsimd(dst, y, js):
+            nc.gpsimd.tensor_tensor(dst[:], y[:], weight[:, js], MULT)
 
         def window(i, js):
             return pages[i][:].indirect(put[:, js.start // 16 : js.stop // 16])
 
-        def scatter(i, k, weighed):
-            nc.vector.tensor_copy(window(i, PARTS[k]), weighed[:])
+        def scatter(i, js, weighed):
+            nc.vector.tensor_copy(window(i, js), weighed[:])
 
         def weigh_and_scatter(i, js, y):
             nc.vector.tensor_tensor(window(i, js), y[:], weight[:, js], MULT)
 
-        h_bf = [hidden_tile(0, b, HALF) for b in range(2)]
+        h00 = tenant("h00", [P, 4 * PASS], BF16, "first_h")
         for u in range(4):
-            gate(0, u)
+            gate(0, u, u % 2)
         for u in range(4):
-            multiply_on_vector(0, u, h_bf[0], 0)
-            gate(1, u)
-        nc.vector.quantize_mx(out=wb_q[1][:].bitcast(FP8X4), scales=wb_s[1][:], in_=second_bf[:])
-        quantise_rows(0, 0, h_bf[0], "first_bf0", "h_s00")
-        for u in range(4):
-            multiply_on_vector(1, u, h_bf[1], 0)
-        gate(0, 4)
-        wd_bf = {
-            0: keep.tile([P, 2 * PASS], BF16, name="wd_bf0", tag="h_bf00", align_bytes=64),
-            1: keep.tile([P, 2 * PASS], BF16, name="wd_bf1", align_bytes=64),
-        }
-        for half in range(2):
-            dst = wd_bf[half][:].rearrange("p (t m i) -> p m t i", t=2, i=PACK)
-            src = wd_raw[:].rearrange("p i (m t) -> p m t i", t=PACK)[:, :, 2 * half : 2 * half + 2]
-            if half == 0:
+            multiply_on_vector(0, u, 2 + u % 3, hidden(h00, u))
+            if u < 3:
+                gate(1, u, u % 2)
+        quantise(wb_q[1][:], wb_s[1][:], second_bf[:])
+        codes = tenant("h_q00", [P, 512], U32, "wb3")
+        scales = tenant("h_s00", [P, 512], U8, "wb3", 2048)
+        quantise(codes[:], scales[:], h00[:])
+        for js in (slice(0, 256), slice(256, 384), FILL):
+            h_q[js.start, 0] = (codes[:, js], scales[:, js])
+        h01 = own("h01", [P, 3 * PASS], BF16)
+        for u in range(3):
+            multiply_on_vector(1, u, 2 + (u + 1) % 3, hidden(h01, u))
+
+        wd_bf = [tenant("wd_bf0", [P, 2 * PASS], BF16, "first_h"), own("wd_bf1", [P, 2 * PASS], BF16)]
+        for pair in range(2):
+            dst = wd_bf[pair][:].rearrange("p (t m i) -> p m t i", t=2, i=PACK)
+            src = wd_raw[:].rearrange("p i (m t) -> p m t i", t=PACK)[:, :, 2 * pair : 2 * pair + 2]
+            if pair == 0:
                 nc.gpsimd.tensor_scalar(dst, src, 1.0, 0.0, MULT, ADD)
             else:
                 nc.scalar.copy(dst, src)
-        wc_p = keep.tile([P, 2 * N], U32, name="wc_p", align_bytes=64)
-        for half in range(2):
+        wc_p = [own(f"wc_p{pair}", [P, N], U32) for pair in range(2)]
+
+        def reorder_wc(pair):
             nc.scalar.copy(
-                wc_p[:, half * N : (half + 1) * N].rearrange("p (t a g m) -> p a g t m", a=2, t=2, m=4),
+                wc_p[pair][:].rearrange("p (t a g m) -> p a g t m", a=2, t=2, m=4),
                 wc_raw[:].bitcast(U32).rearrange("p (a g m t) -> p a g t m", a=2, t=PACK, m=4)[
-                    :, :, :, 2 * half : 2 * half + 2
+                    :, :, :, 2 * pair : 2 * pair + 2
                 ],
             )
-        wd_q = keep.tile([P, PASS], U32, name="wd_q", align_bytes=64)
-        for half in range(2):
-            cols = slice(half * 2 * P, (half + 1) * 2 * P)
-            nc.vector.quantize_mx(out=wd_q[:, cols].bitcast(FP8X4), scales=wd_s[:, cols], in_=wd_bf[half][:])
-        quantise_rows(0, 1, h_bf[1], "wd_bf1", "h_bf00")
-        h_bf = [hidden_tile(1, b, QUARTER) for b in range(2)]
-        multiply_on_vector(0, 4, h_bf[0], 4)
 
-        first = result_tile("weighed00", HALF)
+        reorder_wc(0)
+        wd_q = own("wd_q", [P, PASS], U32)
+        wd_s = own("wd_s", [P, PASS], U8)
+        for pair in range(2):
+            cols = slice(pair * 2 * P, (pair + 1) * 2 * P)
+            quantise(wd_q[:, cols], wd_s[:, cols], wd_bf[pair][:])
+        codes = tenant("h_q01", [P, 384], U32, "wd")
+        scales = tenant("h_s01", [P, 384], U8, "wd", 2048)
+        quantise(codes[:], scales[:], h01[:])
+        for js in (slice(0, 256), slice(256, 384)):
+            h_q[js.start, 1] = (codes[:, js], scales[:, js])
+        gate(1, 3, 1, tenant("act13", [P, JT, PACK], F32, "wd", 4096))
+        h13 = tenant("h13", [P, PASS], BF16, "late_h")
+        multiply_on_vector(1, 3, 3, hidden(h13, 0))
+
+        first_runs = (slice(0, 256), slice(256, 384))
+        weighed = {i: own(f"weighed0{i}", [P, 384], F32) for i in range(3)}
         nc.vector.scalar_tensor_tensor(
-            first[:], sums(0, (0,), 5)[0], bias[:, 0:1], weight[:, PARTS[0]], ADD, MULT
+            weighed[0][:], sum_of(0, first_runs, 5)[:], bias[:, 0:1], weight[:, FIRST], ADD, MULT
         )
-        second = weigh_on_gpsimd(0, 1, sums(0, (1,), 2)[1])
-        third = weigh_on_gpsimd(0, 3, sums(0, (3,), 5)[3])
-        y_held = result_tile("y02", HALF)
-        add_bias(2, sums(0, (2,), 2)[2], y_held[:])
-        scatter(0, 0, first)
-        scatter(1, 0, second)
-        scatter(3, 0, third)
-        for tile in ((0, 5), (1, 4), (0, 6), (0, 7), (1, 6), (1, 5)):
-            stage(*tile)
-        early_bf = keep.tile([P, PASS], BF16, name="early_bf", align_bytes=64)
-        multiply_on_gpsimd(0, 5, h_bf[0], 4)
-        multiply_on_gpsimd(1, 4, h_bf[1], 4)
-        multiply_on_gpsimd(0, 6, early_bf, 6)
-        multiply_on_gpsimd(1, 5, h_bf[1], 4)
-        held = result_tile("weighed02", HALF, "up_sb15")
-        nc.gpsimd.tensor_tensor(held[:], y_held[:], weight[:, PARTS[0]], MULT)
-        quantise_rows(1, 0, h_bf[0], "act15", "weighed03")
-        quantise_rows(1, 1, h_bf[1], "h_q11", "h_s11")
+        codes = own("h_q13", [P, JT], U32)
+        scales = own("h_s13", [P, JT], U8)
+        quantise(codes[:], scales[:], h13[:])
+        h_q[FILL.start, 1] = (codes[:], scales[:])
+        scatter(0, FIRST, weighed[0])
 
-        scatter(2, 0, held)
-        acc = sums(1, (0, 1), 5)
-        first = weigh_on_gpsimd(1, 0, acc[0])
-        second = weigh_on_gpsimd(1, 1, acc[1])
-        y_wide = result_tile("y_wide", HALF)
-        add_bias(2, sums(1, (2,), 6)[2], y_wide[:, 0:QUARTER])
-        acc_held = sums(1, (3,), 7)[3]
-        scatter(0, 1, first)
-        scatter(1, 1, second)
-        stage(1, 7)
-        late_bf = hidden_tile(2, 0, JT)
-        last_bf = hidden_tile(2, 1, QUARTER)
-        multiply_on_gpsimd(0, 7, late_bf, 7)
-        multiply_on_gpsimd(1, 6, last_bf, 6)
-        multiply_on_gpsimd(1, 7, last_bf, 6)
-        y_cover = shared.tile([P, QUARTER], F32, name="y13", offset=UP_ROOM[1, 7], align_bytes=64)
-        add_bias(3, acc_held, y_cover[:])
-        h_q[2, 0] = keep.tile([P, QUARTER], U32, name="h_q20", tag="act17", align_bytes=64)
-        h_s[2, 0] = keep.tile([P, QUARTER], U8, name="h_s20", tag="weighed11", align_bytes=64)
-        for n, tile in enumerate((early_bf, late_bf)):
-            cols = slice(n * JT, (n + 1) * JT)
-            nc.vector.quantize_mx(out=h_q[2, 0][:, cols].bitcast(FP8X4), scales=h_s[2, 0][:, cols], in_=tile[:])
-        quantise_rows(2, 1, last_bf, "h_q21", "h_s21")
-        weigh_and_scatter(3, PARTS[1], y_cover)
+        late = tenant("h_second", [P, 4 * PASS], BF16, "late_h")
+        gate(0, 4, 1)
+        stage_up(0, 4, "up")
+        multiply_on_gpsimd(0, 4, hidden(late, 0))
+        y = own("y01", [P, 384], F32)
+        add_bias(1, sum_of(1, first_runs, 3)[:], y[:])
+        weigh_on_gpsimd(weighed[1], y, FIRST)
+        scatter(1, FIRST, weighed[1])
+        reorder_wc(1)
+        gate(0, 5, 1)
+        stage_up(0, 5, "up")
+        multiply_on_gpsimd(0, 5, hidden(late, 1))
+        y = tenant("y02", [P, 384], F32, "y02")
+        add_bias(2, sum_of(2, first_runs, 5)[:], y[:])
+        weigh_on_gpsimd(weighed[2], y, FIRST)
+        scatter(2, FIRST, weighed[2])
+        gate(1, 4, 1)
+        stage_up(1, 4, "up")
+        multiply_on_gpsimd(1, 4, hidden(late, 2))
+        gate(1, 5, 1, tenant("act15", [P, JT, PACK], F32, "act15"))
+        stage_up(1, 5, "y02")
+        multiply_on_gpsimd(1, 5, hidden(late, 3))
+        y = own("y03", [P, 384], F32)
+        add_bias(3, sum_of(3, first_runs, 3)[:], y[:])
+        gate(0, 6, 1)
+        stage_up(0, 6, "up")
+        held = tenant("weighed03", [P, 384], F32, "act15")
+        weigh_on_gpsimd(held, y, FIRST)
+
+        def quantise_run(js, h_bf):
+            codes = own(f"h_q{js.start}", [P, 2 * QUARTER], U32)
+            scales = own(f"h_s{js.start}", [P, 2 * QUARTER], U8)
+            quantise(codes[:], scales[:], h_bf[:])
+            for a in range(2):
+                cols = slice(a * QUARTER, (a + 1) * QUARTER)
+                h_q[js.start, a] = (codes[:, cols], scales[:, cols])
+
+        quantise_run(SECOND, late)
+        scatter(3, FIRST, held)
+
+        middle = slice(FILL.start, SECOND.stop)
+        early = slice(FILL.start, HELD)
+        cut = HELD - FILL.start
+        late = tenant("h_last", [P, 4 * PASS], BF16, "late_h")
+        multiply_on_gpsimd(0, 6, hidden(late, 0))
+        wide = {i: own(f"y_wide{i}", [P, S - HELD], F32) for i in (2, 3)}
+        for i, (b, u), bank in ((0, (0, 7), 5), (1, (1, 6), 3), (2, (1, 7), 5)):
+            js = middle if i < 2 else early
+            acc = sum_of(i, (FILL, SECOND), bank)
+            y = own(f"y1{i}", [P, js.stop - js.start], F32)
+            add_bias(i, acc[:, 0 : js.stop - js.start], y[:])
+            if i == 2:
+                add_bias(i, acc[:, cut:], wide[i][:, 0 : SECOND.stop - HELD])
+            result = own(f"weighed1{i}", [P, js.stop - js.start], F32)
+            weigh_on_gpsimd(result, y, js)
+            scatter(i, js, result)
+            gate(b, u, 1)
+            stage_up(b, u, "up")
+            multiply_on_gpsimd(b, u, hidden(late, 2 * b + u - 6))
+        acc = sum_of(3, (FILL, SECOND), 3)
+        add_bias(3, acc[:, cut:], wide[3][:, 0 : SECOND.stop - HELD])
+        cover = tenant("y13", [P, cut], F32, "up")
+        add_bias(3, acc[:, 0:cut], cover[:])
+        quantise_run(LAST, late)
+        weigh_and_scatter(3, early, cover)
 
         out_rows = out.rearrange("(p i) t -> p i t", i=PACK)
-        for rows, bank in (((0,), 5), ((1,), 6), ((3, 2), 5)):
-            acc = sums(2, rows, bank)
-            for i in rows:
-                if i == 2:
-                    add_bias(i, acc[i], y_wide[:, QUARTER:])
-                    weigh_and_scatter(i, slice(HALF, S), y_wide)
-                else:
-                    y = result_tile(f"y2{i}", QUARTER)
-                    add_bias(i, acc[i], y[:])
-                    weigh_and_scatter(i, PARTS[2], y)
-                nc.sync.dma_start(out_rows[:, i, :], pages[i][:])
+        for i, bank in enumerate((5, 6, 7, 3)):
+            acc = sum_of(i, (LAST,), bank)
+            if i < 2:
+                y = own(f"y2{i}", [P, QUARTER], F32)
+                add_bias(i, acc[:], y[:])
+                weigh_and_scatter(i, LAST, y)
+            else:
+                add_bias(i, acc[:], wide[i][:, SECOND.stop - HELD :])
+                weigh_and_scatter(i, slice(HELD, S), wide[i])
+            nc.sync.dma_start(out_rows[:, i, :], pages[i][:])

@@ -27,13 +27,11 @@ BANK = 2048
 
 FIRST, FILL, SECOND, LAST = slice(0, 384), slice(384, 512), slice(512, 768), slice(768, 1024)
 WORD_RUNS = (slice(0, 512), SECOND, LAST)
-CLEAR_CUT = 1728
 HELD = 640
 
 ROOM_SIZES = (
     ("wb2", 4096),
     ("wb3", 4096),
-    ("wc_s", 1024),
     ("wd", 8192),
     ("wc", 4096),
     ("weight", 4096),
@@ -42,11 +40,11 @@ ROOM_SIZES = (
     ("wb_bf", 4096),
     ("first_h", 4096),
     ("late_h", 4096),
-    ("up", 2048),
     ("y02", 2048),
     ("act15", 2048),
 )
 ROOM = {name: sum(size for other, size in ROOM_SIZES[:n]) for n, (name, own) in enumerate(ROOM_SIZES)}
+ROOM = {**ROOM, "act04": ROOM["wc"], "up": ROOM["wc"] + 2048}
 
 
 def tile_list_beam_cache_rewrite_kernel(
@@ -95,12 +93,11 @@ def tile_list_beam_cache_rewrite_kernel(
         pages = {i: own(f"page{i}", [P, T2], F32) for i in range(3)}
         nc.gpsimd.memset(pages[1][:], 0.0)
         nc.gpsimd.memset(pages[2][:], 0.0)
-        nc.gpsimd.memset(pages[0][:, CLEAR_CUT:], 0.0)
         warm = own("warm", [P, 2], F32)
         nc.vector.memset(warm[:, 0:1], 0.0)
         nc.scalar.activation(warm[:, 1:2], warm[:, 0:1], ACT.Silu)
-        nc.vector.memset(pages[0][:, 0 : CLEAR_CUT // 2 - 1], 0.0)
-        nc.vector.memset(pages[0][:, CLEAR_CUT // 2 - 1 : CLEAR_CUT], 0.0)
+        nc.vector.memset(pages[0][:, 0 : T2 // 2 - 1], 0.0)
+        nc.vector.memset(pages[0][:, T2 // 2 - 1 :], 0.0)
 
         picked_s = tenant("picked_s", [P, ROOM["wb1"]], U8, "wb2")
         planes = own("planes", [P, S + H], U8)
@@ -115,8 +112,7 @@ def tile_list_beam_cache_rewrite_kernel(
         for n in (2, 3):
             wb_raw[n] = tenant(f"wb_raw{n}", [P, PACK, QUARTER], F32, f"wb{n}")
             nc.sync.dma_start(wb_raw[n][:], wb_rows[:, :, n * QUARTER : (n + 1) * QUARTER])
-        wc_s = tenant("wc_s", [P, H], U8, "wc_s")
-        nc.gpsimd.memset(wc_s[:].bitcast(I32), 0)
+        wc_s = ws_raw
         for r in range(4):
             nc.sync.dma_start(wc_s[r:P:32, :].bitcast(I32), planes[WC_ROW + 8 * r : P : 32, S:].bitcast(I32))
         wd_raw = tenant("wd_raw", [P, PACK, PASS], F32, "wd")
@@ -278,7 +274,7 @@ def tile_list_beam_cache_rewrite_kernel(
         quantise(codes[:], scales[:], h00[:])
         for js in (slice(0, 256), slice(256, 384), FILL):
             h_q[js.start, 0] = (codes[:, js], scales[:, js])
-        h01 = own("h01", [P, 3 * PASS], BF16)
+        h01 = tenant("h01", [P, 3 * PASS], BF16, "late_h")
         for u in range(3):
             multiply_on_vector(1, u, 2 + (u + 1) % 3, hidden(h01, u))
 
@@ -301,6 +297,7 @@ def tile_list_beam_cache_rewrite_kernel(
             )
 
         reorder_wc(0)
+        reorder_wc(1)
         wd_q = own("wd_q", [P, PASS], U32)
         wd_s = own("wd_s", [P, PASS], U8)
         for pair in range(2):
@@ -311,8 +308,8 @@ def tile_list_beam_cache_rewrite_kernel(
         quantise(codes[:], scales[:], h01[:])
         for js in (slice(0, 256), slice(256, 384)):
             h_q[js.start, 1] = (codes[:, js], scales[:, js])
-        gate(1, 3, 1, tenant("act13", [P, JT, PACK], F32, "wd", 4096))
-        h13 = tenant("h13", [P, PASS], BF16, "late_h")
+        gate(1, 3, 1)
+        h13 = own("h13", [P, PASS], BF16)
         multiply_on_vector(1, 3, 3, hidden(h13, 0))
 
         first_runs = (slice(0, 256), slice(256, 384))
@@ -320,40 +317,39 @@ def tile_list_beam_cache_rewrite_kernel(
         nc.vector.scalar_tensor_tensor(
             weighed[0][:], sum_of(0, first_runs, 5)[:], bias[:, 0:1], weight[:, FIRST], ADD, MULT
         )
-        codes = own("h_q13", [P, JT], U32)
-        scales = own("h_s13", [P, JT], U8)
-        quantise(codes[:], scales[:], h13[:])
-        h_q[FILL.start, 1] = (codes[:], scales[:])
         scatter(0, FIRST, weighed[0])
 
         late = tenant("h_second", [P, 4 * PASS], BF16, "late_h")
-        gate(0, 4, 1)
+        gate(0, 4, 0, tenant("act04", [P, JT, PACK], F32, "act04"))
         stage_up(0, 4, "up")
         multiply_on_gpsimd(0, 4, hidden(late, 0))
         y = own("y01", [P, 384], F32)
         add_bias(1, sum_of(1, first_runs, 3)[:], y[:])
         weigh_on_gpsimd(weighed[1], y, FIRST)
         scatter(1, FIRST, weighed[1])
-        reorder_wc(1)
-        gate(0, 5, 1)
+        gate(0, 5, 0)
         stage_up(0, 5, "up")
         multiply_on_gpsimd(0, 5, hidden(late, 1))
         y = tenant("y02", [P, 384], F32, "y02")
         add_bias(2, sum_of(2, first_runs, 5)[:], y[:])
         weigh_on_gpsimd(weighed[2], y, FIRST)
         scatter(2, FIRST, weighed[2])
-        gate(1, 4, 1)
+        gate(1, 4, 0)
         stage_up(1, 4, "up")
         multiply_on_gpsimd(1, 4, hidden(late, 2))
-        gate(1, 5, 1, tenant("act15", [P, JT, PACK], F32, "act15"))
+        gate(1, 5, 0, tenant("act15", [P, JT, PACK], F32, "act15"))
         stage_up(1, 5, "y02")
         multiply_on_gpsimd(1, 5, hidden(late, 3))
-        y = own("y03", [P, 384], F32)
-        add_bias(3, sum_of(3, first_runs, 3)[:], y[:])
-        gate(0, 6, 1)
+        gate(0, 6, 0)
         stage_up(0, 6, "up")
         held = tenant("weighed03", [P, 384], F32, "act15")
-        weigh_on_gpsimd(held, y, FIRST)
+        nc.vector.scalar_tensor_tensor(
+            held[:], sum_of(3, first_runs, 3)[:], bias[:, 3:4], weight[:, FIRST], ADD, MULT
+        )
+        codes = tenant("h_q13", [P, JT], U32, "act15", 1536)
+        scales = own("h_s13", [P, JT], U8)
+        quantise(codes[:], scales[:], h13[:])
+        h_q[FILL.start, 1] = (codes[:], scales[:])
 
         def quantise_run(js, h_bf):
             codes = own(f"h_q{js.start}", [P, 2 * QUARTER], U32)
@@ -382,7 +378,7 @@ def tile_list_beam_cache_rewrite_kernel(
             result = own(f"weighed1{i}", [P, js.stop - js.start], F32)
             weigh_on_gpsimd(result, y, js)
             scatter(i, js, result)
-            gate(b, u, 1)
+            gate(b, u, 0)
             stage_up(b, u, "up")
             multiply_on_gpsimd(b, u, hidden(late, 2 * b + u - 6))
         acc = sum_of(3, (FILL, SECOND), 3)

@@ -44,7 +44,7 @@ ROOM_SIZES = (
     ("act15", 2048),
 )
 ROOM = {name: sum(size for other, size in ROOM_SIZES[:n]) for n, (name, own) in enumerate(ROOM_SIZES)}
-ROOM = {**ROOM, "act04": ROOM["wc"], "up": ROOM["wc"] + 2048}
+ROOM = {**ROOM, "act04": ROOM["wd"] + 4096, "up": ROOM["wd"] + 6144}
 
 
 def tile_list_beam_cache_rewrite_kernel(
@@ -115,13 +115,13 @@ def tile_list_beam_cache_rewrite_kernel(
         wc_s = ws_raw
         for r in range(4):
             nc.sync.dma_start(wc_s[r:P:32, :].bitcast(I32), planes[WC_ROW + 8 * r : P : 32, S:].bitcast(I32))
-        wd_raw = tenant("wd_raw", [P, PACK, PASS], F32, "wd")
-        nc.sync.dma_start(wd_raw[:], wd.rearrange("(p i) c -> p i c", i=PACK))
         wc_raw = tenant("wc_raw", [P, 2 * N], I32, "wc")
         nc.sync.dma_start(
             wc_raw[:].rearrange("p (a c) -> p a c", a=2),
             wc_words.rearrange("a p c i -> p a (c i)").bitcast(I32),
         )
+        wd_raw = tenant("wd_raw", [P, PACK, PASS], F32, "wd")
+        nc.sync.dma_start(wd_raw[:], wd.rearrange("(p i) c -> p i c", i=PACK))
         weight = tenant("weight", [P, S], F32, "weight")
         nc.sync.dma_start(weight[:], wgo)
         pages[3] = tenant("page3", [P, T2], F32, "page3")
@@ -286,9 +286,10 @@ def tile_list_beam_cache_rewrite_kernel(
                 nc.gpsimd.tensor_scalar(dst, src, 1.0, 0.0, MULT, ADD)
             else:
                 nc.scalar.copy(dst, src)
-        wc_p = [own(f"wc_p{pair}", [P, N], U32) for pair in range(2)]
+        wc_p = {}
 
-        def reorder_wc(pair):
+        def reorder_wc(pair, tile):
+            wc_p[pair] = tile
             nc.scalar.copy(
                 wc_p[pair][:].rearrange("p (t a g m) -> p a g t m", a=2, t=2, m=4),
                 wc_raw[:].bitcast(U32).rearrange("p (a g m t) -> p a g t m", a=2, t=PACK, m=4)[
@@ -296,19 +297,18 @@ def tile_list_beam_cache_rewrite_kernel(
                 ],
             )
 
-        reorder_wc(0)
-        reorder_wc(1)
+        reorder_wc(0, own("wc_p0", [P, N], U32))
         wd_q = own("wd_q", [P, PASS], U32)
         wd_s = own("wd_s", [P, PASS], U8)
         for pair in range(2):
             cols = slice(pair * 2 * P, (pair + 1) * 2 * P)
             quantise(wd_q[:, cols], wd_s[:, cols], wd_bf[pair][:])
-        codes = tenant("h_q01", [P, 384], U32, "wd")
-        scales = tenant("h_s01", [P, 384], U8, "wd", 2048)
+        codes = tenant("h_q01", [P, 384], U32, "first_h")
+        scales = tenant("h_s01", [P, 384], U8, "first_h", 1536)
         quantise(codes[:], scales[:], h01[:])
         for js in (slice(0, 256), slice(256, 384)):
             h_q[js.start, 1] = (codes[:, js], scales[:, js])
-        gate(1, 3, 1)
+        gate(1, 3, 1, tenant("act13", [P, JT, PACK], F32, "wd"))
         h13 = own("h13", [P, PASS], BF16)
         multiply_on_vector(1, 3, 3, hidden(h13, 0))
 
@@ -323,6 +323,7 @@ def tile_list_beam_cache_rewrite_kernel(
         gate(0, 4, 0, tenant("act04", [P, JT, PACK], F32, "act04"))
         stage_up(0, 4, "up")
         multiply_on_gpsimd(0, 4, hidden(late, 0))
+        reorder_wc(1, tenant("wc_p1", [P, N], U32, "wd", 2048))
         y = own("y01", [P, 384], F32)
         add_bias(1, sum_of(1, first_runs, 3)[:], y[:])
         weigh_on_gpsimd(weighed[1], y, FIRST)

@@ -39,7 +39,7 @@ ROOM_SIZES = (
     ("wb1", 4096),
     ("wb_bf", 4096),
     ("first_h", 4096),
-    ("late_h", 4096),
+    ("late_h", 5120),
     ("y02", 2048),
     ("act15", 2048),
 )
@@ -278,7 +278,7 @@ def tile_list_beam_cache_rewrite_kernel(
         for u in range(3):
             multiply_on_vector(1, u, 2 + (u + 1) % 3, hidden(h01, u))
 
-        wd_bf = [tenant("wd_bf0", [P, 2 * PASS], BF16, "first_h"), own("wd_bf1", [P, 2 * PASS], BF16)]
+        wd_bf = [tenant("wd_bf0", [P, 2 * PASS], BF16, "first_h"), tenant("wd_bf1", [P, 2 * PASS], BF16, "late_h", 3072)]
         for pair in range(2):
             dst = wd_bf[pair][:].rearrange("p (t m i) -> p m t i", t=2, i=PACK)
             src = wd_raw[:].rearrange("p i (m t) -> p m t i", t=PACK)[:, :, 2 * pair : 2 * pair + 2]
@@ -300,12 +300,13 @@ def tile_list_beam_cache_rewrite_kernel(
         reorder_wc(0, own("wc_p0", [P, N], U32))
         wd_q = own("wd_q", [P, PASS], U32)
         wd_s = own("wd_s", [P, PASS], U8)
+        codes = own("h_q01", [P, 384], U32)
+        scales = own("h_s01", [P, 384], U8)
+        for js in (slice(0, 256), slice(256, 384)):
+            quantise(codes[:, js], scales[:, js], h01[:, PACK * js.start : PACK * js.stop])
         for pair in range(2):
             cols = slice(pair * 2 * P, (pair + 1) * 2 * P)
             quantise(wd_q[:, cols], wd_s[:, cols], wd_bf[pair][:])
-        codes = tenant("h_q01", [P, 384], U32, "first_h")
-        scales = tenant("h_s01", [P, 384], U8, "first_h", 1536)
-        quantise(codes[:], scales[:], h01[:])
         for js in (slice(0, 256), slice(256, 384)):
             h_q[js.start, 1] = (codes[:, js], scales[:, js])
         gate(1, 3, 1, tenant("act13", [P, JT, PACK], F32, "wd"))

@@ -27,6 +27,7 @@ BANK = 2048
 
 FIRST, FILL, SECOND, LAST = slice(0, 384), slice(384, 512), slice(512, 768), slice(768, 1024)
 WORD_RUNS = (slice(0, 512), SECOND, LAST)
+SHARE = 64
 HELD = 640
 
 ROOM_SIZES = (
@@ -369,6 +370,11 @@ def tile_list_beam_cache_rewrite_kernel(
         cut = HELD - FILL.start
         late = tenant("h_last", [P, 4 * PASS], BF16, "late_h")
         multiply_on_gpsimd(0, 6, hidden(late, 0))
+        gate(0, 7, 0)
+        shared_up = up_tile(0, 7, 7)
+        rest = tenant("up_sb07", [P, JT - SHARE, PACK], F32, "up")
+        nc.scalar.copy(rest[:], shared_up[:, SHARE:])
+        nc.vector.tensor_tensor(hidden(late, 1)[:, 0:SHARE], shared_up[:, 0:SHARE], act[0, 7][:, 0:SHARE], MULT)
         wide = {i: own(f"y_wide{i}", [P, S - HELD], F32) for i in (2, 3)}
         for i, (b, u), bank in ((0, (0, 7), 5), (1, (1, 6), 3), (2, (1, 7), 5)):
             js = middle if i < 2 else early
@@ -380,9 +386,12 @@ def tile_list_beam_cache_rewrite_kernel(
             result = own(f"weighed1{i}", [P, js.stop - js.start], F32)
             weigh_on_gpsimd(result, y, js)
             scatter(i, js, result)
-            gate(b, u, 0)
-            stage_up(b, u, "up")
-            multiply_on_gpsimd(b, u, hidden(late, 2 * b + u - 6))
+            if i > 0:
+                gate(b, u, 0)
+                stage_up(b, u, "up")
+                multiply_on_gpsimd(b, u, hidden(late, 2 * b + u - 6))
+            else:
+                nc.gpsimd.tensor_tensor(hidden(late, 1)[:, SHARE:], rest[:], act[0, 7][:, SHARE:], MULT)
         acc = sum_of(3, (FILL, SECOND), 3)
         add_bias(3, acc[:, cut:], wide[3][:, 0 : SECOND.stop - HELD])
         cover = tenant("y13", [P, cut], F32, "up")

@@ -192,9 +192,9 @@ def tile_list_beam_cache_rewrite_kernel(
             act[b, u] = own(f"act{b}{u}", [P, JT, PACK], F32) if tile is None else tile
             nc.scalar.activation(act[b, u][:], acc[:].rearrange("p t j -> p j t"), ACT.Silu)
 
-        def up_tile(b, u, bank):
-            js = slice(u * JT, (u + 1) * JT)
-            up = psum.tile([P, PACK, JT], F32, name=f"up{b}{u}", offset=bank * BANK)
+        def up_tile(b, u, bank, first=0, width=JT):
+            js = slice(u * JT + first, u * JT + first + width)
+            up = psum.tile([P, PACK, width], F32, name=f"up{b}{u}_{first}", offset=bank * BANK)
             for t in (2, 3, 0, 1):
                 nc.tensor.matmul_mx(
                     out=up[:, t, :],
@@ -319,12 +319,14 @@ def tile_list_beam_cache_rewrite_kernel(
         nc.vector.scalar_tensor_tensor(
             weighed[0][:], sum_of(0, first_runs, 5)[:], bias[:, 0:1], weight[:, FIRST], ADD, MULT
         )
-        scatter(0, FIRST, weighed[0])
-
         late = tenant("h_second", [P, 4 * PASS], BF16, "late_h")
         gate(0, 4, 0, tenant("act04", [P, JT, PACK], F32, "act04"))
-        stage_up(0, 4, "up")
-        multiply_on_gpsimd(0, 4, hidden(late, 0))
+        nc.vector.tensor_tensor(hidden(late, 0)[:, 0:SHARE], up_tile(0, 4, 7, 0, SHARE), act[0, 4][:, 0:SHARE], MULT)
+        scatter(0, FIRST, weighed[0])
+
+        rest = tenant("up_sb04", [P, JT - SHARE, PACK], F32, "up")
+        nc.scalar.copy(rest[:], up_tile(0, 4, 6, SHARE, JT - SHARE))
+        nc.gpsimd.tensor_tensor(hidden(late, 0)[:, SHARE:], rest[:], act[0, 4][:, SHARE:], MULT)
         reorder_wc(1, tenant("wc_p1", [P, N], U32, "wd", 2048))
         y = own("y01", [P, 384], F32)
         add_bias(1, sum_of(1, first_runs, 3)[:], y[:])

@@ -90,6 +90,9 @@ def tile_list_beam_cache_rewrite_kernel(
         nc.sync.dma_start(put[:], offs2)
         bias = own("bias", [P, PACK], F32)
         nc.sync.dma_start(bias[:], bo.rearrange("(p i) -> p i", i=PACK))
+        wc_rows = [wc_words[a].rearrange("p c i -> p (c i)").bitcast(I32) for a in range(2)]
+        wc_raw = {0: own("wc_raw0", [P, N], I32)}
+        nc.sync.dma_start(wc_raw[0][:], wc_rows[0])
 
         pages = {i: own(f"page{i}", [P, T2], F32) for i in range(3)}
         nc.gpsimd.memset(pages[1][:], 0.0)
@@ -113,16 +116,13 @@ def tile_list_beam_cache_rewrite_kernel(
         for n in (2, 3):
             wb_raw[n] = tenant(f"wb_raw{n}", [P, PACK, QUARTER], F32, f"wb{n}")
             nc.sync.dma_start(wb_raw[n][:], wb_rows[:, :, n * QUARTER : (n + 1) * QUARTER])
+        wc_raw[1] = tenant("wc_raw1", [P, N], I32, "wc")
+        nc.sync.dma_start(wc_raw[1][:], wc_rows[1])
+        wd_raw = tenant("wd_raw", [P, PACK, PASS], F32, "wd")
+        nc.sync.dma_start(wd_raw[:], wd.rearrange("(p i) c -> p i c", i=PACK))
         wc_s = ws_raw
         for r in range(4):
             nc.sync.dma_start(wc_s[r:P:32, :].bitcast(I32), planes[WC_ROW + 8 * r : P : 32, S:].bitcast(I32))
-        wc_raw = tenant("wc_raw", [P, 2 * N], I32, "wc")
-        nc.sync.dma_start(
-            wc_raw[:].rearrange("p (a c) -> p a c", a=2),
-            wc_words.rearrange("a p c i -> p a (c i)").bitcast(I32),
-        )
-        wd_raw = tenant("wd_raw", [P, PACK, PASS], F32, "wd")
-        nc.sync.dma_start(wd_raw[:], wd.rearrange("(p i) c -> p i c", i=PACK))
         weight = tenant("weight", [P, S], F32, "weight")
         nc.sync.dma_start(weight[:], wgo)
         pages[3] = tenant("page3", [P, T2], F32, "page3")
@@ -166,6 +166,16 @@ def tile_list_beam_cache_rewrite_kernel(
         for pair in (1, 0):
             cols = slice(pair * 2 * P, (pair + 1) * 2 * P)
             quantise(wb_q[0][:, cols], wb_s[0][:, cols], first_bf[pair][:])
+        wc_p = {}
+
+        def reorder_wc(a):
+            wc_p[a] = own(f"wc_p{a}", [P, N], U32)
+            nc.scalar.copy(
+                wc_p[a][:].rearrange("p (t g m) -> p g t m", t=PACK, m=4),
+                wc_raw[a][:].bitcast(U32).rearrange("p (g m t) -> p g t m", t=PACK, m=4),
+            )
+
+        reorder_wc(0)
         gather_words(2, tenant("v_w2", [P, QUARTER], U32, "wb1"))
         second_bf = tenant("second_bf", [P, PACK * PASS], BF16, "wb_bf")
         for n in (2, 3):
@@ -233,7 +243,7 @@ def tile_list_beam_cache_rewrite_kernel(
             for js in runs:
                 for a in range(2):
                     codes, scales = h_q[js.start, a]
-                    lhs = wc_p[i // 2][:, (2 * (i % 2) + a) * P : (2 * (i % 2) + a + 1) * P]
+                    lhs = wc_p[a][:, i * P : (i + 1) * P]
                     passes.append((js, lhs, wc_s[:, a * N + i * P : a * N + (i + 1) * P], codes.bitcast(FP8X4), scales))
             for n, (js, lhs, lhs_s, rhs, rhs_s) in enumerate(passes):
                 nc.tensor.matmul_mx(
@@ -287,18 +297,7 @@ def tile_list_beam_cache_rewrite_kernel(
                 nc.gpsimd.tensor_scalar(dst, src, 1.0, 0.0, MULT, ADD)
             else:
                 nc.scalar.copy(dst, src)
-        wc_p = {}
-
-        def reorder_wc(pair, tile):
-            wc_p[pair] = tile
-            nc.scalar.copy(
-                wc_p[pair][:].rearrange("p (t a g m) -> p a g t m", a=2, t=2, m=4),
-                wc_raw[:].bitcast(U32).rearrange("p (a g m t) -> p a g t m", a=2, t=PACK, m=4)[
-                    :, :, :, 2 * pair : 2 * pair + 2
-                ],
-            )
-
-        reorder_wc(0, own("wc_p0", [P, N], U32))
+        reorder_wc(1)
         wd_q = own("wd_q", [P, PASS], U32)
         wd_s = own("wd_s", [P, PASS], U8)
         codes = own("h_q01", [P, 384], U32)
@@ -327,7 +326,6 @@ def tile_list_beam_cache_rewrite_kernel(
         rest = tenant("up_sb04", [P, JT - SHARE, PACK], F32, "up")
         nc.scalar.copy(rest[:], up_tile(0, 4, 6, SHARE, JT - SHARE))
         nc.gpsimd.tensor_tensor(hidden(late, 0)[:, SHARE:], rest[:], act[0, 4][:, SHARE:], MULT)
-        reorder_wc(1, tenant("wc_p1", [P, N], U32, "wd", 2048))
         y = own("y01", [P, 384], F32)
         add_bias(1, sum_of(1, first_runs, 3)[:], y[:])
         weigh_on_gpsimd(weighed[1], y, FIRST)

@@ -72,17 +72,16 @@ def tile_list_beam_cache_rewrite_kernel(
         tab_w = own("tab_w", [P, T], I32)
         wb_rows = wb.rearrange("(p i) c -> p i c", i=PACK)
 
+        nc.gpsimd.memset(tab_s[:].bitcast(I32), 0)
         nc.gpsimd.memset(ws_raw[:].bitcast(I32), 0)
         nc.sync.dma_start(pick[:], offs)
-        nc.sync.dma_start(
-            tab_s[:].bitcast(I32), tab_scales[0].bitcast(I32).unsqueeze(1).to_broadcast([16, 8, T // 4])
-        )
+        nc.sync.dma_start(tab_s[0:P:8, :].bitcast(I32), tab_scales[0].bitcast(I32))
+        nc.sync.dma_start(wa_raw[:].bitcast(I32), wa_words[0].bitcast(I32))
         nc.sync.dma_start(ws_raw[0:P:8, :].bitcast(I32), wa_scales[0].bitcast(I32))
         nc.sync.dma_start(
             ws_raw[WC_ROW:P:8, :].bitcast(I32).rearrange("q (a c) -> q a c", a=2),
             wc_scales.bitcast(I32).rearrange("a q c -> q a c"),
         )
-        nc.sync.dma_start(wa_raw[:].bitcast(I32), wa_words[0].bitcast(I32))
         nc.sync.dma_start(tab_w[:], tab_words[0].rearrange("p t i -> p (t i)").bitcast(I32))
         wb_raw = {0: own("wb_raw0", [P, PACK, QUARTER], F32), 1: tenant("wb_raw1", [P, PACK, QUARTER], F32, "wb1")}
         for n in range(2):

@@ -16,6 +16,7 @@ FP4X4 = mybir.dt.float4_e2m1fn_x4
 ACT = mybir.ActivationFunctionType
 MULT = mybir.AluOpType.mult
 ADD = mybir.AluOpType.add
+MAX = mybir.AluOpType.max
 
 P = 128
 PACK = 4
@@ -159,7 +160,7 @@ def tile_list_beam_cache_rewrite_kernel(
                 dst = first_bf[pair][:].rearrange("p (t m i) -> p m t i", t=2, i=PACK)[:, n * 64 : (n + 1) * 64]
                 src = wb_raw[n][:].rearrange("p i (m t) -> p m t i", t=PACK)[:, :, 2 * pair : 2 * pair + 2]
                 if (n, pair) == (1, 0):
-                    nc.vector.tensor_copy(dst, src)
+                    nc.vector.tensor_tensor(dst, src, src, MAX)
                 else:
                     nc.scalar.copy(dst, src)
         for pair in (1, 0):

from contextlib import ExitStack

import concourse.mybir as mybir

K, H, N, T, S, T2 = 512, 1024, 512, 2048, 1024, 2048
FLOPS = 2 * S * (2 * K * H + H * N + K * N)

F32 = mybir.dt.float32
BF16 = mybir.dt.bfloat16
I32 = mybir.dt.int32
U32 = mybir.dt.uint32
U16 = mybir.dt.uint16
U8 = mybir.dt.uint8
FP8X4 = mybir.dt.float8_e4m3fn_x4
FP4X4 = mybir.dt.float4_e2m1fn_x4
ACT = mybir.ActivationFunctionType
MULT = mybir.AluOpType.mult
ADD = mybir.AluOpType.add
MAX = mybir.AluOpType.max

P = 128
PACK = 4
PASS = P * PACK
QUARTER = 256
JT = 128
WC_ROW = 4
BANK = 2048

FIRST, FILL, SECOND, LAST = slice(0, 384), slice(384, 512), slice(512, 768), slice(768, 1024)
WORD_RUNS = (slice(0, 512), SECOND, LAST)
SHARE = 64
HELD = 640

ROOM_SIZES = (
    ("wb2", 4096),
    ("wb3", 4096),
    ("wd", 8192),
    ("wc", 4096),
    ("weight", 4096),
    ("page3", 8192),
    ("wb1", 4096),
    ("wb_bf", 4096),
    ("first_h", 4096),
    ("late_h", 5120),
    ("y02", 2048),
    ("act15", 2048),
)
ROOM = {name: sum(size for other, size in ROOM_SIZES[:n]) for n, (name, own) in enumerate(ROOM_SIZES)}
ROOM = {**ROOM, "act04": ROOM["wd"] + 4096, "up": ROOM["wd"] + 6144}


def tile_list_beam_cache_rewrite_kernel(
    tc, tab_words, tab_scales, wa_words, wa_scales, wb, wc_words, wc_scales, wd, bo, wgo, offs, offs2, out
):
    nc = tc.nc
    with ExitStack() as ctx:
        lists = ctx.enter_context(tc.tile_pool(name="lists", bufs=1))
        keep = ctx.enter_context(tc.tile_pool(name="keep", bufs=1))
        shared = ctx.enter_context(tc.tile_pool(name="shared", bufs=1))
        psum = ctx.enter_context(tc.psum_pool(name="psum", bufs=1))

        def own(name, shape, dtype):
            return keep.tile(shape, dtype, name=name, align_bytes=64)

        def tenant(name, shape, dtype, room, at=0):
            return shared.tile(shape, dtype, name=name, offset=ROOM[room] + at, align_bytes=64)

        pick = lists.tile([P, S // 16], U16, name="pick")
        put = lists.tile([P, S // 16], U16, name="put")
        tab_s = own("tab_s", [P, T], U8)
        ws_raw = own("ws_raw", [P, H], U8)
        wa_raw = own("wa_raw", [P, 2 * H], U8)
        tab_w = own("tab_w", [P, T], I32)
        wb_rows = wb.rearrange("(p i) c -> p i c", i=PACK)

        nc.gpsimd.memset(tab_s[:].bitcast(I32), 0)
        nc.gpsimd.memset(ws_raw[:].bitcast(I32), 0)
        nc.sync.dma_start(pick[:], offs)
        nc.sync.dma_start(tab_s[0:P:8, :].bitcast(I32), tab_scales[0].bitcast(I32))
        nc.sync.dma_start(wa_raw[:].bitcast(I32), wa_words[0].bitcast(I32))
        nc.sync.dma_start(ws_raw[0:P:8, :].bitcast(I32), wa_scales[0].bitcast(I32))
        nc.sync.dma_start(
            ws_raw[WC_ROW:P:8, :].bitcast(I32).rearrange("q (a c) -> q a c", a=2),
            wc_scales.bitcast(I32).rearrange("a q c -> q a c"),
        )
        nc.sync.dma_start(tab_w[:], tab_words[0].rearrange("p t i -> p (t i)").bitcast(I32))
        wb_raw = {0: own("wb_raw0", [P, PACK, QUARTER], F32), 1: tenant("wb_raw1", [P, PACK, QUARTER], F32, "wb1")}
        for n in range(2):
            nc.sync.dma_start(wb_raw[n][:], wb_rows[:, :, n * QUARTER : (n + 1) * QUARTER])
        nc.sync.dma_start(put[:], offs2)
        bias = own("bias", [P, PACK], F32)
        nc.sync.dma_start(bias[:], bo.rearrange("(p i) -> p i", i=PACK))
        wc_rows = [wc_words[a].rearrange("p c i -> p (c i)").bitcast(I32) for a in range(2)]
        wc_raw = {0: own("wc_raw0", [P, N], I32)}
        nc.sync.dma_start(wc_raw[0][:], wc_rows[0])

        pages = {i: own(f"page{i}", [P, T2], F32) for i in range(3)}
        nc.gpsimd.memset(pages[1][:], 0.0)
        nc.gpsimd.memset(pages[2][:], 0.0)
        warm = own("warm", [P, 2], F32)
        nc.vector.memset(warm[:, 0:1], 0.0)
        nc.scalar.activation(warm[:, 1:2], warm[:, 0:1], ACT.Silu)
        nc.vector.memset(pages[0][:, 0 : T2 // 2 - 1], 0.0)
        nc.vector.memset(pages[0][:, T2 // 2 - 1 :], 0.0)

        picked_s = tenant("picked_s", [P, ROOM["wb1"]], U8, "wb2")
        planes = own("planes", [P, S + H], U8)
        nc.vector.tensor_copy(picked_s[:, 0:S], tab_s[:].indirect(pick[:]))
        nc.vector.tensor_copy(
            planes[:, S:].rearrange("p (b t g m) -> p b g t m", b=2, t=PACK, m=16),
            ws_raw[:].rearrange("p (b g m t) -> p b g t m", b=2, t=PACK, m=16),
        )
        nc.vector.tensor_copy(planes[:, 0:S].bitcast(I32), picked_s[:, 0:S].bitcast(I32))
        for r in range(1, 4):
            nc.sync.dma_start(planes[r:P:32, :].bitcast(I32), planes[8 * r : P : 32, :].bitcast(I32))
        for n in (2, 3):
            wb_raw[n] = tenant(f"wb_raw{n}", [P, PACK, QUARTER], F32, f"wb{n}")
            nc.sync.dma_start(wb_raw[n][:], wb_rows[:, :, n * QUARTER : (n + 1) * QUARTER])
        wc_raw[1] = tenant("wc_raw1", [P, N], I32, "wc")
        nc.sync.dma_start(wc_raw[1][:], wc_rows[1])
        wd_raw = tenant("wd_raw", [P, PACK, PASS], F32, "wd")
        nc.sync.dma_start(wd_raw[:], wd.rearrange("(p i) c -> p i c", i=PACK))
        wc_s = ws_raw
        for r in range(4):
            nc.sync.dma_start(wc_s[r:P:32, :].bitcast(I32), planes[WC_ROW + 8 * r : P : 32, S:].bitcast(I32))
        weight = tenant("weight", [P, S], F32, "weight")
        nc.sync.dma_start(weight[:], wgo)
        pages[3] = tenant("page3", [P, T2], F32, "page3")
        nc.gpsimd.memset(pages[3][:], 0.0)
        v_s = planes[:, 0:S]
        wa_s = planes[:, S:]

        wa_p = own("wa_p", [P, 2 * H], U8)
        nc.scalar.copy(
            wa_p[:].bitcast(U16).rearrange("p (b t g m) -> p b g t m", b=2, t=PACK, m=8),
            wa_raw[:].bitcast(U16).rearrange("p (b g m t) -> p b g t m", b=2, t=PACK, m=8),
        )
        wb_q = [own(f"wb_q{b}", [P, PASS], U32) for b in range(2)]
        wb_s = [own(f"wb_s{b}", [P, PASS], U8) for b in range(2)]
        v_w = {}

        def gather_words(k, tile):
            js = WORD_RUNS[k]
            v_w[k] = tile
            nc.vector.tensor_copy(tile[:], tab_w[:].bitcast(U32).indirect(pick[:, js.start // 16 : js.stop // 16]))

        def words(js):
            k = max(n for n in range(len(WORD_RUNS)) if WORD_RUNS[n].start <= js.start)
            first = WORD_RUNS[k].start
            return v_w[k][:, js.start - first : js.stop - first].bitcast(FP8X4)

        def quantise(codes, scales, values):
            nc.vector.quantize_mx(out=codes.bitcast(FP8X4), scales=scales, in_=values)

        gather_words(0, own("v_w0", [P, 512], U32))
        gather_words(1, own("v_w1", [P, QUARTER], U32))
        first_bf = [tenant(f"first_bf{pair}", [P, 2 * PASS], BF16, "wb_bf", pair * 2048) for pair in range(2)]
        for n in range(2):
            for pair in range(2):
                dst = first_bf[pair][:].rearrange("p (t m i) -> p m t i", t=2, i=PACK)[:, n * 64 : (n + 1) * 64]
                src = wb_raw[n][:].rearrange("p i (m t) -> p m t i", t=PACK)[:, :, 2 * pair : 2 * pair + 2]
                if (n, pair) == (1, 0):
                    nc.vector.tensor_tensor(dst, src, src, MAX)
                else:
                    nc.scalar.copy(dst, src)
        for pair in (1, 0):
            cols = slice(pair * 2 * P, (pair + 1) * 2 * P)
            quantise(wb_q[0][:, cols], wb_s[0][:, cols], first_bf[pair][:])
        wc_p = {}

        def reorder_wc(a):
            wc_p[a] = own(f"wc_p{a}", [P, N], U32)
            nc.scalar.copy(
                wc_p[a][:].rearrange("p (t g m) -> p g t m", t=PACK, m=4),
                wc_raw[a][:].bitcast(U32).rearrange("p (g m t) -> p g t m", t=PACK, m=4),
            )

        reorder_wc(0)
        gather_words(2, tenant("v_w2", [P, QUARTER], U32, "wb1"))
        second_bf = tenant("second_bf", [P, PACK * PASS], BF16, "wb_bf")
        for n in (2, 3):
            dst = second_bf[:].rearrange("p (t m i) -> p m t i", t=PACK, i=PACK)[:, (n - 2) * 64 : (n - 1) * 64]
            src = wb_raw[n][:].rearrange("p i (m t) -> p m t i", t=PACK)
            nc.gpsimd.tensor_scalar(dst, src, 1.0, 0.0, MULT, ADD)

        act = {}

        def gate(b, u, bank, tile=None):
            js = slice(u * JT, (u + 1) * JT)
            acc = psum.tile([P, PACK, JT], F32, name=f"gate{b}{u}", offset=bank * BANK)
            for t in range(PACK):
                col = b * PASS + t * P
                nc.tensor.matmul_mx(
                    out=acc[:, t, :],
                    lhsT=wa_p[:, 2 * col : 2 * (col + P)].bitcast(FP4X4),
                    lhsT_scale=wa_s[:, col : col + P],
                    rhs=words(js),
                    rhs_scale=v_s[:, js],
                    start=True,
                    stop=True,
                )
            act[b, u] = own(f"act{b}{u}", [P, JT, PACK], F32) if tile is None else tile
            nc.scalar.activation(act[b, u][:], acc[:].rearrange("p t j -> p j t"), ACT.Silu)

        def up_tile(b, u, bank, first=0, width=JT):
            js = slice(u * JT + first, u * JT + first + width)
            up = psum.tile([P, PACK, width], F32, name=f"up{b}{u}_{first}", offset=bank * BANK)
            for t in (2, 3, 0, 1):
                nc.tensor.matmul_mx(
                    out=up[:, t, :],
                    lhsT=wb_q[b][:, t * P : (t + 1) * P].bitcast(FP8X4),
                    lhsT_scale=wb_s[b][:, t * P : (t + 1) * P],
                    rhs=words(js),
                    rhs_scale=v_s[:, js],
                    start=True,
                    stop=True,
                )
            return up[:].rearrange("p t j -> p j t")

        def hidden(h_bf, n):
            return h_bf[:, n * PASS : (n + 1) * PASS].rearrange("p (j t) -> p j t", t=PACK)

        def multiply_on_vector(b, u, bank, dst):
            nc.vector.tensor_tensor(dst, up_tile(b, u, bank), act[b, u][:], MULT)

        up_sb = {}

        def stage_up(b, u, room):
            up_sb[b, u] = tenant(f"up_sb{b}{u}", [P, JT, PACK], F32, room)
            nc.scalar.copy(up_sb[b, u][:], up_tile(b, u, 6 + u % 2))

        def multiply_on_gpsimd(b, u, dst):
            nc.gpsimd.tensor_tensor(dst, up_sb[b, u][:], act[b, u][:], MULT)

        h_q = {}

        def sum_of(i, runs, bank):
            first = runs[0].start
            acc = psum.tile([P, runs[-1].stop - first], F32, name=f"acc{i}_{first}", offset=bank * BANK)
            passes = []
            for js in runs:
                passes.append((js, wd_q[:, i * P : (i + 1) * P], wd_s[:, i * P : (i + 1) * P], words(js), v_s[:, js]))
            for js in runs:
                for a in range(2):
                    codes, scales = h_q[js.start, a]
                    lhs = wc_p[a][:, i * P : (i + 1) * P]
                    passes.append((js, lhs, wc_s[:, a * N + i * P : a * N + (i + 1) * P], codes.bitcast(FP8X4), scales))
            for n, (js, lhs, lhs_s, rhs, rhs_s) in enumerate(passes):
                nc.tensor.matmul_mx(
                    out=acc[:, js.start - first : js.stop - first],
                    lhsT=lhs.bitcast(FP8X4),
                    lhsT_scale=lhs_s,
                    rhs=rhs,
                    rhs_scale=rhs_s,
                    start=(n == 0),
                    stop=(n == len(passes) - 1),
                )
            return acc

        def add_bias(i, acc, dst):
            nc.scalar.activation(dst, acc, ACT.Identity, bias=bias[:, i : i + 1])

        def weigh_on_gpsimd(dst, y, js):
            nc.gpsimd.tensor_tensor(dst[:], y[:], weight[:, js], MULT)

        def window(i, js):
            return pages[i][:].indirect(put[:, js.start // 16 : js.stop // 16])

        def scatter(i, js, weighed):
            nc.vector.tensor_copy(window(i, js), weighed[:])

        def weigh_and_scatter(i, js, y):
            nc.vector.tensor_tensor(window(i, js), y[:], weight[:, js], MULT)

        h00 = tenant("h00", [P, 4 * PASS], BF16, "first_h")
        for u in range(4):
            gate(0, u, u % 2)
        for u in range(4):
            multiply_on_vector(0, u, 2 + u % 3, hidden(h00, u))
            if u < 3:
                gate(1, u, u % 2)
        quantise(wb_q[1][:], wb_s[1][:], second_bf[:])
        codes = tenant("h_q00", [P, 512], U32, "wb3")
        scales = tenant("h_s00", [P, 512], U8, "wb3", 2048)
        quantise(codes[:], scales[:], h00[:])
        for js in (slice(0, 256), slice(256, 384), FILL):
            h_q[js.start, 0] = (codes[:, js], scales[:, js])
        h01 = tenant("h01", [P, 3 * PASS], BF16, "late_h")
        for u in range(3):
            multiply_on_vector(1, u, 2 + (u + 1) % 3, hidden(h01, u))

        wd_bf = [tenant("wd_bf0", [P, 2 * PASS], BF16, "first_h"), tenant("wd_bf1", [P, 2 * PASS], BF16, "late_h", 3072)]
        for pair in range(2):
            dst = wd_bf[pair][:].rearrange("p (t m i) -> p m t i", t=2, i=PACK)
            src = wd_raw[:].rearrange("p i (m t) -> p m t i", t=PACK)[:, :, 2 * pair : 2 * pair + 2]
            if pair == 0:
                nc.gpsimd.tensor_scalar(dst, src, 1.0, 0.0, MULT, ADD)
            else:
                nc.scalar.copy(dst, src)
        reorder_wc(1)
        wd_q = own("wd_q", [P, PASS], U32)
        wd_s = own("wd_s", [P, PASS], U8)
        codes = own("h_q01", [P, 384], U32)
        scales = own("h_s01", [P, 384], U8)
        for js in (slice(0, 256), slice(256, 384)):
            quantise(codes[:, js], scales[:, js], h01[:, PACK * js.start : PACK * js.stop])
        for pair in range(2):
            cols = slice(pair * 2 * P, (pair + 1) * 2 * P)
            quantise(wd_q[:, cols], wd_s[:, cols], wd_bf[pair][:])
        for js in (slice(0, 256), slice(256, 384)):
            h_q[js.start, 1] = (codes[:, js], scales[:, js])
        gate(1, 3, 1, tenant("act13", [P, JT, PACK], F32, "wd"))
        h13 = own("h13", [P, PASS], BF16)
        multiply_on_vector(1, 3, 3, hidden(h13, 0))

        first_runs = (slice(0, 256), slice(256, 384))
        weighed = {i: own(f"weighed0{i}", [P, 384], F32) for i in range(3)}
        nc.vector.scalar_tensor_tensor(
            weighed[0][:], sum_of(0, first_runs, 5)[:], bias[:, 0:1], weight[:, FIRST], ADD, MULT
        )
        late = tenant("h_second", [P, 4 * PASS], BF16, "late_h")
        gate(0, 4, 0, tenant("act04", [P, JT, PACK], F32, "act04"))
        nc.vector.tensor_tensor(hidden(late, 0)[:, 0:SHARE], up_tile(0, 4, 7, 0, SHARE), act[0, 4][:, 0:SHARE], MULT)
        scatter(0, FIRST, weighed[0])

        rest = tenant("up_sb04", [P, JT - SHARE, PACK], F32, "up")
        nc.scalar.copy(rest[:], up_tile(0, 4, 6, SHARE, JT - SHARE))
        nc.gpsimd.tensor_tensor(hidden(late, 0)[:, SHARE:], rest[:], act[0, 4][:, SHARE:], MULT)
        y = own("y01", [P, 384], F32)
        add_bias(1, sum_of(1, first_runs, 3)[:], y[:])
        weigh_on_gpsimd(weighed[1], y, FIRST)
        scatter(1, FIRST, weighed[1])
        gate(0, 5, 0)
        stage_up(0, 5, "up")
        multiply_on_gpsimd(0, 5, hidden(late, 1))
        y = tenant("y02", [P, 384], F32, "y02")
        add_bias(2, sum_of(2, first_runs, 5)[:], y[:])
        weigh_on_gpsimd(weighed[2], y, FIRST)
        scatter(2, FIRST, weighed[2])
        gate(1, 4, 0)
        stage_up(1, 4, "up")
        multiply_on_gpsimd(1, 4, hidden(late, 2))
        gate(1, 5, 0, tenant("act15", [P, JT, PACK], F32, "act15"))
        stage_up(1, 5, "y02")
        multiply_on_gpsimd(1, 5, hidden(late, 3))
        gate(0, 6, 0)
        stage_up(0, 6, "up")
        held = tenant("weighed03", [P, 384], F32, "act15")
        nc.vector.scalar_tensor_tensor(
            held[:], sum_of(3, first_runs, 3)[:], bias[:, 3:4], weight[:, FIRST], ADD, MULT
        )
        codes = tenant("h_q13", [P, JT], U32, "act15", 1536)
        scales = own("h_s13", [P, JT], U8)
        quantise(codes[:], scales[:], h13[:])
        h_q[FILL.start, 1] = (codes[:], scales[:])

        def quantise_run(js, h_bf):
            codes = own(f"h_q{js.start}", [P, 2 * QUARTER], U32)
            scales = own(f"h_s{js.start}", [P, 2 * QUARTER], U8)
            quantise(codes[:], scales[:], h_bf[:])
            for a in range(2):
                cols = slice(a * QUARTER, (a + 1) * QUARTER)
                h_q[js.start, a] = (codes[:, cols], scales[:, cols])

        quantise_run(SECOND, late)
        scatter(3, FIRST, held)

        middle = slice(FILL.start, SECOND.stop)
        early = slice(FILL.start, HELD)
        cut = HELD - FILL.start
        late = tenant("h_last", [P, 4 * PASS], BF16, "late_h")
        multiply_on_gpsimd(0, 6, hidden(late, 0))
        gate(0, 7, 0)
        shared_up = up_tile(0, 7, 7)
        rest = tenant("up_sb07", [P, JT - SHARE, PACK], F32, "up")
        nc.scalar.copy(rest[:], shared_up[:, SHARE:])
        nc.vector.tensor_tensor(hidden(late, 1)[:, 0:SHARE], shared_up[:, 0:SHARE], act[0, 7][:, 0:SHARE], MULT)
        wide = {i: own(f"y_wide{i}", [P, S - HELD], F32) for i in (2, 3)}
        for i, (b, u), bank in ((0, (0, 7), 5), (1, (1, 6), 3), (2, (1, 7), 5)):
            js = middle if i < 2 else early
            acc = sum_of(i, (FILL, SECOND), bank)
            y = own(f"y1{i}", [P, js.stop - js.start], F32)
            add_bias(i, acc[:, 0 : js.stop - js.start], y[:])
            if i == 2:
                add_bias(i, acc[:, cut:], wide[i][:, 0 : SECOND.stop - HELD])
            result = own(f"weighed1{i}", [P, js.stop - js.start], F32)
            weigh_on_gpsimd(result, y, js)
            scatter(i, js, result)
            if i > 0:
                gate(b, u, 0)
                stage_up(b, u, "up")
                multiply_on_gpsimd(b, u, hidden(late, 2 * b + u - 6))
            else:
                nc.gpsimd.tensor_tensor(hidden(late, 1)[:, SHARE:], rest[:], act[0, 7][:, SHARE:], MULT)
        acc = sum_of(3, (FILL, SECOND), 3)
        add_bias(3, acc[:, cut:], wide[3][:, 0 : SECOND.stop - HELD])
        cover = tenant("y13", [P, cut], F32, "up")
        add_bias(3, acc[:, 0:cut], cover[:])
        quantise_run(LAST, late)
        weigh_and_scatter(3, early, cover)

        out_rows = out.rearrange("(p i) t -> p i t", i=PACK)
        for i, bank in enumerate((5, 6, 7, 3)):
            acc = sum_of(i, (LAST,), bank)
            if i < 2:
                y = own(f"y2{i}", [P, QUARTER], F32)
                add_bias(i, acc[:], y[:])
                weigh_and_scatter(i, LAST, y)
            else:
                add_bias(i, acc[:], wide[i][:, SECOND.stop - HELD :])
                weigh_and_scatter(i, slice(HELD, S), wide[i])
            nc.sync.dma_start(out_rows[:, i, :], pages[i][:])
